import numpy as np
import ml_dtypes


def mxq(x, axis, fmt="e4m3"):
    dtype, down = {"e4m3": (ml_dtypes.float8_e4m3fn, 7), "e5m2": (ml_dtypes.float8_e5m2, 14)}[fmt]
    v = np.moveaxis(np.asarray(x, np.float32).astype(ml_dtypes.bfloat16).astype(np.float64), axis, -1)
    blocks = v.reshape(v.shape[:-1] + (-1, 32))
    amax = np.abs(blocks).max(-1, keepdims=True)
    byte = np.maximum(np.where(amax > 0, np.frexp(amax)[1] - 1 + 127, 0) - down, 1)
    scale = np.exp2(byte - 127.0)
    codes = (blocks / scale).astype(np.float32).astype(dtype).astype(np.float64)
    return np.moveaxis((codes * scale).reshape(v.shape), -1, axis)


WIDE = False


def mx_kscale(k):
    if not WIDE:
        return np.ones(k)
    levels = np.array([10, -10, 5, -5, 0])
    if k % 512:
        return np.exp2(np.random.permutation(np.resize(levels, k // 32))).repeat(32)
    a = np.empty((k // 512, 16))
    for p in range(k // 512):
        a[p, :8] = np.random.permutation(np.resize(levels, 8))
        for g in range(8):
            far = levels[np.abs(levels - a[p, g]) >= 10]
            a[p, g + 8] = far[np.random.randint(len(far))]
    return np.exp2(a.ravel()).repeat(32)


def f64(x):
    return np.asarray(x).astype(np.float64)


def striped(idx):
    return np.tile(idx.reshape(-1, 16).T, (8, 1)).astype(np.uint16)


def unstriped(offs):
    return offs[:16].T.reshape(-1).astype(np.int64)


def pack_weight(w):
    k, n = w.shape
    w = f64(np.asarray(w, np.float32).astype(ml_dtypes.bfloat16)).reshape(k // 32, 32, n)
    amax = np.abs(w).max(1)
    byte = np.clip(np.where(amax > 0, np.frexp(amax)[1] - 1 + 127 - 7, 1), 1, 254)
    scaled = (w * np.exp2(127.0 - byte)[:, None, :]).reshape(k, n).astype(np.float32)
    words = np.ascontiguousarray(scaled.reshape(k // 512, 128, 4, n).transpose(0, 1, 3, 2)).astype(ml_dtypes.float8_e4m3fn).view(np.uint8)
    return words, np.ascontiguousarray(byte.astype(np.uint8).reshape(k // 512, 16, n))


def unpack_weight(words, scales):
    g, p, n, _ = words.shape
    vals = np.ascontiguousarray(words).view(ml_dtypes.float8_e4m3fn).astype(np.float64) * np.repeat(np.exp2(scales.astype(np.float64) - 127.0), 8, axis=1)[..., None]
    return vals.transpose(0, 1, 3, 2).reshape(g * 512, n)


K, T, S, H, V, W = 512, 2048, 512, 512, 512, 2048


def setup_inputs():
    n = np.random.standard_normal
    s = mx_kscale(K)[:, None]
    u = mx_kscale(H)
    packed_xT = pack_weight(n((K, T)) * s)
    packed_eT = pack_weight(n((H, W)) / np.sqrt(H) / u[:, None])
    return {
        "x_words": packed_xT[0],
        "x_scales": packed_xT[1],
        "w1": (n((K, H)) / np.sqrt(K) / s * u).astype(np.float32),
        "e_words": packed_eT[0],
        "e_scales": packed_eT[1],
        "lab": (np.where(np.random.uniform(size=(S, V)) < 0.3, 1.0, -1.0)).astype(np.float32),
        "offs": striped(np.random.permutation(T)[:S]),
        "txt": striped(np.random.permutation(W)[:V]),
    }


def reference(x_words, x_scales, w1, e_words, e_scales, lab, offs, txt):
    xq = unpack_weight(x_words, x_scales)[:, unstriped(offs)]
    h = mxq(f64(w1), 0, "e4m3").T @ xq
    e_txt = unpack_weight(e_words, e_scales)[:, unstriped(txt)]
    y = mxq(h, 0, "e4m3").T @ e_txt
    z = f64(lab) * (1.5 * y - 0.5)
    return np.log(np.exp(-1.0 * z) + 1.0)

@@ -1,0 +1,154 @@
+from contextlib import ExitStack
+
+import concourse.mybir as mybir
+
+K, T, S, H, V, W = 512, 2048, 512, 512, 512, 2048
+FLOPS = 2 * K * H * S + 2 * H * S * V
+
+F32 = mybir.dt.float32
+BF16 = mybir.dt.bfloat16
+I32 = mybir.dt.int32
+U32 = mybir.dt.uint32
+U16 = mybir.dt.uint16
+U8 = mybir.dt.uint8
+FP8X4 = mybir.dt.float8_e4m3fn_x4
+ALU = mybir.AluOpType
+ACT = mybir.ActivationFunctionType
+
+P = 128
+PACK = 4
+BLOCKS = S // P
+E_ROW = 4
+M_VECTOR = 80
+SCALE = 1.5
+SHIFT = 0.5 / 1.5
+LINEAR_FROM = 30.0
+
+
+def load_scales(queue, window, scales, row0):
+    for q in range(4):
+        queue.dma_start(
+            out=window[32 * q + row0 : 32 * q + row0 + 4, :].bitcast(I32),
+            in_=scales[0, 4 * q : 4 * q + 4, :].bitcast(I32),
+        )
+
+
+def tile_picked_ysiglip_loss_p_kernel(
+    tc, x_words, x_scales, w1, e_words, e_scales, lab, offs, txt, out
+):
+    nc = tc.nc
+    with ExitStack() as ctx:
+        keep = ctx.enter_context(tc.tile_pool(name="keep", bufs=1))
+        psum = ctx.enter_context(tc.psum_pool(name="psum", bufs=1))
+
+        offs_sb = keep.tile([P, S // 16], U16, name="offs_sb")
+        txt_sb = keep.tile([P, V // 16], U16, name="txt_sb")
+        xw_all = keep.tile([P, T], I32, name="xw_all", align_bytes=64)
+        xs_all = keep.tile([P, T], U8, name="xs_all", align_bytes=64)
+        ew_all = keep.tile([P, W], I32, name="ew_all", align_bytes=64)
+        es_all = keep.tile([P, W], U8, name="es_all", align_bytes=64)
+        w_raw = keep.tile([P, PACK, H], F32, name="w_raw", align_bytes=64)
+        lab_sb = [keep.tile([P, V], F32, name="lab%d" % b, align_bytes=64) for b in range(BLOCKS)]
+        clamped = keep.tile([P, BLOCKS * V + 8], F32, name="clamped", align_bytes=64)
+        expo = keep.tile([P, BLOCKS * V + 8], F32, name="expo", align_bytes=64)
+
+        nc.vector.memset(xs_all[:].bitcast(I32), 0)
+        nc.gpsimd.memset(es_all[:].bitcast(I32), 0)
+        nc.vector.memset(clamped[:, BLOCKS * V : BLOCKS * V + 1], 0.0)
+
+        nc.sync.dma_start(offs_sb[:], offs)
+        nc.sync.dma_start(out=w_raw[:], in_=w1.rearrange("(p j) c -> p j c", j=PACK))
+        load_scales(nc.sync, xs_all, x_scales, 0)
+        nc.sync.dma_start(out=xw_all[:], in_=x_words[0].rearrange("p c r -> p (c r)").bitcast(I32))
+        nc.sync.dma_start(txt_sb[:], txt)
+        nc.sync.dma_start(out=ew_all[:], in_=e_words[0].rearrange("p c r -> p (c r)").bitcast(I32))
+        load_scales(nc.gpsimd, es_all, e_scales, E_ROW)
+        for b in range(BLOCKS):
+            nc.sync.dma_start(out=lab_sb[b][:], in_=lab[b * P : (b + 1) * P, :])
+
+        xs = keep.tile([P, S], U8, name="xs", align_bytes=64)
+        nc.vector.tensor_copy(xs[:], xs_all[:].indirect(offs_sb[:]))
+
+        w_bf = keep.tile([P, PACK * H], BF16, name="w_bf", align_bytes=64)
+        w_dst = w_bf[:].rearrange("p (t m j) -> p m j t", t=PACK, j=PACK)
+        w_src = w_raw[:].rearrange("p j (m t) -> p m j t", t=PACK)
+        nc.vector.tensor_copy(out=w_dst[:, :M_VECTOR], in_=w_src[:, :M_VECTOR])
+        nc.scalar.copy(out=w_dst[:, M_VECTOR:], in_=w_src[:, M_VECTOR:])
+        w_codes = keep.tile([P, H], U32, name="w_codes", align_bytes=64)
+        w_scales = keep.tile([P, H], U8, name="w_scales", align_bytes=64)
+        nc.vector.quantize_mx(out=w_codes[:].bitcast(FP8X4), scales=w_scales[:], in_=w_bf[:])
+
+        xw = keep.tile([P, S], U32, name="xw", align_bytes=64)
+        for half in range(2):
+            nc.vector.tensor_copy(
+                xw[:, half * 256 : (half + 1) * 256],
+                xw_all[:].bitcast(U32).indirect(offs_sb[:, half * 16 : (half + 1) * 16]),
+            )
+
+        h_codes, h_scales = [], []
+        h_bf = []
+        for b in range(BLOCKS):
+            tokens = slice(b * P, (b + 1) * P)
+            h_ps = psum.tile([P, PACK, P], F32, name="h_ps%d" % b)
+            for t in range(PACK):
+                cols = slice(t * P, (t + 1) * P)
+                nc.tensor.matmul_mx(
+                    out=h_ps[:, t, :],
+                    lhsT=w_codes[:, cols].bitcast(FP8X4),
+                    lhsT_scale=w_scales[:, cols],
+                    rhs=xw[:, tokens].bitcast(FP8X4),
+                    rhs_scale=xs[:, tokens],
+                    start=True,
+                    stop=True,
+                )
+            h_bf.append(keep.tile([P, P, PACK], BF16, name="h_bf%d" % b, align_bytes=64))
+            nc.scalar.copy(out=h_bf[b][:], in_=h_ps[:].rearrange("p t n -> p n t"))
+
+        es = keep.tile([P, V], U8, name="es", align_bytes=64)
+        nc.vector.tensor_copy(es[:], es_all[:].indirect(txt_sb[:]))
+
+        for b in range(BLOCKS):
+            h_codes.append(keep.tile([P, P], U32, name="h_codes%d" % b, align_bytes=64))
+            h_scales.append(keep.tile([P, P], U8, name="h_scales%d" % b, align_bytes=64))
+            nc.vector.quantize_mx(
+                out=h_codes[b][:].bitcast(FP8X4),
+                scales=h_scales[b][:],
+                in_=h_bf[b][:].rearrange("p n t -> p (n t)"),
+            )
+
+        ew = keep.tile([P, V], U32, name="ew", align_bytes=64)
+        nc.vector.tensor_copy(ew[:], ew_all[:].bitcast(U32).indirect(txt_sb[:]))
+
+        signed = []
+        for b in range(BLOCKS):
+            y_ps = psum.tile([P, V], F32, name="y_ps%d" % b)
+            nc.tensor.matmul_mx(
+                out=y_ps[:],
+                lhsT=h_codes[b][:].bitcast(FP8X4),
+                lhsT_scale=h_scales[b][:],
+                rhs=ew[:].bitcast(FP8X4),
+                rhs_scale=es[E_ROW:P, :],
+                start=True,
+                stop=True,
+            )
+            signed.append(keep.tile([P, V], F32, name="signed%d" % b, align_bytes=64))
+            nc.vector.scalar_tensor_tensor(
+                out=signed[b][:], in0=y_ps[:], scalar=SHIFT, in1=lab_sb[b][:], op0=ALU.subtract, op1=ALU.mult
+            )
+            cols = slice(b * V, (b + 1) * V)
+            nc.vector.tensor_scalar(
+                out=clamped[:, cols], in0=signed[b][:], scalar1=-LINEAR_FROM / SCALE, scalar2=None, op0=ALU.max
+            )
+            wide = slice(b * V, (b + 1) * V + (1 if b == BLOCKS - 1 else 0))
+            nc.scalar.activation(out=expo[:, wide], in_=clamped[:, wide], func=ACT.Exp, scale=-SCALE)
+
+        one = expo[:, BLOCKS * V : BLOCKS * V + 1]
+        for b in range(BLOCKS):
+            cols = slice(b * V, (b + 1) * V)
+            soft = keep.tile([P, V], F32, name="soft%d" % b, align_bytes=64)
+            nc.scalar.activation(out=soft[:], in_=expo[:, cols], func=ACT.Ln, bias=one)
+            res = keep.tile([P, V], F32, name="res%d" % b, align_bytes=64)
+            nc.vector.scalar_tensor_tensor(
+                out=res[:], in0=signed[b][:], scalar=-SCALE, in1=soft[:], op0=ALU.mult, op1=ALU.max
+            )
+            nc.sync.dma_start(out=out[b * P : (b + 1) * P, :], in_=res[:])

@@ -20,6 +20,7 @@ PACK = 4
 BLOCKS = S // P
 E_ROW = 4
 M_VECTOR = 80
+HALF = V // 2
 SCALE = 1.5
 SHIFT = 0.5 / 1.5
 LINEAR_FROM = 30.0
@@ -39,30 +40,31 @@ def tile_picked_ysiglip_loss_p_kernel(
     nc = tc.nc
     with ExitStack() as ctx:
         keep = ctx.enter_context(tc.tile_pool(name="keep", bufs=1))
+        reuse = ctx.enter_context(tc.tile_pool(name="reuse", bufs=1))
         psum = ctx.enter_context(tc.psum_pool(name="psum", bufs=1))
 
         offs_sb = keep.tile([P, S // 16], U16, name="offs_sb")
         txt_sb = keep.tile([P, V // 16], U16, name="txt_sb")
         xw_all = keep.tile([P, T], I32, name="xw_all", align_bytes=64)
         xs_all = keep.tile([P, T], U8, name="xs_all", align_bytes=64)
-        ew_all = keep.tile([P, W], I32, name="ew_all", align_bytes=64)
-        es_all = keep.tile([P, W], U8, name="es_all", align_bytes=64)
+        ew_all = reuse.tile([P, W], I32, name="ew_all", align_bytes=64, offset=4096)
+        es_all = reuse.tile([P, W], U8, name="es_all", align_bytes=64, offset=0)
         w_raw = keep.tile([P, PACK, H], F32, name="w_raw", align_bytes=64)
         lab_sb = [keep.tile([P, V], F32, name="lab%d" % b, align_bytes=64) for b in range(BLOCKS)]
         clamped = keep.tile([P, BLOCKS * V + 8], F32, name="clamped", align_bytes=64)
         expo = keep.tile([P, BLOCKS * V + 8], F32, name="expo", align_bytes=64)
 
         nc.vector.memset(xs_all[:].bitcast(I32), 0)
-        nc.gpsimd.memset(es_all[:].bitcast(I32), 0)
+        nc.vector.memset(es_all[:].bitcast(I32), 0)
         nc.vector.memset(clamped[:, BLOCKS * V : BLOCKS * V + 1], 0.0)
 
-        nc.sync.dma_start(offs_sb[:], offs)
         nc.sync.dma_start(out=w_raw[:], in_=w1.rearrange("(p j) c -> p j c", j=PACK))
+        nc.sync.dma_start(offs_sb[:], offs)
         load_scales(nc.sync, xs_all, x_scales, 0)
         nc.sync.dma_start(out=xw_all[:], in_=x_words[0].rearrange("p c r -> p (c r)").bitcast(I32))
         nc.sync.dma_start(txt_sb[:], txt)
+        load_scales(nc.sync, es_all, e_scales, E_ROW)
         nc.sync.dma_start(out=ew_all[:], in_=e_words[0].rearrange("p c r -> p (c r)").bitcast(I32))
-        load_scales(nc.gpsimd, es_all, e_scales, E_ROW)
         for b in range(BLOCKS):
             nc.sync.dma_start(out=lab_sb[b][:], in_=lab[b * P : (b + 1) * P, :])
 
@@ -89,7 +91,7 @@ def tile_picked_ysiglip_loss_p_kernel(
         h_bf = []
         for b in range(BLOCKS):
             tokens = slice(b * P, (b + 1) * P)
-            h_ps = psum.tile([P, PACK, P], F32, name="h_ps%d" % b)
+            h_ps = psum.tile([P, PACK, P], F32, name="h_ps%d" % b, tag="h_ps%d" % b)
             for t in range(PACK):
                 cols = slice(t * P, (t + 1) * P)
                 nc.tensor.matmul_mx(
@@ -107,8 +109,8 @@ def tile_picked_ysiglip_loss_p_kernel(
         es = keep.tile([P, V], U8, name="es", align_bytes=64)
         nc.vector.tensor_copy(es[:], es_all[:].indirect(txt_sb[:]))
 
-        for b in range(BLOCKS):
-            h_codes.append(keep.tile([P, P], U32, name="h_codes%d" % b, align_bytes=64))
+        def quantize_h(b, offset):
+            h_codes.append(reuse.tile([P, P], U32, name="h_codes%d" % b, align_bytes=64, offset=offset))
             h_scales.append(keep.tile([P, P], U8, name="h_scales%d" % b, align_bytes=64))
             nc.vector.quantize_mx(
                 out=h_codes[b][:].bitcast(FP8X4),
@@ -116,14 +118,24 @@ def tile_picked_ysiglip_loss_p_kernel(
                 in_=h_bf[b][:].rearrange("p n t -> p (n t)"),
             )
 
-        ew = keep.tile([P, V], U32, name="ew", align_bytes=64)
+        quantize_h(0, 0)
+        ew = reuse.tile([P, V], U32, name="ew", align_bytes=64, offset=1024)
         nc.vector.tensor_copy(ew[:], ew_all[:].bitcast(U32).indirect(txt_sb[:]))
+        for b in range(1, BLOCKS):
+            quantize_h(b, 4096 + 512 * b)
 
-        signed = []
+        y_ps, signed = [], {}
+
+        def signed_logits(b):
+            signed[b] = keep.tile([P, V], F32, name="signed%d" % b, align_bytes=64)
+            nc.vector.scalar_tensor_tensor(
+                out=signed[b][:], in0=y_ps[b][:], scalar=SHIFT, in1=lab_sb[b][:], op0=ALU.subtract, op1=ALU.mult
+            )
+
         for b in range(BLOCKS):
-            y_ps = psum.tile([P, V], F32, name="y_ps%d" % b)
+            y_ps.append(psum.tile([P, V], F32, name="y_ps%d" % b))
             nc.tensor.matmul_mx(
-                out=y_ps[:],
+                out=y_ps[b][:],
                 lhsT=h_codes[b][:].bitcast(FP8X4),
                 lhsT_scale=h_scales[b][:],
                 rhs=ew[:].bitcast(FP8X4),
@@ -131,24 +143,38 @@ def tile_picked_ysiglip_loss_p_kernel(
                 start=True,
                 stop=True,
             )
-            signed.append(keep.tile([P, V], F32, name="signed%d" % b, align_bytes=64))
-            nc.vector.scalar_tensor_tensor(
-                out=signed[b][:], in0=y_ps[:], scalar=SHIFT, in1=lab_sb[b][:], op0=ALU.subtract, op1=ALU.mult
-            )
-            cols = slice(b * V, (b + 1) * V)
-            nc.vector.tensor_scalar(
-                out=clamped[:, cols], in0=signed[b][:], scalar1=-LINEAR_FROM / SCALE, scalar2=None, op0=ALU.max
-            )
-            wide = slice(b * V, (b + 1) * V + (1 if b == BLOCKS - 1 else 0))
-            nc.scalar.activation(out=expo[:, wide], in_=clamped[:, wide], func=ACT.Exp, scale=-SCALE)
+            if b == 0:
+                nc.scalar.activation(out=clamped[:, :V], in_=y_ps[b][:], func=ACT.Abs, scale=SCALE, bias=-0.5)
+                nc.scalar.activation(out=expo[:, :V], in_=clamped[:, :V], func=ACT.Exp, scale=-1.0)
+                continue
+            signed_logits(b)
+            cuts = [0, HALF, V] if b == BLOCKS - 1 else [0, V]
+            for lo, hi in zip(cuts, cuts[1:]):
+                nc.vector.tensor_scalar(
+                    out=clamped[:, b * V + lo : b * V + hi],
+                    in0=signed[b][:, lo:hi],
+                    scalar1=-LINEAR_FROM / SCALE,
+                    scalar2=None,
+                    op0=ALU.max,
+                )
+                wide = slice(b * V + lo, b * V + hi + (1 if b * V + hi == BLOCKS * V else 0))
+                nc.scalar.activation(out=expo[:, wide], in_=clamped[:, wide], func=ACT.Exp, scale=-SCALE)
+
+        signed_logits(0)
+        linear = keep.tile([P, V], F32, name="linear", align_bytes=64)
+        nc.vector.tensor_scalar(
+            out=linear[:], in0=signed[0][:], scalar1=-SCALE, scalar2=0.0, op0=ALU.mult, op1=ALU.max
+        )
 
         one = expo[:, BLOCKS * V : BLOCKS * V + 1]
-        for b in range(BLOCKS):
-            cols = slice(b * V, (b + 1) * V)
-            soft = keep.tile([P, V], F32, name="soft%d" % b, align_bytes=64)
-            nc.scalar.activation(out=soft[:], in_=expo[:, cols], func=ACT.Ln, bias=one)
-            res = keep.tile([P, V], F32, name="res%d" % b, align_bytes=64)
-            nc.vector.scalar_tensor_tensor(
-                out=res[:], in0=signed[b][:], scalar=-SCALE, in1=soft[:], op0=ALU.mult, op1=ALU.max
-            )
-            nc.sync.dma_start(out=out[b * P : (b + 1) * P, :], in_=res[:])
+        for b, lo, hi in [(1, 0, HALF), (1, HALF, V), (2, 0, V), (3, 0, V), (0, 0, HALF), (0, HALF, V)]:
+            soft = keep.tile([P, hi - lo], F32, name="soft%d_%d" % (b, lo), align_bytes=64)
+            nc.scalar.activation(out=soft[:], in_=expo[:, b * V + lo : b * V + hi], func=ACT.Ln, bias=one)
+            res = keep.tile([P, hi - lo], F32, name="res%d_%d" % (b, lo), align_bytes=64)
+            if b == 0:
+                nc.vector.tensor_tensor(out=res[:], in0=linear[:, lo:hi], in1=soft[:], op=ALU.add)
+            else:
+                nc.vector.scalar_tensor_tensor(
+                    out=res[:], in0=signed[b][:, lo:hi], scalar=-SCALE, in1=soft[:], op0=ALU.mult, op1=ALU.max
+                )
+            nc.sync.dma_start(out=out[b * P : (b + 1) * P, lo:hi], in_=res[:])

@@ -19,7 +19,6 @@ P = 128
 PACK = 4
 BLOCKS = S // P
 E_ROW = 4
-M_VECTOR = 80
 HALF = V // 2
 SCALE = 1.5
 SHIFT = 0.5 / 1.5
@@ -27,10 +26,10 @@ LINEAR_FROM = 30.0
 
 
 def load_scales(queue, window, scales, row0):
-    for q in range(4):
+    for r in range(4):
         queue.dma_start(
-            out=window[32 * q + row0 : 32 * q + row0 + 4, :].bitcast(I32),
-            in_=scales[0, 4 * q : 4 * q + 4, :].bitcast(I32),
+            out=window[row0 + r : P : 32, :].bitcast(I32),
+            in_=scales[0, r:16:4, :].bitcast(I32),
         )
 
 
@@ -45,39 +44,44 @@ def tile_picked_ysiglip_loss_p_kernel(
 
         offs_sb = keep.tile([P, S // 16], U16, name="offs_sb")
         txt_sb = keep.tile([P, V // 16], U16, name="txt_sb")
-        xw_all = keep.tile([P, T], I32, name="xw_all", align_bytes=64)
-        xs_all = keep.tile([P, T], U8, name="xs_all", align_bytes=64)
-        ew_all = reuse.tile([P, W], I32, name="ew_all", align_bytes=64, offset=4096)
+        xw_all = reuse.tile([P, T], I32, name="xw_all", align_bytes=64, offset=20480)
+        xs_all = reuse.tile([P, T], U8, name="xs_all", align_bytes=64, offset=28672)
+        ew_all = reuse.tile([P, W], I32, name="ew_all", align_bytes=64, offset=12288)
         es_all = reuse.tile([P, W], U8, name="es_all", align_bytes=64, offset=0)
-        w_raw = keep.tile([P, PACK, H], F32, name="w_raw", align_bytes=64)
-        lab_sb = [keep.tile([P, V], F32, name="lab%d" % b, align_bytes=64) for b in range(BLOCKS)]
-        clamped = keep.tile([P, BLOCKS * V + 8], F32, name="clamped", align_bytes=64)
-        expo = keep.tile([P, BLOCKS * V + 8], F32, name="expo", align_bytes=64)
+        w_raw = reuse.tile([P, PACK, H], F32, name="w_raw", align_bytes=64, offset=4096)
+        clamped = keep.tile([P, BLOCKS * V + 32], F32, name="clamped", align_bytes=64)
+        expo = keep.tile([P, BLOCKS * V + 32], F32, name="expo", align_bytes=64)
 
         nc.vector.memset(xs_all[:].bitcast(I32), 0)
+        zero = reuse.tile([P, 32], F32, name="zero", align_bytes=64, offset=20480 - 64)
+        nc.vector.memset(zero[:], 0.0)
+        nc.vector.tensor_copy(out=clamped[:, BLOCKS * V : BLOCKS * V + 32], in_=zero[:])
         nc.vector.memset(es_all[:].bitcast(I32), 0)
-        nc.vector.memset(clamped[:, BLOCKS * V : BLOCKS * V + 1], 0.0)
 
-        nc.sync.dma_start(out=w_raw[:], in_=w1.rearrange("(p j) c -> p j c", j=PACK))
         nc.sync.dma_start(offs_sb[:], offs)
+        nc.sync.dma_start(out=w_raw[:], in_=w1.rearrange("(p j) c -> p j c", j=PACK))
         load_scales(nc.sync, xs_all, x_scales, 0)
         nc.sync.dma_start(out=xw_all[:], in_=x_words[0].rearrange("p c r -> p (c r)").bitcast(I32))
         nc.sync.dma_start(txt_sb[:], txt)
         load_scales(nc.sync, es_all, e_scales, E_ROW)
         nc.sync.dma_start(out=ew_all[:], in_=e_words[0].rearrange("p c r -> p (c r)").bitcast(I32))
-        for b in range(BLOCKS):
-            nc.sync.dma_start(out=lab_sb[b][:], in_=lab[b * P : (b + 1) * P, :])
 
-        xs = keep.tile([P, S], U8, name="xs", align_bytes=64)
-        nc.vector.tensor_copy(xs[:], xs_all[:].indirect(offs_sb[:]))
 
         w_bf = keep.tile([P, PACK * H], BF16, name="w_bf", align_bytes=64)
         w_dst = w_bf[:].rearrange("p (t m j) -> p m j t", t=PACK, j=PACK)
         w_src = w_raw[:].rearrange("p j (m t) -> p m j t", t=PACK)
-        nc.vector.tensor_copy(out=w_dst[:, :M_VECTOR], in_=w_src[:, :M_VECTOR])
-        nc.scalar.copy(out=w_dst[:, M_VECTOR:], in_=w_src[:, M_VECTOR:])
+        nc.vector.tensor_copy(out=w_dst[:, :64], in_=w_src[:, :64])
+        nc.scalar.copy(out=w_dst[:, 64:], in_=w_src[:, 64:])
+        xs = keep.tile([P, S], U8, name="xs", align_bytes=64)
+        nc.vector.tensor_copy(xs[:], xs_all[:].indirect(offs_sb[:]))
+        lab_blocks = lab.rearrange("(b p) v -> p b v", p=P)
+        lab_inner = reuse.tile([P, 2, V], F32, name="lab_inner", align_bytes=64, offset=4096)
+        lab_outer = reuse.tile([P, 2, V], F32, name="lab_outer", align_bytes=64, offset=8192)
+        nc.sync.dma_start(out=lab_inner[:], in_=lab_blocks[:, 1:3, :])
+        nc.sync.dma_start(out=lab_outer[:], in_=lab_blocks[:, 0:4:3, :])
+        lab_sb = [lab_outer[:, 0, :], lab_inner[:, 0, :], lab_inner[:, 1, :], lab_outer[:, 1, :]]
         w_codes = keep.tile([P, H], U32, name="w_codes", align_bytes=64)
-        w_scales = keep.tile([P, H], U8, name="w_scales", align_bytes=64)
+        w_scales = reuse.tile([P, H], U8, name="w_scales", align_bytes=64, offset=28672)
         nc.vector.quantize_mx(out=w_codes[:].bitcast(FP8X4), scales=w_scales[:], in_=w_bf[:])
 
         xw = keep.tile([P, S], U32, name="xw", align_bytes=64)
@@ -103,7 +107,7 @@ def tile_picked_ysiglip_loss_p_kernel(
                     start=True,
                     stop=True,
                 )
-            h_bf.append(keep.tile([P, P, PACK], BF16, name="h_bf%d" % b, align_bytes=64))
+            h_bf.append(reuse.tile([P, P, PACK], BF16, name="h_bf%d" % b, align_bytes=64, offset=32768 + 2048 * b))
             nc.scalar.copy(out=h_bf[b][:], in_=h_ps[:].rearrange("p t n -> p n t"))
 
         es = keep.tile([P, V], U8, name="es", align_bytes=64)
@@ -120,61 +124,109 @@ def tile_picked_ysiglip_loss_p_kernel(
 
         quantize_h(0, 0)
         ew = reuse.tile([P, V], U32, name="ew", align_bytes=64, offset=1024)
-        nc.vector.tensor_copy(ew[:], ew_all[:].bitcast(U32).indirect(txt_sb[:]))
-        for b in range(1, BLOCKS):
-            quantize_h(b, 4096 + 512 * b)
-
-        y_ps, signed = [], {}
-
-        def signed_logits(b):
-            signed[b] = keep.tile([P, V], F32, name="signed%d" % b, align_bytes=64)
-            nc.vector.scalar_tensor_tensor(
-                out=signed[b][:], in0=y_ps[b][:], scalar=SHIFT, in1=lab_sb[b][:], op0=ALU.subtract, op1=ALU.mult
+        for half in range(2):
+            nc.vector.tensor_copy(
+                ew[:, half * HALF : (half + 1) * HALF],
+                ew_all[:].bitcast(U32).indirect(txt_sb[:, half * 16 : (half + 1) * 16]),
             )
+        for b in range(1, BLOCKS):
+            quantize_h(b, 12288 + 512 * b)
 
-        for b in range(BLOCKS):
-            y_ps.append(psum.tile([P, V], F32, name="y_ps%d" % b))
+        y_ps = {}
+        for b, lo, hi, bank in [
+            (0, 0, HALF, "y_ps0"),
+            (0, HALF, V, "y_ps1"),
+            (1, HALF, V, "y_ps3"),
+            (2, 0, V, "h_ps0"),
+            (1, 0, HALF, "y_ps2"),
+            (3, 0, V, "h_ps1"),
+        ]:
+            acc = psum.tile([P, hi - lo], F32, name="y_ps%d_%d" % (b, lo), tag=bank)
             nc.tensor.matmul_mx(
-                out=y_ps[b][:],
+                out=acc[:],
                 lhsT=h_codes[b][:].bitcast(FP8X4),
                 lhsT_scale=h_scales[b][:],
-                rhs=ew[:].bitcast(FP8X4),
-                rhs_scale=es[E_ROW:P, :],
+                rhs=ew[:, lo:hi].bitcast(FP8X4),
+                rhs_scale=es[E_ROW:P, lo:hi],
                 start=True,
                 stop=True,
             )
-            if b == 0:
-                nc.scalar.activation(out=clamped[:, :V], in_=y_ps[b][:], func=ACT.Abs, scale=SCALE, bias=-0.5)
-                nc.scalar.activation(out=expo[:, :V], in_=clamped[:, :V], func=ACT.Exp, scale=-1.0)
-                continue
-            signed_logits(b)
-            cuts = [0, HALF, V] if b == BLOCKS - 1 else [0, V]
-            for lo, hi in zip(cuts, cuts[1:]):
-                nc.vector.tensor_scalar(
-                    out=clamped[:, b * V + lo : b * V + hi],
-                    in0=signed[b][:, lo:hi],
-                    scalar1=-LINEAR_FROM / SCALE,
-                    scalar2=None,
-                    op0=ALU.max,
-                )
-                wide = slice(b * V + lo, b * V + hi + (1 if b * V + hi == BLOCKS * V else 0))
-                nc.scalar.activation(out=expo[:, wide], in_=clamped[:, wide], func=ACT.Exp, scale=-SCALE)
+            for c in range(lo, hi, HALF):
+                y_ps[b, c] = acc[:, c - lo : c - lo + HALF]
+            y_ps[b, lo, hi] = acc[:]
 
-        signed_logits(0)
-        linear = keep.tile([P, V], F32, name="linear", align_bytes=64)
-        nc.vector.tensor_scalar(
-            out=linear[:], in0=signed[0][:], scalar1=-SCALE, scalar2=0.0, op0=ALU.mult, op1=ALU.max
-        )
+        last_bf = 32768 + 2048 * 3
+        signed = {
+            (1, HALF): reuse.tile([P, HALF], F32, name="signed1", align_bytes=64, offset=last_bf - 512)[:],
+            (0, 0): clamped[:, 2 * V : 2 * V + HALF],
+            (0, HALF): clamped[:, 2 * V + HALF : 3 * V],
+            (1, 0): clamped[:, 3 * V : 3 * V + HALF],
+        }
+        signed2 = reuse.tile([P, V], F32, name="signed2", align_bytes=64, offset=last_bf + 512)
+        signed3 = keep.tile([P, V], F32, name="signed3", align_bytes=64)
+        for c in (0, HALF):
+            signed[2, c] = signed2[:, c : c + HALF]
+            signed[3, c] = signed3[:, c : c + HALF]
+
+        def magnitude(b, lo):
+            nc.scalar.activation(
+                out=clamped[:, b * V + lo : b * V + lo + HALF], in_=y_ps[b, lo], func=ACT.Abs, scale=SCALE, bias=-0.5
+            )
+
+        def signed_logits(dst, src, b, lo, hi):
+            nc.vector.scalar_tensor_tensor(
+                out=dst, in0=src, scalar=SHIFT, in1=lab_sb[b][:, lo:hi], op0=ALU.subtract, op1=ALU.mult
+            )
+
+        def clamp(src, b, lo, hi):
+            nc.vector.tensor_scalar(
+                out=clamped[:, b * V + lo : b * V + hi],
+                in0=src,
+                scalar1=SCALE,
+                scalar2=-LINEAR_FROM,
+                op0=ALU.mult,
+                op1=ALU.max,
+            )
+
+        def exp_minus(b, lo, hi):
+            wide = slice(b * V + lo, b * V + hi + (1 if b * V + hi == BLOCKS * V else 0))
+            nc.scalar.activation(out=expo[:, wide], in_=clamped[:, wide], func=ACT.Exp, scale=-1.0)
+
+        magnitude(0, 0)
+        magnitude(0, HALF)
+        exp_minus(0, 0, V)
+        magnitude(1, 0)
+        signed_logits(signed[1, HALF], y_ps[1, HALF], 1, HALF, V)
+        signed_logits(signed2[:], y_ps[2, 0, V], 2, 0, V)
+        clamp(signed[1, HALF], 1, HALF, V)
+        exp_minus(1, 0, V)
+        signed_logits(signed[3, 0], y_ps[3, 0], 3, 0, HALF)
+        clamp(signed2[:], 2, 0, V)
+        exp_minus(2, 0, V)
+        signed_logits(signed[3, HALF], y_ps[3, HALF], 3, HALF, V)
+        for lo in (0, HALF):
+            clamp(signed[3, lo], 3, lo, lo + HALF)
+            exp_minus(3, lo, lo + HALF)
+
+        by_magnitude = [(0, 0), (0, HALF), (1, 0)]
+        linear = {}
+        for b, lo in by_magnitude:
+            signed_logits(signed[b, lo], y_ps[b, lo], b, lo, lo + HALF)
+        for b, lo in by_magnitude:
+            linear[b, lo] = keep.tile([P, HALF], F32, name="linear%d_%d" % (b, lo), align_bytes=64)
+            nc.vector.tensor_scalar(
+                out=linear[b, lo][:], in0=signed[b, lo], scalar1=-SCALE, scalar2=0.0, op0=ALU.mult, op1=ALU.max
+            )
 
         one = expo[:, BLOCKS * V : BLOCKS * V + 1]
-        for b, lo, hi in [(1, 0, HALF), (1, HALF, V), (2, 0, V), (3, 0, V), (0, 0, HALF), (0, HALF, V)]:
-            soft = keep.tile([P, hi - lo], F32, name="soft%d_%d" % (b, lo), align_bytes=64)
-            nc.scalar.activation(out=soft[:], in_=expo[:, b * V + lo : b * V + hi], func=ACT.Ln, bias=one)
-            res = keep.tile([P, hi - lo], F32, name="res%d_%d" % (b, lo), align_bytes=64)
-            if b == 0:
-                nc.vector.tensor_tensor(out=res[:], in0=linear[:, lo:hi], in1=soft[:], op=ALU.add)
+        for b, lo in [(1, HALF), (2, 0), (2, HALF), (3, 0), (3, HALF)] + by_magnitude:
+            soft = keep.tile([P, HALF], F32, name="soft%d_%d" % (b, lo), align_bytes=64)
+            nc.scalar.activation(out=soft[:], in_=expo[:, b * V + lo : b * V + lo + HALF], func=ACT.Ln, bias=one)
+            res = keep.tile([P, HALF], F32, name="res%d_%d" % (b, lo), align_bytes=64)
+            if (b, lo) in by_magnitude:
+                nc.vector.tensor_tensor(out=res[:], in0=linear[b, lo][:], in1=soft[:], op=ALU.add)
             else:
                 nc.vector.scalar_tensor_tensor(
-                    out=res[:], in0=signed[b][:, lo:hi], scalar=-SCALE, in1=soft[:], op0=ALU.mult, op1=ALU.max
+                    out=res[:], in0=signed[b, lo], scalar=-SCALE, in1=soft[:], op0=ALU.mult, op1=ALU.max
                 )
-            nc.sync.dma_start(out=out[b * P : (b + 1) * P, lo:hi], in_=res[:])
+            nc.sync.dma_start(out=out[b * P : (b + 1) * P, lo : lo + HALF], in_=res[:])

@@ -22,7 +22,9 @@ E_ROW = 4
 HALF = V // 2
 SCALE = 1.5
 SHIFT = 0.5 / 1.5
-LINEAR_FROM = 30.0
+FLOOR_AT = -40.0
+
+KIB = 1024
 
 
 def load_scales(queue, window, scales, row0):
@@ -42,47 +44,52 @@ def tile_picked_ysiglip_loss_p_kernel(
         reuse = ctx.enter_context(tc.tile_pool(name="reuse", bufs=1))
         psum = ctx.enter_context(tc.psum_pool(name="psum", bufs=1))
 
+        def placed(shape, dtype, name, offset):
+            return reuse.tile(shape, dtype, name=name, align_bytes=64, offset=offset)
+
         offs_sb = keep.tile([P, S // 16], U16, name="offs_sb")
         txt_sb = keep.tile([P, V // 16], U16, name="txt_sb")
-        xw_all = reuse.tile([P, T], I32, name="xw_all", align_bytes=64, offset=20480)
-        xs_all = reuse.tile([P, T], U8, name="xs_all", align_bytes=64, offset=28672)
-        ew_all = reuse.tile([P, W], I32, name="ew_all", align_bytes=64, offset=12288)
-        es_all = reuse.tile([P, W], U8, name="es_all", align_bytes=64, offset=0)
-        w_raw = reuse.tile([P, PACK, H], F32, name="w_raw", align_bytes=64, offset=4096)
-        clamped = keep.tile([P, BLOCKS * V + 32], F32, name="clamped", align_bytes=64)
-        expo = keep.tile([P, BLOCKS * V + 32], F32, name="expo", align_bytes=64)
+        floor = keep.tile([P, 1], F32, name="floor")
 
+        w_raw = placed([P, PACK, H], F32, "w_raw", 0)
+        xs_all = placed([P, T], U8, "xs_all", 8 * KIB)
         nc.vector.memset(xs_all[:].bitcast(I32), 0)
-        zero = reuse.tile([P, 32], F32, name="zero", align_bytes=64, offset=20480 - 64)
-        nc.vector.memset(zero[:], 0.0)
-        nc.vector.tensor_copy(out=clamped[:, BLOCKS * V : BLOCKS * V + 32], in_=zero[:])
+        es_all = placed([P, W], U8, "es_all", 10 * KIB)
         nc.vector.memset(es_all[:].bitcast(I32), 0)
+        seed = placed([P, 32], F32, "seed", 20 * KIB - 64)
+        nc.vector.memset(seed[:], 1.0)
+        floor_at = keep.tile([P, 1], F32, name="floor_at")
+        nc.vector.tensor_scalar(out=floor_at[:], in0=seed[:, 0:1], scalar1=FLOOR_AT, scalar2=None, op0=ALU.mult)
+        nc.scalar.activation(out=floor[:], in_=floor_at[:], func=ACT.Sigmoid)
 
         nc.sync.dma_start(offs_sb[:], offs)
         nc.sync.dma_start(out=w_raw[:], in_=w1.rearrange("(p j) c -> p j c", j=PACK))
-        load_scales(nc.sync, xs_all, x_scales, 0)
-        nc.sync.dma_start(out=xw_all[:], in_=x_words[0].rearrange("p c r -> p (c r)").bitcast(I32))
         nc.sync.dma_start(txt_sb[:], txt)
+        load_scales(nc.sync, xs_all, x_scales, 0)
+        xw_all = placed([P, T], I32, "xw_all", 12 * KIB)
+        nc.sync.dma_start(out=xw_all[:], in_=x_words[0].rearrange("p c r -> p (c r)").bitcast(I32))
         load_scales(nc.sync, es_all, e_scales, E_ROW)
+        ew_all = placed([P, W], I32, "ew_all", 20 * KIB)
         nc.sync.dma_start(out=ew_all[:], in_=e_words[0].rearrange("p c r -> p (c r)").bitcast(I32))
 
-
-        w_bf = keep.tile([P, PACK * H], BF16, name="w_bf", align_bytes=64)
-        w_dst = w_bf[:].rearrange("p (t m j) -> p m j t", t=PACK, j=PACK)
         w_src = w_raw[:].rearrange("p j (m t) -> p m j t", t=PACK)
-        nc.vector.tensor_copy(out=w_dst[:, :64], in_=w_src[:, :64])
-        nc.scalar.copy(out=w_dst[:, 64:], in_=w_src[:, 64:])
+        w_bf = [placed([P, 2 * P * PACK], BF16, "w_bf%d" % half, (28 + 2 * half) * KIB) for half in range(2)]
+        w_dst = [w_bf[half][:].rearrange("p (t m j) -> p m j t", t=2, j=PACK) for half in range(2)]
+        nc.vector.tensor_copy(out=w_dst[0], in_=w_src[:, :, :, 0:2])
+        nc.scalar.copy(out=w_dst[1], in_=w_src[:, :, :, 2:4])
+
         xs = keep.tile([P, S], U8, name="xs", align_bytes=64)
         nc.vector.tensor_copy(xs[:], xs_all[:].indirect(offs_sb[:]))
-        lab_blocks = lab.rearrange("(b p) v -> p b v", p=P)
-        lab_inner = reuse.tile([P, 2, V], F32, name="lab_inner", align_bytes=64, offset=4096)
-        lab_outer = reuse.tile([P, 2, V], F32, name="lab_outer", align_bytes=64, offset=8192)
-        nc.sync.dma_start(out=lab_inner[:], in_=lab_blocks[:, 1:3, :])
-        nc.sync.dma_start(out=lab_outer[:], in_=lab_blocks[:, 0:4:3, :])
-        lab_sb = [lab_outer[:, 0, :], lab_inner[:, 0, :], lab_inner[:, 1, :], lab_outer[:, 1, :]]
+
         w_codes = keep.tile([P, H], U32, name="w_codes", align_bytes=64)
-        w_scales = reuse.tile([P, H], U8, name="w_scales", align_bytes=64, offset=28672)
-        nc.vector.quantize_mx(out=w_codes[:].bitcast(FP8X4), scales=w_scales[:], in_=w_bf[:])
+        w_scales = placed([P, H], U8, "w_scales", 8 * KIB)
+        for half in range(2):
+            cols = slice(half * 2 * P, (half + 1) * 2 * P)
+            nc.vector.quantize_mx(out=w_codes[:, cols].bitcast(FP8X4), scales=w_scales[:, cols], in_=w_bf[half][:])
+
+        lab_sb = []
+        for b in range(BLOCKS):
+            lab_sb.append(placed([P, V], F32, "lab%d" % b, 2 * b * KIB))
 
         xw = keep.tile([P, S], U32, name="xw", align_bytes=64)
         for half in range(2):
@@ -90,8 +97,9 @@ def tile_picked_ysiglip_loss_p_kernel(
                 xw[:, half * 256 : (half + 1) * 256],
                 xw_all[:].bitcast(U32).indirect(offs_sb[:, half * 16 : (half + 1) * 16]),
             )
+        for b in range(BLOCKS):
+            nc.sync.dma_start(out=lab_sb[b][:], in_=lab[b * P : (b + 1) * P, :])
 
-        h_codes, h_scales = [], []
         h_bf = []
         for b in range(BLOCKS):
             tokens = slice(b * P, (b + 1) * P)
@@ -107,14 +115,16 @@ def tile_picked_ysiglip_loss_p_kernel(
                     start=True,
                     stop=True,
                 )
-            h_bf.append(reuse.tile([P, P, PACK], BF16, name="h_bf%d" % b, align_bytes=64, offset=32768 + 2048 * b))
+            h_bf.append(placed([P, P, PACK], BF16, "h_bf%d" % b, (32 + b) * KIB))
             nc.scalar.copy(out=h_bf[b][:], in_=h_ps[:].rearrange("p t n -> p n t"))
 
-        es = keep.tile([P, V], U8, name="es", align_bytes=64)
+        es = placed([P, V], U8, "es", 14 * KIB)
         nc.vector.tensor_copy(es[:], es_all[:].indirect(txt_sb[:]))
 
+        h_codes, h_scales = [], []
+
         def quantize_h(b, offset):
-            h_codes.append(reuse.tile([P, P], U32, name="h_codes%d" % b, align_bytes=64, offset=offset))
+            h_codes.append(placed([P, P], U32, "h_codes%d" % b, offset))
             h_scales.append(keep.tile([P, P], U8, name="h_scales%d" % b, align_bytes=64))
             nc.vector.quantize_mx(
                 out=h_codes[b][:].bitcast(FP8X4),
@@ -122,25 +132,20 @@ def tile_picked_ysiglip_loss_p_kernel(
                 in_=h_bf[b][:].rearrange("p n t -> p (n t)"),
             )
 
-        quantize_h(0, 0)
-        ew = reuse.tile([P, V], U32, name="ew", align_bytes=64, offset=1024)
+        quantize_h(0, 10 * KIB)
+        ew = keep.tile([P, V], U32, name="ew", align_bytes=64)
         for half in range(2):
             nc.vector.tensor_copy(
                 ew[:, half * HALF : (half + 1) * HALF],
                 ew_all[:].bitcast(U32).indirect(txt_sb[:, half * 16 : (half + 1) * 16]),
             )
         for b in range(1, BLOCKS):
-            quantize_h(b, 12288 + 512 * b)
+            quantize_h(b, 20 * KIB + 512 * b)
 
+        products = [(0, 0, HALF), (0, HALF, V), (1, 0, HALF), (1, HALF, V), (2, 0, V), (3, 0, V)]
+        banks = ["y_ps0", "y_ps1", "y_ps2", "y_ps3", "h_ps0", "h_ps1"]
         y_ps = {}
-        for b, lo, hi, bank in [
-            (0, 0, HALF, "y_ps0"),
-            (0, HALF, V, "y_ps1"),
-            (1, HALF, V, "y_ps3"),
-            (2, 0, V, "h_ps0"),
-            (1, 0, HALF, "y_ps2"),
-            (3, 0, V, "h_ps1"),
-        ]:
+        for (b, lo, hi), bank in zip(products, banks):
             acc = psum.tile([P, hi - lo], F32, name="y_ps%d_%d" % (b, lo), tag=bank)
             nc.tensor.matmul_mx(
                 out=acc[:],
@@ -151,82 +156,42 @@ def tile_picked_ysiglip_loss_p_kernel(
                 start=True,
                 stop=True,
             )
-            for c in range(lo, hi, HALF):
-                y_ps[b, c] = acc[:, c - lo : c - lo + HALF]
-            y_ps[b, lo, hi] = acc[:]
+            y_ps[b, lo] = acc[:]
+        y_ps[3, HALF] = y_ps[3, 0][:, HALF:V]
+        y_ps[3, 0] = y_ps[3, 0][:, 0:HALF]
 
-        last_bf = 32768 + 2048 * 3
-        signed = {
-            (1, HALF): reuse.tile([P, HALF], F32, name="signed1", align_bytes=64, offset=last_bf - 512)[:],
-            (0, 0): clamped[:, 2 * V : 2 * V + HALF],
-            (0, HALF): clamped[:, 2 * V + HALF : 3 * V],
-            (1, 0): clamped[:, 3 * V : 3 * V + HALF],
-        }
-        signed2 = reuse.tile([P, V], F32, name="signed2", align_bytes=64, offset=last_bf + 512)
-        signed3 = keep.tile([P, V], F32, name="signed3", align_bytes=64)
-        for c in (0, HALF):
-            signed[2, c] = signed2[:, c : c + HALF]
-            signed[3, c] = signed3[:, c : c + HALF]
-
-        def magnitude(b, lo):
-            nc.scalar.activation(
-                out=clamped[:, b * V + lo : b * V + lo + HALF], in_=y_ps[b, lo], func=ACT.Abs, scale=SCALE, bias=-0.5
-            )
-
-        def signed_logits(dst, src, b, lo, hi):
+        logits = products[:5] + [(3, 0, HALF), (3, HALF, V)]
+        signed = {}
+        prob = keep.tile([P, BLOCKS, V], F32, name="prob", align_bytes=64)
+        for i, (b, lo, hi) in enumerate(logits):
+            signed[b, lo] = placed([P, hi - lo], F32, "signed%d_%d" % (b, lo), (33 + 2 * b + lo // HALF) * KIB)
             nc.vector.scalar_tensor_tensor(
-                out=dst, in0=src, scalar=SHIFT, in1=lab_sb[b][:, lo:hi], op0=ALU.subtract, op1=ALU.mult
+                out=signed[b, lo][:],
+                in0=y_ps[b, lo],
+                scalar=SHIFT,
+                in1=lab_sb[b][:, lo:hi],
+                op0=ALU.subtract,
+                op1=ALU.mult,
+            )
+            nc.scalar.activation(out=prob[:, b, lo:hi], in_=signed[b, lo][:], func=ACT.Sigmoid, scale=SCALE)
+
+        linear = placed([P, BLOCKS, V], F32, "linear", 0)
+        for b, lo, hi in reversed(logits):
+            nc.vector.tensor_scalar(
+                out=linear[:, b, lo:hi], in0=signed[b, lo][:], scalar1=-SCALE, scalar2=None, op0=ALU.mult
             )
 
-        def clamp(src, b, lo, hi):
-            nc.vector.tensor_scalar(
-                out=clamped[:, b * V + lo : b * V + hi],
-                in0=src,
-                scalar1=SCALE,
-                scalar2=-LINEAR_FROM,
+        log_prob = placed([P, BLOCKS, V], F32, "log_prob", 40 * KIB)
+        res = keep.tile([P, BLOCKS, V], F32, name="res", align_bytes=64)
+        pieces = [(b, lo, lo + HALF) for b in range(BLOCKS) for lo in (0, HALF)]
+        for b, lo, hi in pieces:
+            nc.scalar.activation(out=log_prob[:, b, lo:hi], in_=prob[:, b, lo:hi], func=ACT.Ln, bias=floor[:])
+            nc.vector.scalar_tensor_tensor(
+                out=res[:, b, lo:hi],
+                in0=log_prob[:, b, lo:hi],
+                scalar=-1.0,
+                in1=linear[:, b, lo:hi],
                 op0=ALU.mult,
                 op1=ALU.max,
             )
-
-        def exp_minus(b, lo, hi):
-            wide = slice(b * V + lo, b * V + hi + (1 if b * V + hi == BLOCKS * V else 0))
-            nc.scalar.activation(out=expo[:, wide], in_=clamped[:, wide], func=ACT.Exp, scale=-1.0)
-
-        magnitude(0, 0)
-        magnitude(0, HALF)
-        exp_minus(0, 0, V)
-        magnitude(1, 0)
-        signed_logits(signed[1, HALF], y_ps[1, HALF], 1, HALF, V)
-        signed_logits(signed2[:], y_ps[2, 0, V], 2, 0, V)
-        clamp(signed[1, HALF], 1, HALF, V)
-        exp_minus(1, 0, V)
-        signed_logits(signed[3, 0], y_ps[3, 0], 3, 0, HALF)
-        clamp(signed2[:], 2, 0, V)
-        exp_minus(2, 0, V)
-        signed_logits(signed[3, HALF], y_ps[3, HALF], 3, HALF, V)
-        for lo in (0, HALF):
-            clamp(signed[3, lo], 3, lo, lo + HALF)
-            exp_minus(3, lo, lo + HALF)
-
-        by_magnitude = [(0, 0), (0, HALF), (1, 0)]
-        linear = {}
-        for b, lo in by_magnitude:
-            signed_logits(signed[b, lo], y_ps[b, lo], b, lo, lo + HALF)
-        for b, lo in by_magnitude:
-            linear[b, lo] = keep.tile([P, HALF], F32, name="linear%d_%d" % (b, lo), align_bytes=64)
-            nc.vector.tensor_scalar(
-                out=linear[b, lo][:], in0=signed[b, lo], scalar1=-SCALE, scalar2=0.0, op0=ALU.mult, op1=ALU.max
-            )
-
-        one = expo[:, BLOCKS * V : BLOCKS * V + 1]
-        for b, lo in [(1, HALF), (2, 0), (2, HALF), (3, 0), (3, HALF)] + by_magnitude:
-            soft = keep.tile([P, HALF], F32, name="soft%d_%d" % (b, lo), align_bytes=64)
-            nc.scalar.activation(out=soft[:], in_=expo[:, b * V + lo : b * V + lo + HALF], func=ACT.Ln, bias=one)
-            res = keep.tile([P, HALF], F32, name="res%d_%d" % (b, lo), align_bytes=64)
-            if (b, lo) in by_magnitude:
-                nc.vector.tensor_tensor(out=res[:], in0=linear[b, lo][:], in1=soft[:], op=ALU.add)
-            else:
-                nc.vector.scalar_tensor_tensor(
-                    out=res[:], in0=signed[b, lo], scalar=-SCALE, in1=soft[:], op0=ALU.mult, op1=ALU.max
-                )
-            nc.sync.dma_start(out=out[b * P : (b + 1) * P, lo : lo + HALF], in_=res[:])
+            nc.sync.dma_start(out=out[b * P : (b + 1) * P, lo:hi], in_=res[:, b, lo:hi])

@@ -52,37 +52,39 @@ def tile_picked_ysiglip_loss_p_kernel(
         floor = keep.tile([P, 1], F32, name="floor")
 
         w_raw = placed([P, PACK, H], F32, "w_raw", 0)
-        xs_all = placed([P, T], U8, "xs_all", 8 * KIB)
+        xs_all = placed([P, T], U8, "xs_all", 27 * KIB)
         nc.vector.memset(xs_all[:].bitcast(I32), 0)
-        es_all = placed([P, W], U8, "es_all", 10 * KIB)
-        nc.vector.memset(es_all[:].bitcast(I32), 0)
-        seed = placed([P, 32], F32, "seed", 20 * KIB - 64)
-        nc.vector.memset(seed[:], 1.0)
-        floor_at = keep.tile([P, 1], F32, name="floor_at")
-        nc.vector.tensor_scalar(out=floor_at[:], in0=seed[:, 0:1], scalar1=FLOOR_AT, scalar2=None, op0=ALU.mult)
-        nc.scalar.activation(out=floor[:], in_=floor_at[:], func=ACT.Sigmoid)
+        seed = w_raw[:, 2, 0:1]
+        nc.vector.memset(seed, 1.0)
+        floor_at = placed([P, 32], F32, "floor_at", 12 * KIB - 64)
+        nc.vector.tensor_scalar(out=floor_at[:, 0:1], in0=seed, scalar1=FLOOR_AT, scalar2=None, op0=ALU.mult)
+        nc.scalar.activation(out=floor[:], in_=floor_at[:, 0:1], func=ACT.Sigmoid)
 
+        w_rows = w1.rearrange("(p j) c -> p j c", j=PACK)
         nc.sync.dma_start(offs_sb[:], offs)
-        nc.sync.dma_start(out=w_raw[:], in_=w1.rearrange("(p j) c -> p j c", j=PACK))
+        nc.sync.dma_start(out=w_raw[:, 0:2, :], in_=w_rows[:, 0:2, :])
         nc.sync.dma_start(txt_sb[:], txt)
         load_scales(nc.sync, xs_all, x_scales, 0)
+        nc.sync.dma_start(out=w_raw[:, 2:4, :], in_=w_rows[:, 2:4, :])
         xw_all = placed([P, T], I32, "xw_all", 12 * KIB)
         nc.sync.dma_start(out=xw_all[:], in_=x_words[0].rearrange("p c r -> p (c r)").bitcast(I32))
+        es_all = placed([P, W], U8, "es_all", 10 * KIB)
+        nc.vector.memset(es_all[:].bitcast(I32), 0)
         load_scales(nc.sync, es_all, e_scales, E_ROW)
+
+        xs = keep.tile([P, S], U8, name="xs", align_bytes=64)
+        nc.vector.tensor_copy(xs[:], xs_all[:].indirect(offs_sb[:]))
         ew_all = placed([P, W], I32, "ew_all", 20 * KIB)
         nc.sync.dma_start(out=ew_all[:], in_=e_words[0].rearrange("p c r -> p (c r)").bitcast(I32))
 
         w_src = w_raw[:].rearrange("p j (m t) -> p m j t", t=PACK)
-        w_bf = [placed([P, 2 * P * PACK], BF16, "w_bf%d" % half, (28 + 2 * half) * KIB) for half in range(2)]
+        w_bf = [placed([P, 2 * P * PACK], BF16, "w_bf%d" % half, (50 + 2 * half) * KIB) for half in range(2)]
         w_dst = [w_bf[half][:].rearrange("p (t m j) -> p m j t", t=2, j=PACK) for half in range(2)]
         nc.vector.tensor_copy(out=w_dst[0], in_=w_src[:, :, :, 0:2])
         nc.scalar.copy(out=w_dst[1], in_=w_src[:, :, :, 2:4])
 
-        xs = keep.tile([P, S], U8, name="xs", align_bytes=64)
-        nc.vector.tensor_copy(xs[:], xs_all[:].indirect(offs_sb[:]))
-
         w_codes = keep.tile([P, H], U32, name="w_codes", align_bytes=64)
-        w_scales = placed([P, H], U8, "w_scales", 8 * KIB)
+        w_scales = keep.tile([P, H], U8, name="w_scales", align_bytes=64)
         for half in range(2):
             cols = slice(half * 2 * P, (half + 1) * 2 * P)
             nc.vector.quantize_mx(out=w_codes[:, cols].bitcast(FP8X4), scales=w_scales[:, cols], in_=w_bf[half][:])
@@ -118,7 +120,7 @@ def tile_picked_ysiglip_loss_p_kernel(
             h_bf.append(placed([P, P, PACK], BF16, "h_bf%d" % b, (32 + b) * KIB))
             nc.scalar.copy(out=h_bf[b][:], in_=h_ps[:].rearrange("p t n -> p n t"))
 
-        es = placed([P, V], U8, "es", 14 * KIB)
+        es = keep.tile([P, V], U8, name="es", align_bytes=64)
         nc.vector.tensor_copy(es[:], es_all[:].indirect(txt_sb[:]))
 
         h_codes, h_scales = [], []
@@ -132,17 +134,12 @@ def tile_picked_ysiglip_loss_p_kernel(
                 in_=h_bf[b][:].rearrange("p n t -> p (n t)"),
             )
 
-        quantize_h(0, 10 * KIB)
         ew = keep.tile([P, V], U32, name="ew", align_bytes=64)
-        for half in range(2):
-            nc.vector.tensor_copy(
-                ew[:, half * HALF : (half + 1) * HALF],
-                ew_all[:].bitcast(U32).indirect(txt_sb[:, half * 16 : (half + 1) * 16]),
-            )
-        for b in range(1, BLOCKS):
+        nc.vector.tensor_copy(ew[:], ew_all[:].bitcast(U32).indirect(txt_sb[:]))
+        for b in range(BLOCKS):
             quantize_h(b, 20 * KIB + 512 * b)
 
-        products = [(0, 0, HALF), (0, HALF, V), (1, 0, HALF), (1, HALF, V), (2, 0, V), (3, 0, V)]
+        products = [(0, 0, HALF), (0, HALF, V), (1, 0, V), (2, 0, V), (3, 0, V)]
         banks = ["y_ps0", "y_ps1", "y_ps2", "y_ps3", "h_ps0", "h_ps1"]
         y_ps = {}
         for (b, lo, hi), bank in zip(products, banks):
@@ -160,11 +157,11 @@ def tile_picked_ysiglip_loss_p_kernel(
         y_ps[3, HALF] = y_ps[3, 0][:, HALF:V]
         y_ps[3, 0] = y_ps[3, 0][:, 0:HALF]
 
-        logits = products[:5] + [(3, 0, HALF), (3, HALF, V)]
-        signed = {}
         prob = keep.tile([P, BLOCKS, V], F32, name="prob", align_bytes=64)
-        for i, (b, lo, hi) in enumerate(logits):
-            signed[b, lo] = placed([P, hi - lo], F32, "signed%d_%d" % (b, lo), (33 + 2 * b + lo // HALF) * KIB)
+        signed = {}
+
+        def signed_logits(b, lo, hi, offset):
+            signed[b, lo] = placed([P, hi - lo], F32, "signed%d_%d" % (b, lo), offset)
             nc.vector.scalar_tensor_tensor(
                 out=signed[b, lo][:],
                 in0=y_ps[b, lo],
@@ -173,25 +170,44 @@ def tile_picked_ysiglip_loss_p_kernel(
                 op0=ALU.subtract,
                 op1=ALU.mult,
             )
-            nc.scalar.activation(out=prob[:, b, lo:hi], in_=signed[b, lo][:], func=ACT.Sigmoid, scale=SCALE)
 
-        linear = placed([P, BLOCKS, V], F32, "linear", 0)
-        for b, lo, hi in reversed(logits):
+        def linear_part(dst, b, lo):
             nc.vector.tensor_scalar(
-                out=linear[:, b, lo:hi], in0=signed[b, lo][:], scalar1=-SCALE, scalar2=None, op0=ALU.mult
+                out=dst, in0=signed[b, lo][:], scalar1=-SCALE, scalar2=0.0, op0=ALU.mult, op1=ALU.max
             )
 
-        log_prob = placed([P, BLOCKS, V], F32, "log_prob", 40 * KIB)
+        by_magnitude = [(0, 0, HALF)]
+        by_sign = [(0, HALF, V), (1, 0, V), (2, 0, V), (3, 0, HALF), (3, HALF, V)]
+        for b, lo, hi in by_magnitude:
+            magnitude = keep.tile([P, hi - lo], F32, name="magnitude%d_%d" % (b, lo), align_bytes=64)
+            nc.scalar.activation(out=magnitude[:], in_=y_ps[b, lo], func=ACT.Abs, scale=SCALE, bias=-0.5)
+            nc.scalar.activation(out=prob[:, b, lo:hi], in_=magnitude[:], func=ACT.Sigmoid)
+        for b, lo, hi in by_sign:
+            signed_logits(b, lo, hi, (34 + 2 * b + lo // HALF) * KIB)
+            nc.scalar.activation(out=prob[:, b, lo:hi], in_=signed[b, lo][:], func=ACT.Sigmoid, scale=SCALE)
+
+        linear = placed([P, BLOCKS, V], F32, "linear", 7 * KIB + 512)
+        for b, lo, hi in by_sign[-1:] + by_sign[:-1]:
+            linear_part(linear[:, b, lo:hi], b, lo)
+        for i, (b, lo, hi) in enumerate(by_magnitude):
+            signed_logits(b, lo, hi, [5 * KIB + 512, 6 * KIB + 512][i])
+            linear_part(linear[:, b, lo:hi], b, lo)
+
+        log_prob = placed([P, BLOCKS, V], F32, "log_prob", (34 + 7) * KIB)
         res = keep.tile([P, BLOCKS, V], F32, name="res", align_bytes=64)
-        pieces = [(b, lo, lo + HALF) for b in range(BLOCKS) for lo in (0, HALF)]
+        pieces = [(0, HALF, 384), (0, 384, V), (1, 0, HALF), (1, HALF, V), (2, 0, HALF), (2, HALF, V), (3, 0, HALF), (3, HALF, V), (0, 0, 128), (0, 128, HALF)]
+        stores = {(b, hi): lo for b, lo, hi in pieces}
         for b, lo, hi in pieces:
             nc.scalar.activation(out=log_prob[:, b, lo:hi], in_=prob[:, b, lo:hi], func=ACT.Ln, bias=floor[:])
+            first = lo - lo % HALF
             nc.vector.scalar_tensor_tensor(
                 out=res[:, b, lo:hi],
                 in0=log_prob[:, b, lo:hi],
                 scalar=-1.0,
                 in1=linear[:, b, lo:hi],
                 op0=ALU.mult,
-                op1=ALU.max,
+                op1=ALU.add if (b, first, first + HALF) in by_magnitude else ALU.max,
             )
-            nc.sync.dma_start(out=out[b * P : (b + 1) * P, lo:hi], in_=res[:, b, lo:hi])
+            if (b, hi) in stores:
+                start = stores[b, hi]
+                nc.sync.dma_start(out=out[b * P : (b + 1) * P, start:hi], in_=res[:, b, start:hi])

@@ -35,6 +35,14 @@ def load_scales(queue, window, scales, row0):
         )
 
 
+def place_scales(nc, plane, picked, row0):
+    for r in range(4):
+        nc.sync.dma_start(
+            out=plane[row0 + r : P : 32, :].bitcast(I32),
+            in_=picked[8 * r : P : 32, :].bitcast(I32),
+        )
+
+
 def tile_picked_ysiglip_loss_p_kernel(
     tc, x_words, x_scales, w1, e_words, e_scales, lab, offs, txt, out
 ):
@@ -59,18 +67,20 @@ def tile_picked_ysiglip_loss_p_kernel(
         floor_at = placed([P, 32], F32, "floor_at", 12 * KIB - 64)
         nc.vector.tensor_scalar(out=floor_at[:, 0:1], in0=seed, scalar1=FLOOR_AT, scalar2=None, op0=ALU.mult)
         nc.scalar.activation(out=floor[:], in_=floor_at[:, 0:1], func=ACT.Sigmoid)
+        es_all = placed([P, W], U8, "es_all", 8 * KIB)
+        nc.vector.memset(es_all[:].bitcast(I32), 0)
+        es = keep.tile([P, V], U8, name="es", align_bytes=64)
+        nc.gpsimd.memset(es[:].bitcast(I32), 0)
 
         w_rows = w1.rearrange("(p j) c -> p j c", j=PACK)
         nc.sync.dma_start(offs_sb[:], offs)
-        nc.sync.dma_start(out=w_raw[:, 0:2, :], in_=w_rows[:, 0:2, :])
         nc.sync.dma_start(txt_sb[:], txt)
+        nc.sync.dma_start(out=w_raw[:, 0:2, :], in_=w_rows[:, 0:2, :])
         load_scales(nc.sync, xs_all, x_scales, 0)
         nc.sync.dma_start(out=w_raw[:, 2:4, :], in_=w_rows[:, 2:4, :])
+        nc.sync.dma_start(out=es_all[0:P:8, :].bitcast(I32), in_=e_scales[0].bitcast(I32))
         xw_all = placed([P, T], I32, "xw_all", 12 * KIB)
         nc.sync.dma_start(out=xw_all[:], in_=x_words[0].rearrange("p c r -> p (c r)").bitcast(I32))
-        es_all = placed([P, W], U8, "es_all", 10 * KIB)
-        nc.vector.memset(es_all[:].bitcast(I32), 0)
-        load_scales(nc.sync, es_all, e_scales, E_ROW)
 
         xs = keep.tile([P, S], U8, name="xs", align_bytes=64)
         nc.vector.tensor_copy(xs[:], xs_all[:].indirect(offs_sb[:]))
@@ -83,6 +93,10 @@ def tile_picked_ysiglip_loss_p_kernel(
         nc.vector.tensor_copy(out=w_dst[0], in_=w_src[:, :, :, 0:2])
         nc.scalar.copy(out=w_dst[1], in_=w_src[:, :, :, 2:4])
 
+        es_picked = keep.tile([P, V], U8, name="es_picked", align_bytes=64)
+        nc.vector.tensor_copy(es_picked[:], es_all[:].indirect(txt_sb[:]))
+        place_scales(nc, es, es_picked, E_ROW)
+
         w_codes = keep.tile([P, H], U32, name="w_codes", align_bytes=64)
         w_scales = keep.tile([P, H], U8, name="w_scales", align_bytes=64)
         for half in range(2):
@@ -91,7 +105,7 @@ def tile_picked_ysiglip_loss_p_kernel(
 
         lab_sb = []
         for b in range(BLOCKS):
-            lab_sb.append(placed([P, V], F32, "lab%d" % b, 2 * b * KIB))
+            lab_sb.append(placed([P, V], F32, "lab%d" % b, [8, 52, 50, 12][b] * KIB))
 
         xw = keep.tile([P, S], U32, name="xw", align_bytes=64)
         for half in range(2):
@@ -119,9 +133,6 @@ def tile_picked_ysiglip_loss_p_kernel(
                 )
             h_bf.append(placed([P, P, PACK], BF16, "h_bf%d" % b, (32 + b) * KIB))
             nc.scalar.copy(out=h_bf[b][:], in_=h_ps[:].rearrange("p t n -> p n t"))
-
-        es = keep.tile([P, V], U8, name="es", align_bytes=64)
-        nc.vector.tensor_copy(es[:], es_all[:].indirect(txt_sb[:]))
 
         h_codes, h_scales = [], []
 
@@ -186,11 +197,11 @@ def tile_picked_ysiglip_loss_p_kernel(
             signed_logits(b, lo, hi, (34 + 2 * b + lo // HALF) * KIB)
             nc.scalar.activation(out=prob[:, b, lo:hi], in_=signed[b, lo][:], func=ACT.Sigmoid, scale=SCALE)
 
-        linear = placed([P, BLOCKS, V], F32, "linear", 7 * KIB + 512)
+        linear = placed([P, BLOCKS, V], F32, "linear", 13 * KIB + 512)
         for b, lo, hi in by_sign[-1:] + by_sign[:-1]:
             linear_part(linear[:, b, lo:hi], b, lo)
         for i, (b, lo, hi) in enumerate(by_magnitude):
-            signed_logits(b, lo, hi, [5 * KIB + 512, 6 * KIB + 512][i])
+            signed_logits(b, lo, hi, [11 * KIB + 512, 12 * KIB + 512][i])
             linear_part(linear[:, b, lo:hi], b, lo)
 
         log_prob = placed([P, BLOCKS, V], F32, "log_prob", (34 + 7) * KIB)

@@ -25,14 +25,8 @@ SHIFT = 0.5 / 1.5
 FLOOR_AT = -40.0
 
 KIB = 1024
-
-
-def load_scales(queue, window, scales, row0):
-    for r in range(4):
-        queue.dma_start(
-            out=window[row0 + r : P : 32, :].bitcast(I32),
-            in_=scales[0, r:16:4, :].bitcast(I32),
-        )
+E_HEAD = 256
+W_HEAD = 768
 
 
 def place_scales(nc, plane, picked, row0):
@@ -59,35 +53,41 @@ def tile_picked_ysiglip_loss_p_kernel(
         txt_sb = keep.tile([P, V // 16], U16, name="txt_sb")
         floor = keep.tile([P, 1], F32, name="floor")
 
-        w_raw = placed([P, PACK, H], F32, "w_raw", 0)
+        w_raw = placed([P, PACK * H], F32, "w_raw", 0)
         xs_all = placed([P, T], U8, "xs_all", 27 * KIB)
-        nc.vector.memset(xs_all[:].bitcast(I32), 0)
-        seed = w_raw[:, 2, 0:1]
-        nc.vector.memset(seed, 1.0)
-        floor_at = placed([P, 32], F32, "floor_at", 12 * KIB - 64)
-        nc.vector.tensor_scalar(out=floor_at[:, 0:1], in0=seed, scalar1=FLOOR_AT, scalar2=None, op0=ALU.mult)
-        nc.scalar.activation(out=floor[:], in_=floor_at[:, 0:1], func=ACT.Sigmoid)
         es_all = placed([P, W], U8, "es_all", 8 * KIB)
+        nc.vector.memset(xs_all[:].bitcast(I32), 0)
         nc.vector.memset(es_all[:].bitcast(I32), 0)
+        seed = placed([P, 1], F32, "seed", 12 * KIB)
+        nc.gpsimd.memset(seed[:], FLOOR_AT / 2)
+        nc.gpsimd.memset(w_raw[:, W_HEAD : W_HEAD + 1], FLOOR_AT / 2)
+        floor_at = keep.tile([P, 1], F32, name="floor_at")
+        nc.vector.tensor_tensor(out=floor_at[:], in0=seed[:], in1=w_raw[:, W_HEAD : W_HEAD + 1], op=ALU.add)
+        nc.scalar.activation(out=floor[:], in_=floor_at[:], func=ACT.Sigmoid)
+        xs = keep.tile([P, S], U8, name="xs", align_bytes=64)
+        nc.gpsimd.memset(xs[:].bitcast(I32), 0)
         es = keep.tile([P, V], U8, name="es", align_bytes=64)
         nc.gpsimd.memset(es[:].bitcast(I32), 0)
 
-        w_rows = w1.rearrange("(p j) c -> p j c", j=PACK)
+        w_rows = w1.rearrange("(p j) c -> p (j c)", j=PACK)
+        nc.sync.dma_start(out=w_raw[:, 0:W_HEAD], in_=w_rows[:, 0:W_HEAD])
         nc.sync.dma_start(offs_sb[:], offs)
         nc.sync.dma_start(txt_sb[:], txt)
-        nc.sync.dma_start(out=w_raw[:, 0:2, :], in_=w_rows[:, 0:2, :])
-        load_scales(nc.sync, xs_all, x_scales, 0)
-        nc.sync.dma_start(out=w_raw[:, 2:4, :], in_=w_rows[:, 2:4, :])
+        nc.sync.dma_start(out=xs_all[0:P:8, :].bitcast(I32), in_=x_scales[0].bitcast(I32))
         nc.sync.dma_start(out=es_all[0:P:8, :].bitcast(I32), in_=e_scales[0].bitcast(I32))
+        nc.sync.dma_start(out=w_raw[:, W_HEAD:], in_=w_rows[:, W_HEAD:])
         xw_all = placed([P, T], I32, "xw_all", 12 * KIB)
         nc.sync.dma_start(out=xw_all[:], in_=x_words[0].rearrange("p c r -> p (c r)").bitcast(I32))
 
-        xs = keep.tile([P, S], U8, name="xs", align_bytes=64)
-        nc.vector.tensor_copy(xs[:], xs_all[:].indirect(offs_sb[:]))
+        xs_picked = keep.tile([P, S], U8, name="xs_picked", align_bytes=64)
+        nc.vector.tensor_copy(xs_picked[:], xs_all[:].indirect(offs_sb[:]))
         ew_all = placed([P, W], I32, "ew_all", 20 * KIB)
-        nc.sync.dma_start(out=ew_all[:], in_=e_words[0].rearrange("p c r -> p (c r)").bitcast(I32))
+        e_rows = e_words[0].rearrange("p c r -> p (c r)").bitcast(I32)
+        nc.sync.dma_start(out=ew_all[:, 0:E_HEAD], in_=e_rows[:, 0:E_HEAD])
+        place_scales(nc, xs, xs_picked, 0)
+        nc.sync.dma_start(out=ew_all[:, E_HEAD:W], in_=e_rows[:, E_HEAD:W])
 
-        w_src = w_raw[:].rearrange("p j (m t) -> p m j t", t=PACK)
+        w_src = w_raw[:].rearrange("p (j m t) -> p m j t", j=PACK, t=PACK)
         w_bf = [placed([P, 2 * P * PACK], BF16, "w_bf%d" % half, (50 + 2 * half) * KIB) for half in range(2)]
         w_dst = [w_bf[half][:].rearrange("p (t m j) -> p m j t", t=2, j=PACK) for half in range(2)]
         nc.vector.tensor_copy(out=w_dst[0], in_=w_src[:, :, :, 0:2])

@@ -103,6 +103,17 @@ def tile_picked_ysiglip_loss_p_kernel(
             cols = slice(half * 2 * P, (half + 1) * 2 * P)
             nc.vector.quantize_mx(out=w_codes[:, cols].bitcast(FP8X4), scales=w_scales[:, cols], in_=w_bf[half][:])
 
+        warm = psum.tile([P, V], F32, name="warm", tag="y_ps3")
+        nc.tensor.matmul_mx(
+            out=warm[:, 0:256],
+            lhsT=w_codes[:, 0:P].bitcast(FP8X4),
+            lhsT_scale=w_scales[:, 0:P],
+            rhs=w_codes[:, 0:256].bitcast(FP8X4),
+            rhs_scale=xs[:, 0:256],
+            start=True,
+            stop=True,
+        )
+
         lab_sb = []
         for b in range(BLOCKS):
             lab_sb.append(placed([P, V], F32, "lab%d" % b, [8, 52, 50, 12][b] * KIB))
@@ -133,6 +144,16 @@ def tile_picked_ysiglip_loss_p_kernel(
                 )
             h_bf.append(placed([P, P, PACK], BF16, "h_bf%d" % b, (32 + b) * KIB))
             nc.scalar.copy(out=h_bf[b][:], in_=h_ps[:].rearrange("p t n -> p n t"))
+
+        nc.tensor.matmul_mx(
+            out=warm[:, 0:256],
+            lhsT=w_codes[:, 0:P].bitcast(FP8X4),
+            lhsT_scale=w_scales[:, 0:P],
+            rhs=w_codes[:, 0:256].bitcast(FP8X4),
+            rhs_scale=es[E_ROW:P, 0:256],
+            start=True,
+            stop=True,
+        )
 
         h_codes, h_scales = [], []
 

@@ -25,15 +25,19 @@ SHIFT = 0.5 / 1.5
 FLOOR_AT = -40.0
 
 KIB = 1024
+QUARTER = V // 4
+BY_MAGNITUDE = HALF
 E_HEAD = 256
-W_HEAD = 768
+W_HEAD = 384
+X_ROWS = 112
+E_ROWS = 48
 
 
-def place_scales(nc, plane, picked, row0):
+def place_scales(nc, plane, picked, first, row0):
     for r in range(4):
         nc.sync.dma_start(
             out=plane[row0 + r : P : 32, :].bitcast(I32),
-            in_=picked[8 * r : P : 32, :].bitcast(I32),
+            in_=picked[first + r : first + 16 : 4, :].bitcast(I32),
         )
 
 
@@ -56,35 +60,36 @@ def tile_picked_ysiglip_loss_p_kernel(
         w_raw = placed([P, PACK * H], F32, "w_raw", 0)
         xs_all = placed([P, T], U8, "xs_all", 27 * KIB)
         es_all = placed([P, W], U8, "es_all", 8 * KIB)
-        nc.vector.memset(xs_all[:].bitcast(I32), 0)
-        nc.vector.memset(es_all[:].bitcast(I32), 0)
-        seed = placed([P, 1], F32, "seed", 12 * KIB)
-        nc.gpsimd.memset(seed[:], FLOOR_AT / 2)
-        nc.gpsimd.memset(w_raw[:, W_HEAD : W_HEAD + 1], FLOOR_AT / 2)
-        floor_at = keep.tile([P, 1], F32, name="floor_at")
-        nc.vector.tensor_tensor(out=floor_at[:], in0=seed[:], in1=w_raw[:, W_HEAD : W_HEAD + 1], op=ALU.add)
-        nc.scalar.activation(out=floor[:], in_=floor_at[:], func=ACT.Sigmoid)
+        xw_all = placed([P, T], I32, "xw_all", 12 * KIB)
+
+        w_rows = w1.rearrange("(p j) c -> p (j c)", j=PACK)
+        nc.sync.dma_start(out=w_raw[:, 0:W_HEAD], in_=w_rows[:, 0:W_HEAD])
+        nc.sync.dma_start(out=xs_all[X_ROWS : X_ROWS + 16, :].bitcast(I32), in_=x_scales[0].bitcast(I32))
+        nc.sync.dma_start(offs_sb[:], offs)
+        nc.sync.dma_start(out=es_all[E_ROWS : E_ROWS + 16, :].bitcast(I32), in_=e_scales[0].bitcast(I32))
+        nc.sync.dma_start(txt_sb[:], txt)
+        nc.sync.dma_start(out=w_raw[:, W_HEAD:], in_=w_rows[:, W_HEAD:])
+        nc.sync.dma_start(out=xw_all[:], in_=x_words[0].rearrange("p c r -> p (c r)").bitcast(I32))
+
+        one_col = keep.tile([P, 1], F32, name="one_col")
+        nc.vector.memset(one_col[:], 1.0)
+        nc.scalar.activation(out=floor[:], in_=one_col[:], func=ACT.Sigmoid, scale=FLOOR_AT)
+        for lo, hi in [(0, 96), (96, X_ROWS)]:
+            nc.vector.memset(xs_all[lo:hi, :].bitcast(I32), 0)
+        for lo, hi in [(0, 32), (32, E_ROWS)]:
+            nc.vector.memset(es_all[lo:hi, :].bitcast(I32), 0)
+        nc.gpsimd.memset(es_all[64:P, :].bitcast(I32), 0)
         xs = keep.tile([P, S], U8, name="xs", align_bytes=64)
         nc.gpsimd.memset(xs[:].bitcast(I32), 0)
         es = keep.tile([P, V], U8, name="es", align_bytes=64)
         nc.gpsimd.memset(es[:].bitcast(I32), 0)
-
-        w_rows = w1.rearrange("(p j) c -> p (j c)", j=PACK)
-        nc.sync.dma_start(out=w_raw[:, 0:W_HEAD], in_=w_rows[:, 0:W_HEAD])
-        nc.sync.dma_start(offs_sb[:], offs)
-        nc.sync.dma_start(txt_sb[:], txt)
-        nc.sync.dma_start(out=xs_all[0:P:8, :].bitcast(I32), in_=x_scales[0].bitcast(I32))
-        nc.sync.dma_start(out=es_all[0:P:8, :].bitcast(I32), in_=e_scales[0].bitcast(I32))
-        nc.sync.dma_start(out=w_raw[:, W_HEAD:], in_=w_rows[:, W_HEAD:])
-        xw_all = placed([P, T], I32, "xw_all", 12 * KIB)
-        nc.sync.dma_start(out=xw_all[:], in_=x_words[0].rearrange("p c r -> p (c r)").bitcast(I32))
 
         xs_picked = keep.tile([P, S], U8, name="xs_picked", align_bytes=64)
         nc.vector.tensor_copy(xs_picked[:], xs_all[:].indirect(offs_sb[:]))
         ew_all = placed([P, W], I32, "ew_all", 20 * KIB)
         e_rows = e_words[0].rearrange("p c r -> p (c r)").bitcast(I32)
         nc.sync.dma_start(out=ew_all[:, 0:E_HEAD], in_=e_rows[:, 0:E_HEAD])
-        place_scales(nc, xs, xs_picked, 0)
+        place_scales(nc, xs, xs_picked, X_ROWS, 0)
         nc.sync.dma_start(out=ew_all[:, E_HEAD:W], in_=e_rows[:, E_HEAD:W])
 
         w_src = w_raw[:].rearrange("p (j m t) -> p m j t", j=PACK, t=PACK)
@@ -95,7 +100,7 @@ def tile_picked_ysiglip_loss_p_kernel(
 
         es_picked = keep.tile([P, V], U8, name="es_picked", align_bytes=64)
         nc.vector.tensor_copy(es_picked[:], es_all[:].indirect(txt_sb[:]))
-        place_scales(nc, es, es_picked, E_ROW)
+        place_scales(nc, es, es_picked, E_ROWS, E_ROW)
 
         w_codes = keep.tile([P, H], U32, name="w_codes", align_bytes=64)
         w_scales = keep.tile([P, H], U8, name="w_scales", align_bytes=64)
@@ -185,61 +190,70 @@ def tile_picked_ysiglip_loss_p_kernel(
                 start=True,
                 stop=True,
             )
-            y_ps[b, lo] = acc[:]
-        y_ps[3, HALF] = y_ps[3, 0][:, HALF:V]
-        y_ps[3, 0] = y_ps[3, 0][:, 0:HALF]
+            for c in range(lo, hi, QUARTER):
+                y_ps[b * V + c] = (acc, b * V + lo)
 
-        prob = keep.tile([P, BLOCKS, V], F32, name="prob", align_bytes=64)
-        signed = {}
+        def product(lo, hi):
+            acc, first = y_ps[lo]
+            return acc[:, lo - first : hi - first]
 
-        def signed_logits(b, lo, hi, offset):
-            signed[b, lo] = placed([P, hi - lo], F32, "signed%d_%d" % (b, lo), offset)
+        def signed_logits(dst, lo, hi):
             nc.vector.scalar_tensor_tensor(
-                out=signed[b, lo][:],
-                in0=y_ps[b, lo],
+                out=dst,
+                in0=product(lo, hi),
                 scalar=SHIFT,
-                in1=lab_sb[b][:, lo:hi],
+                in1=lab_sb[lo // V][:, lo % V : lo % V + hi - lo],
                 op0=ALU.subtract,
                 op1=ALU.mult,
             )
 
-        def linear_part(dst, b, lo):
-            nc.vector.tensor_scalar(
-                out=dst, in0=signed[b, lo][:], scalar1=-SCALE, scalar2=0.0, op0=ALU.mult, op1=ALU.max
+        def linear_part(dst, src):
+            nc.vector.tensor_scalar(out=dst, in0=src, scalar1=-SCALE, scalar2=0.0, op0=ALU.mult, op1=ALU.max)
+
+        total = BLOCKS * V
+        prob = keep.tile([P, total + 16], F32, name="prob", align_bytes=64)
+        magnitude = keep.tile([P, BY_MAGNITUDE], F32, name="magnitude", align_bytes=64)
+        for lo in range(0, BY_MAGNITUDE, HALF):
+            nc.scalar.activation(
+                out=magnitude[:, lo : lo + HALF], in_=product(lo, lo + HALF), func=ACT.Abs, scale=SCALE, bias=-0.5
             )
+            nc.scalar.activation(out=prob[:, lo : lo + HALF], in_=magnitude[:, lo : lo + HALF], func=ACT.Sigmoid)
 
-        by_magnitude = [(0, 0, HALF)]
-        by_sign = [(0, HALF, V), (1, 0, V), (2, 0, V), (3, 0, HALF), (3, HALF, V)]
-        for b, lo, hi in by_magnitude:
-            magnitude = keep.tile([P, hi - lo], F32, name="magnitude%d_%d" % (b, lo), align_bytes=64)
-            nc.scalar.activation(out=magnitude[:], in_=y_ps[b, lo], func=ACT.Abs, scale=SCALE, bias=-0.5)
-            nc.scalar.activation(out=prob[:, b, lo:hi], in_=magnitude[:], func=ACT.Sigmoid)
-        for b, lo, hi in by_sign:
-            signed_logits(b, lo, hi, (34 + 2 * b + lo // HALF) * KIB)
-            nc.scalar.activation(out=prob[:, b, lo:hi], in_=signed[b, lo][:], func=ACT.Sigmoid, scale=SCALE)
+        signed = placed([P, total], F32, "signed", 35 * KIB)
+        cuts = list(range(BY_MAGNITUDE, total, HALF)) + [total - QUARTER]
+        for lo, hi in zip(cuts[:-1], cuts[1:]):
+            signed_logits(signed[:, lo:hi], lo, hi)
+            nc.scalar.activation(out=prob[:, lo:hi], in_=signed[:, lo:hi], func=ACT.Sigmoid, scale=SCALE)
+        signed_last = keep.tile([P, QUARTER + 1], F32, name="signed_last", align_bytes=64)
+        nc.gpsimd.memset(signed_last[:, QUARTER : QUARTER + 1], 30.0)
+        signed_logits(signed_last[:, 0:QUARTER], total - QUARTER, total)
+        nc.scalar.activation(out=prob[:, total - QUARTER : total + 1], in_=signed_last[:], func=ACT.Sigmoid, scale=SCALE)
+        one = prob[:, total : total + 1]
 
-        linear = placed([P, BLOCKS, V], F32, "linear", 13 * KIB + 512)
-        for b, lo, hi in by_sign[-1:] + by_sign[:-1]:
-            linear_part(linear[:, b, lo:hi], b, lo)
-        for i, (b, lo, hi) in enumerate(by_magnitude):
-            signed_logits(b, lo, hi, [11 * KIB + 512, 12 * KIB + 512][i])
-            linear_part(linear[:, b, lo:hi], b, lo)
+        linear = placed([P, total], F32, "linear", 13 * KIB + 512)
+        for lo, hi in [(BY_MAGNITUDE, 2 * V), (2 * V, total - QUARTER)]:
+            linear_part(linear[:, lo:hi], signed[:, lo:hi])
+        linear_part(linear[:, total - QUARTER : total], signed_last[:, 0:QUARTER])
+        signed_late = placed([P, BY_MAGNITUDE], F32, "signed_late", 12 * KIB + 512 - 4 * BY_MAGNITUDE)
+        for lo in range(0, BY_MAGNITUDE, HALF):
+            signed_logits(signed_late[:, lo : lo + HALF], lo, lo + HALF)
+        linear_part(linear[:, 0:BY_MAGNITUDE], signed_late[:])
 
-        log_prob = placed([P, BLOCKS, V], F32, "log_prob", (34 + 7) * KIB)
-        res = keep.tile([P, BLOCKS, V], F32, name="res", align_bytes=64)
-        pieces = [(0, HALF, 384), (0, 384, V), (1, 0, HALF), (1, HALF, V), (2, 0, HALF), (2, HALF, V), (3, 0, HALF), (3, HALF, V), (0, 0, 128), (0, 128, HALF)]
-        stores = {(b, hi): lo for b, lo, hi in pieces}
-        for b, lo, hi in pieces:
-            nc.scalar.activation(out=log_prob[:, b, lo:hi], in_=prob[:, b, lo:hi], func=ACT.Ln, bias=floor[:])
-            first = lo - lo % HALF
+        log_prob = keep.tile([P, total], F32, name="log_prob", align_bytes=64)
+        res = keep.tile([P, total], F32, name="res", align_bytes=64)
+        pieces = [(256, 384), (384, 512)] + [(lo, lo + HALF) for lo in range(V, total, HALF)] + [(0, 128), (128, 256)]
+        stores = {hi: lo for lo, hi in pieces}
+        for lo, hi in pieces:
+            nc.scalar.activation(out=log_prob[:, lo:hi], in_=prob[:, lo:hi], func=ACT.Ln, bias=floor[:], scale=one)
             nc.vector.scalar_tensor_tensor(
-                out=res[:, b, lo:hi],
-                in0=log_prob[:, b, lo:hi],
+                out=res[:, lo:hi],
+                in0=log_prob[:, lo:hi],
                 scalar=-1.0,
-                in1=linear[:, b, lo:hi],
+                in1=linear[:, lo:hi],
                 op0=ALU.mult,
-                op1=ALU.add if (b, first, first + HALF) in by_magnitude else ALU.max,
+                op1=ALU.add if lo < BY_MAGNITUDE else ALU.max,
             )
-            if (b, hi) in stores:
-                start = stores[b, hi]
-                nc.sync.dma_start(out=out[b * P : (b + 1) * P, start:hi], in_=res[:, b, start:hi])
+            if hi in stores:
+                first = stores[hi]
+                b = first // V
+                nc.sync.dma_start(out=out[b * P : (b + 1) * P, first - b * V : hi - b * V], in_=res[:, first:hi])

@@ -25,8 +25,6 @@ SHIFT = 0.5 / 1.5
 FLOOR_AT = -40.0
 
 KIB = 1024
-QUARTER = V // 4
-BY_MAGNITUDE = HALF
 E_HEAD = 256
 W_HEAD = 384
 X_ROWS = 112
@@ -190,70 +188,61 @@ def tile_picked_ysiglip_loss_p_kernel(
                 start=True,
                 stop=True,
             )
-            for c in range(lo, hi, QUARTER):
-                y_ps[b * V + c] = (acc, b * V + lo)
+            y_ps[b, lo] = acc[:]
+        y_ps[3, HALF] = y_ps[3, 0][:, HALF:V]
+        y_ps[3, 0] = y_ps[3, 0][:, 0:HALF]
 
-        def product(lo, hi):
-            acc, first = y_ps[lo]
-            return acc[:, lo - first : hi - first]
+        prob = keep.tile([P, BLOCKS, V], F32, name="prob", align_bytes=64)
+        signed = {}
 
-        def signed_logits(dst, lo, hi):
+        def signed_logits(b, lo, hi, offset):
+            signed[b, lo] = placed([P, hi - lo], F32, "signed%d_%d" % (b, lo), offset)
             nc.vector.scalar_tensor_tensor(
-                out=dst,
-                in0=product(lo, hi),
+                out=signed[b, lo][:],
+                in0=y_ps[b, lo],
                 scalar=SHIFT,
-                in1=lab_sb[lo // V][:, lo % V : lo % V + hi - lo],
+                in1=lab_sb[b][:, lo:hi],
                 op0=ALU.subtract,
                 op1=ALU.mult,
             )
 
-        def linear_part(dst, src):
-            nc.vector.tensor_scalar(out=dst, in0=src, scalar1=-SCALE, scalar2=0.0, op0=ALU.mult, op1=ALU.max)
-
-        total = BLOCKS * V
-        prob = keep.tile([P, total + 16], F32, name="prob", align_bytes=64)
-        magnitude = keep.tile([P, BY_MAGNITUDE], F32, name="magnitude", align_bytes=64)
-        for lo in range(0, BY_MAGNITUDE, HALF):
-            nc.scalar.activation(
-                out=magnitude[:, lo : lo + HALF], in_=product(lo, lo + HALF), func=ACT.Abs, scale=SCALE, bias=-0.5
+        def linear_part(dst, b, lo):
+            nc.vector.tensor_scalar(
+                out=dst, in0=signed[b, lo][:], scalar1=-SCALE, scalar2=0.0, op0=ALU.mult, op1=ALU.max
             )
-            nc.scalar.activation(out=prob[:, lo : lo + HALF], in_=magnitude[:, lo : lo + HALF], func=ACT.Sigmoid)
 
-        signed = placed([P, total], F32, "signed", 35 * KIB)
-        cuts = list(range(BY_MAGNITUDE, total, HALF)) + [total - QUARTER]
-        for lo, hi in zip(cuts[:-1], cuts[1:]):
-            signed_logits(signed[:, lo:hi], lo, hi)
-            nc.scalar.activation(out=prob[:, lo:hi], in_=signed[:, lo:hi], func=ACT.Sigmoid, scale=SCALE)
-        signed_last = keep.tile([P, QUARTER + 1], F32, name="signed_last", align_bytes=64)
-        nc.gpsimd.memset(signed_last[:, QUARTER : QUARTER + 1], 30.0)
-        signed_logits(signed_last[:, 0:QUARTER], total - QUARTER, total)
-        nc.scalar.activation(out=prob[:, total - QUARTER : total + 1], in_=signed_last[:], func=ACT.Sigmoid, scale=SCALE)
-        one = prob[:, total : total + 1]
+        by_magnitude = [(0, 0, HALF)]
+        by_sign = [(0, HALF, V), (1, 0, V), (2, 0, V), (3, 0, HALF), (3, HALF, V)]
+        for b, lo, hi in by_magnitude:
+            magnitude = keep.tile([P, hi - lo], F32, name="magnitude%d_%d" % (b, lo), align_bytes=64)
+            nc.scalar.activation(out=magnitude[:], in_=y_ps[b, lo], func=ACT.Abs, scale=SCALE, bias=-0.5)
+            nc.scalar.activation(out=prob[:, b, lo:hi], in_=magnitude[:], func=ACT.Sigmoid)
+        for b, lo, hi in by_sign:
+            signed_logits(b, lo, hi, (34 + 2 * b + lo // HALF) * KIB)
+            nc.scalar.activation(out=prob[:, b, lo:hi], in_=signed[b, lo][:], func=ACT.Sigmoid, scale=SCALE)
 
-        linear = placed([P, total], F32, "linear", 13 * KIB + 512)
-        for lo, hi in [(BY_MAGNITUDE, 2 * V), (2 * V, total - QUARTER)]:
-            linear_part(linear[:, lo:hi], signed[:, lo:hi])
-        linear_part(linear[:, total - QUARTER : total], signed_last[:, 0:QUARTER])
-        signed_late = placed([P, BY_MAGNITUDE], F32, "signed_late", 12 * KIB + 512 - 4 * BY_MAGNITUDE)
-        for lo in range(0, BY_MAGNITUDE, HALF):
-            signed_logits(signed_late[:, lo : lo + HALF], lo, lo + HALF)
-        linear_part(linear[:, 0:BY_MAGNITUDE], signed_late[:])
+        linear = placed([P, BLOCKS, V], F32, "linear", 13 * KIB + 512)
+        for b, lo, hi in by_sign[-1:] + by_sign[:-1]:
+            linear_part(linear[:, b, lo:hi], b, lo)
+        for i, (b, lo, hi) in enumerate(by_magnitude):
+            signed_logits(b, lo, hi, [11 * KIB + 512, 12 * KIB + 512][i])
+            linear_part(linear[:, b, lo:hi], b, lo)
 
-        log_prob = keep.tile([P, total], F32, name="log_prob", align_bytes=64)
-        res = keep.tile([P, total], F32, name="res", align_bytes=64)
-        pieces = [(256, 384), (384, 512)] + [(lo, lo + HALF) for lo in range(V, total, HALF)] + [(0, 128), (128, 256)]
-        stores = {hi: lo for lo, hi in pieces}
-        for lo, hi in pieces:
-            nc.scalar.activation(out=log_prob[:, lo:hi], in_=prob[:, lo:hi], func=ACT.Ln, bias=floor[:], scale=one)
+        log_prob = placed([P, BLOCKS, V], F32, "log_prob", (34 + 7) * KIB)
+        res = keep.tile([P, BLOCKS, V], F32, name="res", align_bytes=64)
+        pieces = [(0, HALF, 384), (0, 384, V), (1, 0, HALF), (1, HALF, V), (2, 0, HALF), (2, HALF, V), (3, 0, HALF), (3, HALF, V), (0, 0, 128), (0, 128, HALF)]
+        stores = {(b, hi): lo for b, lo, hi in pieces}
+        for b, lo, hi in pieces:
+            nc.scalar.activation(out=log_prob[:, b, lo:hi], in_=prob[:, b, lo:hi], func=ACT.Ln, bias=floor[:])
+            first = lo - lo % HALF
             nc.vector.scalar_tensor_tensor(
-                out=res[:, lo:hi],
-                in0=log_prob[:, lo:hi],
+                out=res[:, b, lo:hi],
+                in0=log_prob[:, b, lo:hi],
                 scalar=-1.0,
-                in1=linear[:, lo:hi],
+                in1=linear[:, b, lo:hi],
                 op0=ALU.mult,
-                op1=ALU.add if lo < BY_MAGNITUDE else ALU.max,
+                op1=ALU.add if (b, first, first + HALF) in by_magnitude else ALU.max,
             )
-            if hi in stores:
-                first = stores[hi]
-                b = first // V
-                nc.sync.dma_start(out=out[b * P : (b + 1) * P, first - b * V : hi - b * V], in_=res[:, first:hi])
+            if (b, hi) in stores:
+                start = stores[b, hi]
+                nc.sync.dma_start(out=out[b * P : (b + 1) * P, start:hi], in_=res[:, b, start:hi])

@@ -119,7 +119,7 @@ def tile_picked_ysiglip_loss_p_kernel(
 
         lab_sb = []
         for b in range(BLOCKS):
-            lab_sb.append(placed([P, V], F32, "lab%d" % b, [8, 52, 50, 12][b] * KIB))
+            lab_sb.append(placed([P, V], F32, "lab%d" % b, [0, 52, 50, 12][b] * KIB))
 
         xw = keep.tile([P, S], U32, name="xw", align_bytes=64)
         for half in range(2):
@@ -230,7 +230,7 @@ def tile_picked_ysiglip_loss_p_kernel(
 
         log_prob = placed([P, BLOCKS, V], F32, "log_prob", (34 + 7) * KIB)
         res = keep.tile([P, BLOCKS, V], F32, name="res", align_bytes=64)
-        pieces = [(0, HALF, 384), (0, 384, V), (1, 0, HALF), (1, HALF, V), (2, 0, HALF), (2, HALF, V), (3, 0, HALF), (3, HALF, V), (0, 0, 128), (0, 128, HALF)]
+        pieces = [(0, HALF, V)] + [(b, lo, lo + HALF) for b in range(1, BLOCKS) for lo in (0, HALF)] + [(0, 0, HALF)]
         stores = {(b, hi): lo for b, lo, hi in pieces}
         for b, lo, hi in pieces:
             nc.scalar.activation(out=log_prob[:, b, lo:hi], in_=prob[:, b, lo:hi], func=ACT.Ln, bias=floor[:])

@@ -18,24 +18,37 @@ ACT = mybir.ActivationFunctionType
 P = 128
 PACK = 4
 BLOCKS = S // P
-E_ROW = 4
 HALF = V // 2
+SCALE_ROWS = 16
+LIST_HALF = HALF // 16
+
 SCALE = 1.5
+BIAS = -0.5
 SHIFT = 0.5 / 1.5
 FLOOR_AT = -40.0
 
-KIB = 1024
-E_HEAD = 256
-W_HEAD = 384
 X_ROWS = 112
 E_ROWS = 48
+E_ROW = 4
+W_HEAD = 384
+E_HEAD = 256
+
+KIB = 1024
+AT_W_RAW = 0
+AT_ES_ALL = 8 * KIB
+AT_XW_ALL = 12 * KIB
+AT_EW_ALL = 20 * KIB
+AT_XS_ALL = 27 * KIB
+AT_H_BF = 32 * KIB
+AT_SIGNED = 33 * KIB
+AT_W_BF = 50 * KIB
 
 
-def place_scales(nc, plane, picked, first, row0):
+def move_scale_rows(nc, operand, picked, first, row0):
     for r in range(4):
         nc.sync.dma_start(
-            out=plane[row0 + r : P : 32, :].bitcast(I32),
-            in_=picked[first + r : first + 16 : 4, :].bitcast(I32),
+            out=operand[row0 + r : P : 32, :].bitcast(I32),
+            in_=picked[first + r : first + SCALE_ROWS : 4, :].bitcast(I32),
         )
 
 
@@ -55,16 +68,16 @@ def tile_picked_ysiglip_loss_p_kernel(
         txt_sb = keep.tile([P, V // 16], U16, name="txt_sb")
         floor = keep.tile([P, 1], F32, name="floor")
 
-        w_raw = placed([P, PACK * H], F32, "w_raw", 0)
-        xs_all = placed([P, T], U8, "xs_all", 27 * KIB)
-        es_all = placed([P, W], U8, "es_all", 8 * KIB)
-        xw_all = placed([P, T], I32, "xw_all", 12 * KIB)
+        w_raw = placed([P, PACK * H], F32, "w_raw", AT_W_RAW)
+        xs_all = placed([P, T], U8, "xs_all", AT_XS_ALL)
+        es_all = placed([P, W], U8, "es_all", AT_ES_ALL)
+        xw_all = placed([P, T], I32, "xw_all", AT_XW_ALL)
 
         w_rows = w1.rearrange("(p j) c -> p (j c)", j=PACK)
         nc.sync.dma_start(out=w_raw[:, 0:W_HEAD], in_=w_rows[:, 0:W_HEAD])
-        nc.sync.dma_start(out=xs_all[X_ROWS : X_ROWS + 16, :].bitcast(I32), in_=x_scales[0].bitcast(I32))
+        nc.sync.dma_start(out=xs_all[X_ROWS : X_ROWS + SCALE_ROWS, :].bitcast(I32), in_=x_scales[0].bitcast(I32))
         nc.sync.dma_start(offs_sb[:], offs)
-        nc.sync.dma_start(out=es_all[E_ROWS : E_ROWS + 16, :].bitcast(I32), in_=e_scales[0].bitcast(I32))
+        nc.sync.dma_start(out=es_all[E_ROWS : E_ROWS + SCALE_ROWS, :].bitcast(I32), in_=e_scales[0].bitcast(I32))
         nc.sync.dma_start(txt_sb[:], txt)
         nc.sync.dma_start(out=w_raw[:, W_HEAD:], in_=w_rows[:, W_HEAD:])
         nc.sync.dma_start(out=xw_all[:], in_=x_words[0].rearrange("p c r -> p (c r)").bitcast(I32))
@@ -72,33 +85,32 @@ def tile_picked_ysiglip_loss_p_kernel(
         one_col = keep.tile([P, 1], F32, name="one_col")
         nc.vector.memset(one_col[:], 1.0)
         nc.scalar.activation(out=floor[:], in_=one_col[:], func=ACT.Sigmoid, scale=FLOOR_AT)
-        for lo, hi in [(0, 96), (96, X_ROWS)]:
-            nc.vector.memset(xs_all[lo:hi, :].bitcast(I32), 0)
-        for lo, hi in [(0, 32), (32, E_ROWS)]:
-            nc.vector.memset(es_all[lo:hi, :].bitcast(I32), 0)
-        nc.gpsimd.memset(es_all[64:P, :].bitcast(I32), 0)
+
+        nc.vector.memset(xs_all[0:X_ROWS, :].bitcast(I32), 0)
+        nc.vector.memset(es_all[0:E_ROWS, :].bitcast(I32), 0)
+        nc.vector.memset(es_all[E_ROWS + SCALE_ROWS : P, :].bitcast(I32), 0)
         xs = keep.tile([P, S], U8, name="xs", align_bytes=64)
-        nc.gpsimd.memset(xs[:].bitcast(I32), 0)
+        nc.vector.memset(xs[:].bitcast(I32), 0)
         es = keep.tile([P, V], U8, name="es", align_bytes=64)
-        nc.gpsimd.memset(es[:].bitcast(I32), 0)
+        nc.vector.memset(es[:].bitcast(I32), 0)
 
         xs_picked = keep.tile([P, S], U8, name="xs_picked", align_bytes=64)
         nc.vector.tensor_copy(xs_picked[:], xs_all[:].indirect(offs_sb[:]))
-        ew_all = placed([P, W], I32, "ew_all", 20 * KIB)
+        ew_all = placed([P, W], I32, "ew_all", AT_EW_ALL)
         e_rows = e_words[0].rearrange("p c r -> p (c r)").bitcast(I32)
         nc.sync.dma_start(out=ew_all[:, 0:E_HEAD], in_=e_rows[:, 0:E_HEAD])
-        place_scales(nc, xs, xs_picked, X_ROWS, 0)
+        move_scale_rows(nc, xs, xs_picked, X_ROWS, 0)
         nc.sync.dma_start(out=ew_all[:, E_HEAD:W], in_=e_rows[:, E_HEAD:W])
 
         w_src = w_raw[:].rearrange("p (j m t) -> p m j t", j=PACK, t=PACK)
-        w_bf = [placed([P, 2 * P * PACK], BF16, "w_bf%d" % half, (50 + 2 * half) * KIB) for half in range(2)]
+        w_bf = [placed([P, 2 * P * PACK], BF16, "w_bf%d" % half, AT_W_BF + 2 * half * KIB) for half in range(2)]
         w_dst = [w_bf[half][:].rearrange("p (t m j) -> p m j t", t=2, j=PACK) for half in range(2)]
         nc.vector.tensor_copy(out=w_dst[0], in_=w_src[:, :, :, 0:2])
         nc.scalar.copy(out=w_dst[1], in_=w_src[:, :, :, 2:4])
 
         es_picked = keep.tile([P, V], U8, name="es_picked", align_bytes=64)
         nc.vector.tensor_copy(es_picked[:], es_all[:].indirect(txt_sb[:]))
-        place_scales(nc, es, es_picked, E_ROWS, E_ROW)
+        move_scale_rows(nc, es, es_picked, E_ROWS, E_ROW)
 
         w_codes = keep.tile([P, H], U32, name="w_codes", align_bytes=64)
         w_scales = keep.tile([P, H], U8, name="w_scales", align_bytes=64)
@@ -106,33 +118,36 @@ def tile_picked_ysiglip_loss_p_kernel(
             cols = slice(half * 2 * P, (half + 1) * 2 * P)
             nc.vector.quantize_mx(out=w_codes[:, cols].bitcast(FP8X4), scales=w_scales[:, cols], in_=w_bf[half][:])
 
-        warm = psum.tile([P, V], F32, name="warm", tag="y_ps3")
-        nc.tensor.matmul_mx(
-            out=warm[:, 0:256],
-            lhsT=w_codes[:, 0:P].bitcast(FP8X4),
-            lhsT_scale=w_scales[:, 0:P],
-            rhs=w_codes[:, 0:256].bitcast(FP8X4),
-            rhs_scale=xs[:, 0:256],
-            start=True,
-            stop=True,
-        )
+        warm = psum.tile([P, P], F32, name="warm", tag="y_ps3")
 
-        lab_sb = []
-        for b in range(BLOCKS):
-            lab_sb.append(placed([P, V], F32, "lab%d" % b, [0, 52, 50, 12][b] * KIB))
+        def warm_up(moved_scales):
+            nc.tensor.matmul_mx(
+                out=warm[:],
+                lhsT=w_codes[:, 0:P].bitcast(FP8X4),
+                lhsT_scale=w_scales[:, 0:P],
+                rhs=w_codes[:, 0:P].bitcast(FP8X4),
+                rhs_scale=moved_scales,
+                start=True,
+                stop=True,
+            )
+
+        warm_up(xs[:, 0:P])
+
+        lab_at = [AT_W_RAW, AT_W_BF + 2 * KIB, AT_W_BF, AT_XW_ALL]
+        lab_sb = [placed([P, V], F32, "lab%d" % b, lab_at[b]) for b in range(BLOCKS)]
 
         xw = keep.tile([P, S], U32, name="xw", align_bytes=64)
         for half in range(2):
             nc.vector.tensor_copy(
-                xw[:, half * 256 : (half + 1) * 256],
-                xw_all[:].bitcast(U32).indirect(offs_sb[:, half * 16 : (half + 1) * 16]),
+                xw[:, half * HALF : (half + 1) * HALF],
+                xw_all[:].bitcast(U32).indirect(offs_sb[:, half * LIST_HALF : (half + 1) * LIST_HALF]),
             )
         for b in range(BLOCKS):
             nc.sync.dma_start(out=lab_sb[b][:], in_=lab[b * P : (b + 1) * P, :])
 
         h_bf = []
         for b in range(BLOCKS):
-            tokens = slice(b * P, (b + 1) * P)
+            images = slice(b * P, (b + 1) * P)
             h_ps = psum.tile([P, PACK, P], F32, name="h_ps%d" % b, tag="h_ps%d" % b)
             for t in range(PACK):
                 cols = slice(t * P, (t + 1) * P)
@@ -140,28 +155,21 @@ def tile_picked_ysiglip_loss_p_kernel(
                     out=h_ps[:, t, :],
                     lhsT=w_codes[:, cols].bitcast(FP8X4),
                     lhsT_scale=w_scales[:, cols],
-                    rhs=xw[:, tokens].bitcast(FP8X4),
-                    rhs_scale=xs[:, tokens],
+                    rhs=xw[:, images].bitcast(FP8X4),
+                    rhs_scale=xs[:, images],
                     start=True,
                     stop=True,
                 )
-            h_bf.append(placed([P, P, PACK], BF16, "h_bf%d" % b, (32 + b) * KIB))
+            h_bf.append(placed([P, P, PACK], BF16, "h_bf%d" % b, AT_H_BF + b * KIB))
             nc.scalar.copy(out=h_bf[b][:], in_=h_ps[:].rearrange("p t n -> p n t"))
 
-        nc.tensor.matmul_mx(
-            out=warm[:, 0:256],
-            lhsT=w_codes[:, 0:P].bitcast(FP8X4),
-            lhsT_scale=w_scales[:, 0:P],
-            rhs=w_codes[:, 0:256].bitcast(FP8X4),
-            rhs_scale=es[E_ROW:P, 0:256],
-            start=True,
-            stop=True,
-        )
+        warm_up(es[E_ROW:P, 0:P])
 
+        ew = keep.tile([P, V], U32, name="ew", align_bytes=64)
+        nc.vector.tensor_copy(ew[:], ew_all[:].bitcast(U32).indirect(txt_sb[:]))
         h_codes, h_scales = [], []
-
-        def quantize_h(b, offset):
-            h_codes.append(placed([P, P], U32, "h_codes%d" % b, offset))
+        for b in range(BLOCKS):
+            h_codes.append(placed([P, P], U32, "h_codes%d" % b, AT_EW_ALL + 4 * P * b))
             h_scales.append(keep.tile([P, P], U8, name="h_scales%d" % b, align_bytes=64))
             nc.vector.quantize_mx(
                 out=h_codes[b][:].bitcast(FP8X4),
@@ -169,13 +177,9 @@ def tile_picked_ysiglip_loss_p_kernel(
                 in_=h_bf[b][:].rearrange("p n t -> p (n t)"),
             )
 
-        ew = keep.tile([P, V], U32, name="ew", align_bytes=64)
-        nc.vector.tensor_copy(ew[:], ew_all[:].bitcast(U32).indirect(txt_sb[:]))
-        for b in range(BLOCKS):
-            quantize_h(b, 20 * KIB + 512 * b)
-
-        products = [(0, 0, HALF), (0, HALF, V), (1, 0, V), (2, 0, V), (3, 0, V)]
-        banks = ["y_ps0", "y_ps1", "y_ps2", "y_ps3", "h_ps0", "h_ps1"]
+        last = BLOCKS - 1
+        products = [(0, 0, HALF), (0, HALF, V)] + [(b, 0, V) for b in range(1, BLOCKS)]
+        banks = ["y_ps0", "y_ps1", "y_ps2", "y_ps3", "h_ps0"]
         y_ps = {}
         for (b, lo, hi), bank in zip(products, banks):
             acc = psum.tile([P, hi - lo], F32, name="y_ps%d_%d" % (b, lo), tag=bank)
@@ -189,8 +193,8 @@ def tile_picked_ysiglip_loss_p_kernel(
                 stop=True,
             )
             y_ps[b, lo] = acc[:]
-        y_ps[3, HALF] = y_ps[3, 0][:, HALF:V]
-        y_ps[3, 0] = y_ps[3, 0][:, 0:HALF]
+        y_ps[last, HALF] = y_ps[last, 0][:, HALF:V]
+        y_ps[last, 0] = y_ps[last, 0][:, 0:HALF]
 
         prob = keep.tile([P, BLOCKS, V], F32, name="prob", align_bytes=64)
         signed = {}
@@ -206,43 +210,44 @@ def tile_picked_ysiglip_loss_p_kernel(
                 op1=ALU.mult,
             )
 
-        def linear_part(dst, b, lo):
-            nc.vector.tensor_scalar(
-                out=dst, in0=signed[b, lo][:], scalar1=-SCALE, scalar2=0.0, op0=ALU.mult, op1=ALU.max
-            )
+        magnitude = keep.tile([P, HALF], F32, name="magnitude", align_bytes=64)
+        nc.scalar.activation(out=magnitude[:], in_=y_ps[0, 0], func=ACT.Abs, scale=SCALE, bias=BIAS)
+        nc.scalar.activation(out=prob[:, 0, 0:HALF], in_=magnitude[:], func=ACT.Sigmoid)
 
-        by_magnitude = [(0, 0, HALF)]
-        by_sign = [(0, HALF, V), (1, 0, V), (2, 0, V), (3, 0, HALF), (3, HALF, V)]
-        for b, lo, hi in by_magnitude:
-            magnitude = keep.tile([P, hi - lo], F32, name="magnitude%d_%d" % (b, lo), align_bytes=64)
-            nc.scalar.activation(out=magnitude[:], in_=y_ps[b, lo], func=ACT.Abs, scale=SCALE, bias=-0.5)
-            nc.scalar.activation(out=prob[:, b, lo:hi], in_=magnitude[:], func=ACT.Sigmoid)
+        by_sign = products[1:-1] + [(last, 0, HALF), (last, HALF, V)]
         for b, lo, hi in by_sign:
-            signed_logits(b, lo, hi, (34 + 2 * b + lo // HALF) * KIB)
+            signed_logits(b, lo, hi, AT_SIGNED + (2 * b + lo // HALF) * KIB)
             nc.scalar.activation(out=prob[:, b, lo:hi], in_=signed[b, lo][:], func=ACT.Sigmoid, scale=SCALE)
 
-        linear = placed([P, BLOCKS, V], F32, "linear", 13 * KIB + 512)
-        for b, lo, hi in by_sign[-1:] + by_sign[:-1]:
-            linear_part(linear[:, b, lo:hi], b, lo)
-        for i, (b, lo, hi) in enumerate(by_magnitude):
-            signed_logits(b, lo, hi, [11 * KIB + 512, 12 * KIB + 512][i])
-            linear_part(linear[:, b, lo:hi], b, lo)
+        linear = placed([P, BLOCKS, V], F32, "linear", AT_XW_ALL + 3 * KIB // 2)
 
-        log_prob = placed([P, BLOCKS, V], F32, "log_prob", (34 + 7) * KIB)
-        res = keep.tile([P, BLOCKS, V], F32, name="res", align_bytes=64)
-        pieces = [(0, HALF, V)] + [(b, lo, lo + HALF) for b in range(1, BLOCKS) for lo in (0, HALF)] + [(0, 0, HALF)]
-        stores = {(b, hi): lo for b, lo, hi in pieces}
-        for b, lo, hi in pieces:
-            nc.scalar.activation(out=log_prob[:, b, lo:hi], in_=prob[:, b, lo:hi], func=ACT.Ln, bias=floor[:])
-            first = lo - lo % HALF
-            nc.vector.scalar_tensor_tensor(
-                out=res[:, b, lo:hi],
-                in0=log_prob[:, b, lo:hi],
-                scalar=-1.0,
-                in1=linear[:, b, lo:hi],
+        def linear_part(b, lo, hi):
+            nc.vector.tensor_scalar(
+                out=linear[:, b, lo:hi],
+                in0=signed[b, lo][:],
+                scalar1=-SCALE,
+                scalar2=0.0,
                 op0=ALU.mult,
-                op1=ALU.add if (b, first, first + HALF) in by_magnitude else ALU.max,
+                op1=ALU.max,
             )
-            if (b, hi) in stores:
-                start = stores[b, hi]
-                nc.sync.dma_start(out=out[b * P : (b + 1) * P, start:hi], in_=res[:, b, start:hi])
+
+        for b, lo, hi in by_sign[-1:] + by_sign[:-1]:
+            linear_part(b, lo, hi)
+        signed_logits(0, 0, HALF, AT_XW_ALL - KIB // 2)
+        linear_part(0, 0, HALF)
+
+        log_prob = placed([P, BLOCKS, V], F32, "log_prob", AT_SIGNED + (2 * last + 1) * KIB)
+        res = keep.tile([P, BLOCKS, V], F32, name="res", align_bytes=64)
+        halves = [(b, lo) for b in range(BLOCKS) for lo in (0, HALF)]
+        for b, lo in halves[1:] + halves[:1]:
+            cols = slice(lo, lo + HALF)
+            nc.scalar.activation(out=log_prob[:, b, cols], in_=prob[:, b, cols], func=ACT.Ln, bias=floor[:])
+            nc.vector.scalar_tensor_tensor(
+                out=res[:, b, cols],
+                in0=log_prob[:, b, cols],
+                scalar=-1.0,
+                in1=linear[:, b, cols],
+                op0=ALU.mult,
+                op1=ALU.add if (b, lo) == halves[0] else ALU.max,
+            )
+            nc.sync.dma_start(out=out[b * P : (b + 1) * P, cols], in_=res[:, b, cols])

@@ -25,12 +25,12 @@ LIST_HALF = HALF // 16
 SCALE = 1.5
 BIAS = -0.5
 SHIFT = 0.5 / 1.5
-FLOOR_AT = -40.0
+FLOOR_AT = -28.0
 
 X_ROWS = 112
 E_ROWS = 48
 E_ROW = 4
-W_HEAD = 384
+W_HEAD = 256
 E_HEAD = 256
 
 KIB = 1024
@@ -40,8 +40,10 @@ AT_XW_ALL = 12 * KIB
 AT_EW_ALL = 20 * KIB
 AT_XS_ALL = 27 * KIB
 AT_H_BF = 32 * KIB
-AT_SIGNED = 33 * KIB
-AT_W_BF = 50 * KIB
+AT_SIGNED = 36 * KIB
+AT_W_BF = 56 * KIB
+AT_W_CODES = 60 * KIB
+AT_ES_PICKED = 35 * KIB
 
 
 def move_scale_rows(nc, operand, picked, first, row0):
@@ -66,7 +68,7 @@ def tile_picked_ysiglip_loss_p_kernel(
 
         offs_sb = keep.tile([P, S // 16], U16, name="offs_sb")
         txt_sb = keep.tile([P, V // 16], U16, name="txt_sb")
-        floor = keep.tile([P, 1], F32, name="floor")
+        one_half = keep.tile([P, 1], F32, name="one_half")
 
         w_raw = placed([P, PACK * H], F32, "w_raw", AT_W_RAW)
         xs_all = placed([P, T], U8, "xs_all", AT_XS_ALL)
@@ -74,17 +76,18 @@ def tile_picked_ysiglip_loss_p_kernel(
         xw_all = placed([P, T], I32, "xw_all", AT_XW_ALL)
 
         w_rows = w1.rearrange("(p j) c -> p (j c)", j=PACK)
-        nc.sync.dma_start(out=w_raw[:, 0:W_HEAD], in_=w_rows[:, 0:W_HEAD])
-        nc.sync.dma_start(out=xs_all[X_ROWS : X_ROWS + SCALE_ROWS, :].bitcast(I32), in_=x_scales[0].bitcast(I32))
         nc.sync.dma_start(offs_sb[:], offs)
-        nc.sync.dma_start(out=es_all[E_ROWS : E_ROWS + SCALE_ROWS, :].bitcast(I32), in_=e_scales[0].bitcast(I32))
+        nc.scalar.dma_start(out=xs_all[X_ROWS : X_ROWS + SCALE_ROWS, :].bitcast(I32), in_=x_scales[0].bitcast(I32))
         nc.sync.dma_start(txt_sb[:], txt)
-        nc.sync.dma_start(out=w_raw[:, W_HEAD:], in_=w_rows[:, W_HEAD:])
+        nc.scalar.dma_start(out=es_all[E_ROWS : E_ROWS + SCALE_ROWS, :].bitcast(I32), in_=e_scales[0].bitcast(I32))
+        nc.sync.dma_start(out=w_raw[:], in_=w_rows)
         nc.sync.dma_start(out=xw_all[:], in_=x_words[0].rearrange("p c r -> p (c r)").bitcast(I32))
 
         one_col = keep.tile([P, 1], F32, name="one_col")
-        nc.vector.memset(one_col[:], 1.0)
-        nc.scalar.activation(out=floor[:], in_=one_col[:], func=ACT.Sigmoid, scale=FLOOR_AT)
+        nc.vector.memset(one_col[:], 0.0)
+        nc.scalar.activation(out=one_half[:], in_=one_col[:], func=ACT.Sigmoid)
+        last_signed = keep.tile([P, HALF + 1], F32, name="last_signed", align_bytes=64)
+        nc.vector.memset(last_signed[:, HALF : HALF + 1], FLOOR_AT)
 
         nc.vector.memset(xs_all[0:X_ROWS, :].bitcast(I32), 0)
         nc.vector.memset(es_all[0:E_ROWS, :].bitcast(I32), 0)
@@ -98,9 +101,8 @@ def tile_picked_ysiglip_loss_p_kernel(
         nc.vector.tensor_copy(xs_picked[:], xs_all[:].indirect(offs_sb[:]))
         ew_all = placed([P, W], I32, "ew_all", AT_EW_ALL)
         e_rows = e_words[0].rearrange("p c r -> p (c r)").bitcast(I32)
-        nc.sync.dma_start(out=ew_all[:, 0:E_HEAD], in_=e_rows[:, 0:E_HEAD])
         move_scale_rows(nc, xs, xs_picked, X_ROWS, 0)
-        nc.sync.dma_start(out=ew_all[:, E_HEAD:W], in_=e_rows[:, E_HEAD:W])
+        nc.sync.dma_start(out=ew_all[:], in_=e_rows)
 
         w_src = w_raw[:].rearrange("p (j m t) -> p m j t", j=PACK, t=PACK)
         w_bf = [placed([P, 2 * P * PACK], BF16, "w_bf%d" % half, AT_W_BF + 2 * half * KIB) for half in range(2)]
@@ -108,44 +110,50 @@ def tile_picked_ysiglip_loss_p_kernel(
         nc.vector.tensor_copy(out=w_dst[0], in_=w_src[:, :, :, 0:2])
         nc.scalar.copy(out=w_dst[1], in_=w_src[:, :, :, 2:4])
 
-        es_picked = keep.tile([P, V], U8, name="es_picked", align_bytes=64)
+        es_picked = placed([P, V], U8, "es_picked", AT_ES_PICKED)
         nc.vector.tensor_copy(es_picked[:], es_all[:].indirect(txt_sb[:]))
         move_scale_rows(nc, es, es_picked, E_ROWS, E_ROW)
 
-        w_codes = keep.tile([P, H], U32, name="w_codes", align_bytes=64)
+        w_codes = placed([P, H], U32, "w_codes", AT_W_CODES)
         w_scales = keep.tile([P, H], U8, name="w_scales", align_bytes=64)
         for half in range(2):
             cols = slice(half * 2 * P, (half + 1) * 2 * P)
             nc.vector.quantize_mx(out=w_codes[:, cols].bitcast(FP8X4), scales=w_scales[:, cols], in_=w_bf[half][:])
 
-        warm = psum.tile([P, P], F32, name="warm", tag="y_ps3")
+        warm = psum.tile([P, H], F32, name="warm", tag="y_ps3")
 
         def warm_up(moved_scales):
             nc.tensor.matmul_mx(
                 out=warm[:],
                 lhsT=w_codes[:, 0:P].bitcast(FP8X4),
                 lhsT_scale=w_scales[:, 0:P],
-                rhs=w_codes[:, 0:P].bitcast(FP8X4),
+                rhs=w_codes[:].bitcast(FP8X4),
                 rhs_scale=moved_scales,
                 start=True,
                 stop=True,
             )
 
-        warm_up(xs[:, 0:P])
+        warm_up(w_scales[:])
+        warm_up(xs[:])
 
-        lab_at = [AT_W_RAW, AT_W_BF + 2 * KIB, AT_W_BF, AT_XW_ALL]
-        lab_sb = [placed([P, V], F32, "lab%d" % b, lab_at[b]) for b in range(BLOCKS)]
+        lab_rows = lab.rearrange("(b p) v -> p b v", p=P)
+        lab_low = placed([P, 2, V], F32, "lab_low", AT_W_RAW)
+        lab_2 = placed([P, V], F32, "lab_2", AT_W_BF)
+        lab_3 = placed([P, V], F32, "lab_3", AT_XW_ALL)
 
-        xw = keep.tile([P, S], U32, name="xw", align_bytes=64)
+        xw = [keep.tile([P, HALF], U32, name="xw%d" % half, align_bytes=64) for half in range(2)]
         for half in range(2):
             nc.vector.tensor_copy(
-                xw[:, half * HALF : (half + 1) * HALF],
+                xw[half][:],
                 xw_all[:].bitcast(U32).indirect(offs_sb[:, half * LIST_HALF : (half + 1) * LIST_HALF]),
             )
-        for b in range(BLOCKS):
-            nc.sync.dma_start(out=lab_sb[b][:], in_=lab[b * P : (b + 1) * P, :])
+        nc.sync.dma_start(out=lab_low[:], in_=lab_rows[:, 0:2, :])
+        nc.sync.dma_start(out=lab_2[:], in_=lab_rows[:, 2, :])
+        nc.sync.dma_start(out=lab_3[:], in_=lab_rows[:, 3, :])
 
-        h_bf = []
+        h_late = keep.tile([P, 2, P, PACK], BF16, name="h_late", align_bytes=64)
+        h_bf = [placed([P, P, PACK], BF16, "h_bf%d" % b, AT_H_BF + b * KIB)[:] for b in range(2)]
+        h_bf += [h_late[:, 0], h_late[:, 1]]
         for b in range(BLOCKS):
             images = slice(b * P, (b + 1) * P)
             h_ps = psum.tile([P, PACK, P], F32, name="h_ps%d" % b, tag="h_ps%d" % b)
@@ -155,99 +163,119 @@ def tile_picked_ysiglip_loss_p_kernel(
                     out=h_ps[:, t, :],
                     lhsT=w_codes[:, cols].bitcast(FP8X4),
                     lhsT_scale=w_scales[:, cols],
-                    rhs=xw[:, images].bitcast(FP8X4),
+                    rhs=xw[b // 2][:, (b % 2) * P : (b % 2 + 1) * P].bitcast(FP8X4),
                     rhs_scale=xs[:, images],
                     start=True,
                     stop=True,
                 )
-            h_bf.append(placed([P, P, PACK], BF16, "h_bf%d" % b, AT_H_BF + b * KIB))
-            nc.scalar.copy(out=h_bf[b][:], in_=h_ps[:].rearrange("p t n -> p n t"))
+            nc.scalar.copy(out=h_bf[b], in_=h_ps[:].rearrange("p t n -> p n t"))
+        h_codes = [keep.tile([P, 2 * P], U32, name="h_codes%d" % pair, align_bytes=64) for pair in range(2)]
+        early_scales = [placed([P, P], U8, "h_scales%d" % b, AT_ES_PICKED + b * P) for b in range(2)]
+        late_scales = [placed([P, P], U8, "h_scales%d" % (2 + b), AT_H_BF + KIB + b * P) for b in range(2)]
+        h_scales = [tile[:] for tile in early_scales + late_scales]
+        ew = [
+            keep.tile([P, HALF], U32, name="ew0", align_bytes=64),
+            placed([P, HALF], U32, "ew1", AT_H_BF),
+        ]
 
-        warm_up(es[E_ROW:P, 0:P])
+        def gather_e_words(half):
+            nc.vector.tensor_copy(
+                ew[half][:],
+                ew_all[:].bitcast(U32).indirect(txt_sb[:, half * LIST_HALF : (half + 1) * LIST_HALF]),
+            )
 
-        ew = keep.tile([P, V], U32, name="ew", align_bytes=64)
-        nc.vector.tensor_copy(ew[:], ew_all[:].bitcast(U32).indirect(txt_sb[:]))
-        h_codes, h_scales = [], []
-        for b in range(BLOCKS):
-            h_codes.append(placed([P, P], U32, "h_codes%d" % b, AT_EW_ALL + 4 * P * b))
-            h_scales.append(keep.tile([P, P], U8, name="h_scales%d" % b, align_bytes=64))
+        def quantise_h(b):
             nc.vector.quantize_mx(
-                out=h_codes[b][:].bitcast(FP8X4),
-                scales=h_scales[b][:],
-                in_=h_bf[b][:].rearrange("p n t -> p (n t)"),
+                out=h_codes[b // 2][:, (b % 2) * P : (b % 2 + 1) * P].bitcast(FP8X4),
+                scales=h_scales[b],
+                in_=h_bf[b].rearrange("p n t -> p (n t)"),
             )
 
-        last = BLOCKS - 1
-        products = [(0, 0, HALF), (0, HALF, V)] + [(b, 0, V) for b in range(1, BLOCKS)]
-        banks = ["y_ps0", "y_ps1", "y_ps2", "y_ps3", "h_ps0"]
-        y_ps = {}
-        for (b, lo, hi), bank in zip(products, banks):
-            acc = psum.tile([P, hi - lo], F32, name="y_ps%d_%d" % (b, lo), tag=bank)
-            nc.tensor.matmul_mx(
-                out=acc[:],
-                lhsT=h_codes[b][:].bitcast(FP8X4),
-                lhsT_scale=h_scales[b][:],
-                rhs=ew[:, lo:hi].bitcast(FP8X4),
-                rhs_scale=es[E_ROW:P, lo:hi],
-                start=True,
-                stop=True,
-            )
-            y_ps[b, lo] = acc[:]
-        y_ps[last, HALF] = y_ps[last, 0][:, HALF:V]
-        y_ps[last, 0] = y_ps[last, 0][:, 0:HALF]
+        for half in range(2):
+            gather_e_words(half)
+            quantise_h(2 * half)
+            quantise_h(2 * half + 1)
 
-        prob = keep.tile([P, BLOCKS, V], F32, name="prob", align_bytes=64)
+        def products(name, bank, parts):
+            acc = psum.tile([P, 2, HALF], F32, name=name, tag=bank)
+            for slot, (b, half) in enumerate(parts):
+                cols = slice((b % 2) * P, (b % 2 + 1) * P)
+                nc.tensor.matmul_mx(
+                    out=acc[:, slot, :],
+                    lhsT=h_codes[b // 2][:, cols].bitcast(FP8X4),
+                    lhsT_scale=h_scales[b],
+                    rhs=ew[half][:].bitcast(FP8X4),
+                    rhs_scale=es[E_ROW:P, half * HALF : (half + 1) * HALF],
+                    start=True,
+                    stop=True,
+                )
+            return acc
+
+        y_first = products("y_first", "y_ps0", [(0, 0), (1, 0)])
+        y_second = products("y_second", "y_ps1", [(0, 1), (1, 1)])
+        y_2 = products("y_2", "y_ps2", [(2, 0), (2, 1)])
+        y_3 = products("y_3", "y_ps3", [(3, 0), (3, 1)])
+
+        def signed_logits(name, y, labels, offset):
+            tile = placed(list(y.shape), F32, name, offset)
+            nc.vector.scalar_tensor_tensor(
+                out=tile[:], in0=y, scalar=SHIFT, in1=labels, op0=ALU.subtract, op1=ALU.mult
+            )
+            return tile
+
+        tanh_first = keep.tile([P, 2, HALF], F32, name="tanh_first", align_bytes=64)
+        nc.scalar.activation(out=tanh_first[:], in_=y_second[:], func=ACT.Tanh, scale=SCALE / 2, bias=BIAS / 2)
+
+        order = [(0, 0), (1, 0), (2, 0), (2, 1), (3, 0), (3, 1), (0, 1), (1, 1)]
+        prob_row = keep.tile([P, 6 * HALF + 1], F32, name="prob_row", align_bytes=64)
+        prob = prob_row[:, 0 : 6 * HALF].rearrange("p (n v) -> p n v", v=HALF)
+        floor = prob_row[:, 6 * HALF : 6 * HALF + 1]
+        halves_of = lambda tile: tile[:].rearrange("p (h v) -> p h v", h=2)
+        by_sign = [
+            (0, 2, y_first[:], lab_low[:, :, 0:HALF]),
+            (2, 4, y_2[:], halves_of(lab_2)),
+            (4, 5, y_3[:, 0:1, :], halves_of(lab_3)[:, 0:1, :]),
+            (5, 6, y_3[:, 1:2, :], halves_of(lab_3)[:, 1:2, :]),
+        ]
         signed = {}
+        for lo, hi, y, labels in by_sign[:-1]:
+            signed[lo] = signed_logits("signed%d" % lo, y, labels, AT_SIGNED + lo * KIB)
+            nc.scalar.activation(out=prob[:, lo:hi, :], in_=signed[lo][:], func=ACT.Sigmoid, scale=SCALE)
+        lo, hi, y, labels = by_sign[-1]
+        signed[lo] = last_signed[:, 0:HALF].rearrange("p (n v) -> p n v", n=1)
+        nc.vector.scalar_tensor_tensor(
+            out=signed[lo], in0=y, scalar=SHIFT, in1=labels, op0=ALU.subtract, op1=ALU.mult
+        )
+        nc.scalar.activation(out=prob_row[:, lo * HALF :], in_=last_signed[:], func=ACT.Sigmoid, scale=SCALE)
+        linear = placed([P, 8, HALF], F32, "linear", AT_XW_ALL + 3 * KIB // 2)
 
-        def signed_logits(b, lo, hi, offset):
-            signed[b, lo] = placed([P, hi - lo], F32, "signed%d_%d" % (b, lo), offset)
-            nc.vector.scalar_tensor_tensor(
-                out=signed[b, lo][:],
-                in0=y_ps[b, lo],
-                scalar=SHIFT,
-                in1=lab_sb[b][:, lo:hi],
-                op0=ALU.subtract,
-                op1=ALU.mult,
-            )
-
-        magnitude = keep.tile([P, HALF], F32, name="magnitude", align_bytes=64)
-        nc.scalar.activation(out=magnitude[:], in_=y_ps[0, 0], func=ACT.Abs, scale=SCALE, bias=BIAS)
-        nc.scalar.activation(out=prob[:, 0, 0:HALF], in_=magnitude[:], func=ACT.Sigmoid)
-
-        by_sign = products[1:-1] + [(last, 0, HALF), (last, HALF, V)]
-        for b, lo, hi in by_sign:
-            signed_logits(b, lo, hi, AT_SIGNED + (2 * b + lo // HALF) * KIB)
-            nc.scalar.activation(out=prob[:, b, lo:hi], in_=signed[b, lo][:], func=ACT.Sigmoid, scale=SCALE)
-
-        linear = placed([P, BLOCKS, V], F32, "linear", AT_XW_ALL + 3 * KIB // 2)
-
-        def linear_part(b, lo, hi):
+        def linear_part(lo, hi):
             nc.vector.tensor_scalar(
-                out=linear[:, b, lo:hi],
-                in0=signed[b, lo][:],
-                scalar1=-SCALE,
-                scalar2=0.0,
-                op0=ALU.mult,
-                op1=ALU.max,
+                out=linear[:, lo:hi, :], in0=signed[lo][:], scalar1=-SCALE, scalar2=0.0, op0=ALU.mult, op1=ALU.max
             )
 
-        for b, lo, hi in by_sign[-1:] + by_sign[:-1]:
-            linear_part(b, lo, hi)
-        signed_logits(0, 0, HALF, AT_XW_ALL - KIB // 2)
-        linear_part(0, 0, HALF)
+        for lo, hi, y, labels in by_sign:
+            linear_part(lo, hi)
+        signed[6] = signed_logits("signed6", y_second[:], lab_low[:, :, HALF:V], AT_XW_ALL - 3 * KIB // 2)
+        magnitude = placed([P, 2, HALF], F32, "magnitude", AT_SIGNED)
+        nc.vector.scalar_tensor_tensor(
+            out=magnitude[:], in0=tanh_first[:], scalar=-1.0, in1=tanh_first[:], op0=ALU.mult, op1=ALU.max
+        )
+        linear_part(6, 8)
 
-        log_prob = placed([P, BLOCKS, V], F32, "log_prob", AT_SIGNED + (2 * last + 1) * KIB)
-        res = keep.tile([P, BLOCKS, V], F32, name="res", align_bytes=64)
-        halves = [(b, lo) for b in range(BLOCKS) for lo in (0, HALF)]
-        for b, lo in halves[1:] + halves[:1]:
-            cols = slice(lo, lo + HALF)
-            nc.scalar.activation(out=log_prob[:, b, cols], in_=prob[:, b, cols], func=ACT.Ln, bias=floor[:])
+        log_prob = keep.tile([P, 8, HALF], F32, name="log_prob", align_bytes=64)
+        res = keep.tile([P, 8, HALF], F32, name="res", align_bytes=64)
+        for n, (b, half) in enumerate(order):
+            if n < 6:
+                nc.scalar.activation(out=log_prob[:, n, :], in_=prob[:, n, :], func=ACT.Ln, bias=floor)
+            else:
+                nc.scalar.activation(out=log_prob[:, n, :], in_=magnitude[:, n - 6, :], func=ACT.Ln, scale=0.5, bias=one_half[:])
             nc.vector.scalar_tensor_tensor(
-                out=res[:, b, cols],
-                in0=log_prob[:, b, cols],
+                out=res[:, n, :],
+                in0=log_prob[:, n, :],
                 scalar=-1.0,
-                in1=linear[:, b, cols],
+                in1=linear[:, n, :],
                 op0=ALU.mult,
-                op1=ALU.add if (b, lo) == halves[0] else ALU.max,
+                op1=ALU.max if n < 6 else ALU.add,
             )
-            nc.sync.dma_start(out=out[b * P : (b + 1) * P, cols], in_=res[:, b, cols])
+            nc.sync.dma_start(out=out[b * P : (b + 1) * P, half * HALF : (half + 1) * HALF], in_=res[:, n, :])

@@ -76,11 +76,12 @@ def tile_picked_ysiglip_loss_p_kernel(
         xw_all = placed([P, T], I32, "xw_all", AT_XW_ALL)
 
         w_rows = w1.rearrange("(p j) c -> p (j c)", j=PACK)
+        nc.sync.dma_start(out=xs_all[X_ROWS : X_ROWS + SCALE_ROWS, :].bitcast(I32), in_=x_scales[0].bitcast(I32))
         nc.sync.dma_start(offs_sb[:], offs)
-        nc.scalar.dma_start(out=xs_all[X_ROWS : X_ROWS + SCALE_ROWS, :].bitcast(I32), in_=x_scales[0].bitcast(I32))
+        nc.sync.dma_start(out=w_raw[:, 0:W_HEAD], in_=w_rows[:, 0:W_HEAD])
+        nc.sync.dma_start(out=es_all[E_ROWS : E_ROWS + SCALE_ROWS, :].bitcast(I32), in_=e_scales[0].bitcast(I32))
         nc.sync.dma_start(txt_sb[:], txt)
-        nc.scalar.dma_start(out=es_all[E_ROWS : E_ROWS + SCALE_ROWS, :].bitcast(I32), in_=e_scales[0].bitcast(I32))
-        nc.sync.dma_start(out=w_raw[:], in_=w_rows)
+        nc.sync.dma_start(out=w_raw[:, W_HEAD:], in_=w_rows[:, W_HEAD:])
         nc.sync.dma_start(out=xw_all[:], in_=x_words[0].rearrange("p c r -> p (c r)").bitcast(I32))
 
         one_col = keep.tile([P, 1], F32, name="one_col")

@@ -42,7 +42,7 @@ AT_XS_ALL = 27 * KIB
 AT_H_BF = 32 * KIB
 AT_SIGNED = 36 * KIB
 AT_W_BF = 56 * KIB
-AT_W_CODES = 60 * KIB
+AT_W_CODES = 70 * KIB
 AT_ES_PICKED = 35 * KIB
 
 
@@ -87,8 +87,8 @@ def tile_picked_ysiglip_loss_p_kernel(
         one_col = keep.tile([P, 1], F32, name="one_col")
         nc.vector.memset(one_col[:], 0.0)
         nc.scalar.activation(out=one_half[:], in_=one_col[:], func=ACT.Sigmoid)
-        last_signed = keep.tile([P, HALF + 1], F32, name="last_signed", align_bytes=64)
-        nc.vector.memset(last_signed[:, HALF : HALF + 1], FLOOR_AT)
+        last_signed = keep.tile([P, V + 1], F32, name="last_signed", align_bytes=64)
+        nc.vector.memset(last_signed[:, V : V + 1], FLOOR_AT)
 
         nc.vector.memset(xs_all[0:X_ROWS, :].bitcast(I32), 0)
         nc.vector.memset(es_all[0:E_ROWS, :].bitcast(I32), 0)
@@ -137,10 +137,8 @@ def tile_picked_ysiglip_loss_p_kernel(
         warm_up(w_scales[:])
         warm_up(xs[:])
 
-        lab_rows = lab.rearrange("(b p) v -> p b v", p=P)
-        lab_low = placed([P, 2, V], F32, "lab_low", AT_W_RAW)
-        lab_2 = placed([P, V], F32, "lab_2", AT_W_BF)
-        lab_3 = placed([P, V], F32, "lab_3", AT_XW_ALL)
+        lab_at = {0: AT_W_RAW, 1: AT_W_RAW + 2 * KIB, 3: AT_W_BF, 2: AT_XW_ALL}
+        lab_sb = {b: placed([P, V], F32, "lab%d" % b, at) for b, at in lab_at.items()}
 
         xw = [keep.tile([P, HALF], U32, name="xw%d" % half, align_bytes=64) for half in range(2)]
         for half in range(2):
@@ -148,9 +146,8 @@ def tile_picked_ysiglip_loss_p_kernel(
                 xw[half][:],
                 xw_all[:].bitcast(U32).indirect(offs_sb[:, half * LIST_HALF : (half + 1) * LIST_HALF]),
             )
-        nc.sync.dma_start(out=lab_low[:], in_=lab_rows[:, 0:2, :])
-        nc.sync.dma_start(out=lab_2[:], in_=lab_rows[:, 2, :])
-        nc.sync.dma_start(out=lab_3[:], in_=lab_rows[:, 3, :])
+        for b in lab_at:
+            nc.sync.dma_start(out=lab_sb[b][:], in_=lab[b * P : (b + 1) * P, :])
 
         h_late = keep.tile([P, 2, P, PACK], BF16, name="h_late", align_bytes=64)
         h_bf = [placed([P, P, PACK], BF16, "h_bf%d" % b, AT_H_BF + b * KIB)[:] for b in range(2)]
@@ -170,113 +167,107 @@ def tile_picked_ysiglip_loss_p_kernel(
                     stop=True,
                 )
             nc.scalar.copy(out=h_bf[b], in_=h_ps[:].rearrange("p t n -> p n t"))
-        h_codes = [keep.tile([P, 2 * P], U32, name="h_codes%d" % pair, align_bytes=64) for pair in range(2)]
-        early_scales = [placed([P, P], U8, "h_scales%d" % b, AT_ES_PICKED + b * P) for b in range(2)]
-        late_scales = [placed([P, P], U8, "h_scales%d" % (2 + b), AT_H_BF + KIB + b * P) for b in range(2)]
-        h_scales = [tile[:] for tile in early_scales + late_scales]
-        ew = [
-            keep.tile([P, HALF], U32, name="ew0", align_bytes=64),
-            placed([P, HALF], U32, "ew1", AT_H_BF),
-        ]
-
-        def gather_e_words(half):
-            nc.vector.tensor_copy(
-                ew[half][:],
-                ew_all[:].bitcast(U32).indirect(txt_sb[:, half * LIST_HALF : (half + 1) * LIST_HALF]),
-            )
+        h_codes = keep.tile([P, S], U32, name="h_codes", align_bytes=64)
+        h_scales = [placed([P, P], U8, "h_scales%d" % b, AT_ES_PICKED + b * P) for b in range(BLOCKS)]
 
         def quantise_h(b):
             nc.vector.quantize_mx(
-                out=h_codes[b // 2][:, (b % 2) * P : (b % 2 + 1) * P].bitcast(FP8X4),
-                scales=h_scales[b],
+                out=h_codes[:, b * P : (b + 1) * P].bitcast(FP8X4),
+                scales=h_scales[b][:],
                 in_=h_bf[b].rearrange("p n t -> p (n t)"),
             )
 
-        for half in range(2):
-            gather_e_words(half)
-            quantise_h(2 * half)
-            quantise_h(2 * half + 1)
+        ew = keep.tile([P, V], U32, name="ew", align_bytes=64)
+        nc.vector.tensor_copy(ew[:], ew_all[:].bitcast(U32).indirect(txt_sb[:]))
+        whole, low, high = slice(0, V), slice(0, HALF), slice(HALF, V)
+        y_ps = {}
 
-        def products(name, bank, parts):
-            acc = psum.tile([P, 2, HALF], F32, name=name, tag=bank)
-            for slot, (b, half) in enumerate(parts):
-                cols = slice((b % 2) * P, (b % 2 + 1) * P)
-                nc.tensor.matmul_mx(
-                    out=acc[:, slot, :],
-                    lhsT=h_codes[b // 2][:, cols].bitcast(FP8X4),
-                    lhsT_scale=h_scales[b],
-                    rhs=ew[half][:].bitcast(FP8X4),
-                    rhs_scale=es[E_ROW:P, half * HALF : (half + 1) * HALF],
-                    start=True,
-                    stop=True,
-                )
-            return acc
-
-        y_first = products("y_first", "y_ps0", [(0, 0), (1, 0)])
-        y_second = products("y_second", "y_ps1", [(0, 1), (1, 1)])
-        y_2 = products("y_2", "y_ps2", [(2, 0), (2, 1)])
-        y_3 = products("y_3", "y_ps3", [(3, 0), (3, 1)])
-
-        def signed_logits(name, y, labels, offset):
-            tile = placed(list(y.shape), F32, name, offset)
-            nc.vector.scalar_tensor_tensor(
-                out=tile[:], in0=y, scalar=SHIFT, in1=labels, op0=ALU.subtract, op1=ALU.mult
+        def product(b, cols, bank):
+            acc = psum.tile([P, V], F32, name="y_ps%d_%d" % (b, cols.start), tag=bank)
+            nc.tensor.matmul_mx(
+                out=acc[:, cols],
+                lhsT=h_codes[:, b * P : (b + 1) * P].bitcast(FP8X4),
+                lhsT_scale=h_scales[b][:],
+                rhs=ew[:, cols].bitcast(FP8X4),
+                rhs_scale=es[E_ROW:P, cols],
+                start=True,
+                stop=True,
             )
-            return tile
+            y_ps[b, cols.start] = acc
+            y_ps.setdefault((b, HALF), acc)
 
-        tanh_first = keep.tile([P, 2, HALF], F32, name="tanh_first", align_bytes=64)
-        nc.scalar.activation(out=tanh_first[:], in_=y_second[:], func=ACT.Tanh, scale=SCALE / 2, bias=BIAS / 2)
+        quantise_h(0)
+        product(0, high, "h_ps0")
+        product(0, low, "y_ps0")
+        for b in range(1, BLOCKS):
+            quantise_h(b)
+            product(b, whole, "y_ps%d" % b)
 
-        order = [(0, 0), (1, 0), (2, 0), (2, 1), (3, 0), (3, 1), (0, 1), (1, 1)]
-        prob_row = keep.tile([P, 6 * HALF + 1], F32, name="prob_row", align_bytes=64)
-        prob = prob_row[:, 0 : 6 * HALF].rearrange("p (n v) -> p n v", v=HALF)
-        floor = prob_row[:, 6 * HALF : 6 * HALF + 1]
-        halves_of = lambda tile: tile[:].rearrange("p (h v) -> p h v", h=2)
-        by_sign = [
-            (0, 2, y_first[:], lab_low[:, :, 0:HALF]),
-            (2, 4, y_2[:], halves_of(lab_2)),
-            (4, 5, y_3[:, 0:1, :], halves_of(lab_3)[:, 0:1, :]),
-            (5, 6, y_3[:, 1:2, :], halves_of(lab_3)[:, 1:2, :]),
-        ]
-        signed = {}
-        for lo, hi, y, labels in by_sign[:-1]:
-            signed[lo] = signed_logits("signed%d" % lo, y, labels, AT_SIGNED + lo * KIB)
-            nc.scalar.activation(out=prob[:, lo:hi, :], in_=signed[lo][:], func=ACT.Sigmoid, scale=SCALE)
-        lo, hi, y, labels = by_sign[-1]
-        signed[lo] = last_signed[:, 0:HALF].rearrange("p (n v) -> p n v", n=1)
-        nc.vector.scalar_tensor_tensor(
-            out=signed[lo], in0=y, scalar=SHIFT, in1=labels, op0=ALU.subtract, op1=ALU.mult
-        )
-        nc.scalar.activation(out=prob_row[:, lo * HALF :], in_=last_signed[:], func=ACT.Sigmoid, scale=SCALE)
-        linear = placed([P, 8, HALF], F32, "linear", AT_XW_ALL + 3 * KIB // 2)
-
-        def linear_part(lo, hi):
-            nc.vector.tensor_scalar(
-                out=linear[:, lo:hi, :], in0=signed[lo][:], scalar1=-SCALE, scalar2=0.0, op0=ALU.mult, op1=ALU.max
+        def signed_logits(dst, b, cols):
+            nc.vector.scalar_tensor_tensor(
+                out=dst, in0=y_ps[b, cols.start][:, cols], scalar=SHIFT, in1=lab_sb[b][:, cols], op0=ALU.subtract, op1=ALU.mult
             )
 
-        for lo, hi, y, labels in by_sign:
-            linear_part(lo, hi)
-        signed[6] = signed_logits("signed6", y_second[:], lab_low[:, :, HALF:V], AT_XW_ALL - 3 * KIB // 2)
-        magnitude = placed([P, 2, HALF], F32, "magnitude", AT_SIGNED)
-        nc.vector.scalar_tensor_tensor(
-            out=magnitude[:], in0=tanh_first[:], scalar=-1.0, in1=tanh_first[:], op0=ALU.mult, op1=ALU.max
-        )
-        linear_part(6, 8)
+        tanh = keep.tile([P, HALF + V], F32, name="tanh", align_bytes=64)
+        prob_1 = keep.tile([P, V], F32, name="prob_1", align_bytes=64)
+        prob_3 = keep.tile([P, V + 1], F32, name="prob_3", align_bytes=64)
+        floor = prob_3[:, V : V + 1]
+        signed_1 = placed([P, V], F32, "signed_1", AT_SIGNED)
+        signed_early = keep.tile([P, HALF], F32, name="signed_early", align_bytes=64)
+        nc.scalar.activation(out=tanh[:, 0:HALF], in_=y_ps[0, HALF][:, high], func=ACT.Tanh, scale=SCALE / 2, bias=BIAS / 2)
+        signed_logits(signed_early[:], 0, low)
+        prob_0 = keep.tile([P, HALF], F32, name="prob_0", align_bytes=64)
+        nc.scalar.activation(out=prob_0[:], in_=signed_early[:], func=ACT.Sigmoid, scale=SCALE)
+        signed_logits(signed_1[:], 1, whole)
+        nc.scalar.activation(out=tanh[:, HALF:], in_=y_ps[2, 0][:], func=ACT.Tanh, scale=SCALE / 2, bias=BIAS / 2)
+        nc.scalar.activation(out=prob_1[:], in_=signed_1[:], func=ACT.Sigmoid, scale=SCALE)
+        signed_logits(last_signed[:, low], 3, low)
+        nc.scalar.activation(out=prob_3[:, low], in_=last_signed[:, low], func=ACT.Sigmoid, scale=SCALE)
+        signed_logits(last_signed[:, high], 3, high)
+        nc.scalar.activation(out=prob_3[:, HALF:], in_=last_signed[:, HALF:], func=ACT.Sigmoid, scale=SCALE)
+        linear = placed([P, BLOCKS, V], F32, "linear", AT_W_BF + 3 * KIB // 2)
+        signed_even = placed([P, 2, V], F32, "signed_even", AT_W_BF - 7 * KIB // 2)
+        magnitude = placed([P, HALF + V], F32, "magnitude", AT_SIGNED)
 
-        log_prob = keep.tile([P, 8, HALF], F32, name="log_prob", align_bytes=64)
-        res = keep.tile([P, 8, HALF], F32, name="res", align_bytes=64)
-        for n, (b, half) in enumerate(order):
-            if n < 6:
-                nc.scalar.activation(out=log_prob[:, n, :], in_=prob[:, n, :], func=ACT.Ln, bias=floor)
-            else:
-                nc.scalar.activation(out=log_prob[:, n, :], in_=magnitude[:, n - 6, :], func=ACT.Ln, scale=0.5, bias=one_half[:])
+        def linear_part(dst, src):
+            nc.vector.tensor_scalar(out=dst, in0=src, scalar1=-SCALE, scalar2=0.0, op0=ALU.mult, op1=ALU.max)
+
+        linear_part(linear[:, 1, :], signed_1[:])
+        linear_part(linear[:, 3, :], last_signed[:, whole])
+        linear_part(linear[:, 0, low], signed_early[:])
+        signed_logits(signed_even[:, 0, high], 0, high)
+        signed_logits(signed_even[:, 1, :], 2, whole)
+        nc.vector.scalar_tensor_tensor(
+            out=magnitude[:], in0=tanh[:], scalar=-1.0, in1=tanh[:], op0=ALU.mult, op1=ALU.max
+        )
+        linear_part(linear[:, 0, high], signed_even[:, 0, high])
+        linear_part(linear[:, 2, :], signed_even[:, 1, :])
+
+        log_prob = keep.tile([P, BLOCKS, V], F32, name="log_prob", align_bytes=64)
+        res = keep.tile([P, BLOCKS, V], F32, name="res", align_bytes=64)
+        by_sign = [(0, low, prob_0[:]), (1, low, prob_1[:, low]), (1, high, prob_1[:, high])]
+        by_sign += [(3, low, prob_3[:, low]), (3, high, prob_3[:, high])]
+        by_magnitude = [(0, high), (2, low), (2, high)]
+        for b, cols, prob in by_sign:
+            nc.scalar.activation(out=log_prob[:, b, cols], in_=prob, func=ACT.Ln, bias=floor)
             nc.vector.scalar_tensor_tensor(
-                out=res[:, n, :],
-                in0=log_prob[:, n, :],
+                out=res[:, b, cols],
+                in0=log_prob[:, b, cols],
                 scalar=-1.0,
-                in1=linear[:, n, :],
+                in1=linear[:, b, cols],
                 op0=ALU.mult,
-                op1=ALU.max if n < 6 else ALU.add,
+                op1=ALU.max,
             )
-            nc.sync.dma_start(out=out[b * P : (b + 1) * P, half * HALF : (half + 1) * HALF], in_=res[:, n, :])
+            nc.sync.dma_start(out=out[b * P : (b + 1) * P, cols], in_=res[:, b, cols])
+        for n, (b, cols) in enumerate(by_magnitude):
+            nc.scalar.activation(
+                out=log_prob[:, b, cols],
+                in_=magnitude[:, n * HALF : (n + 1) * HALF],
+                func=ACT.Ln,
+                scale=0.5,
+                bias=one_half[:],
+            )
+            nc.vector.tensor_tensor(
+                out=res[:, b, cols], in0=linear[:, b, cols], in1=log_prob[:, b, cols], op=ALU.subtract
+            )
+            nc.sync.dma_start(out=out[b * P : (b + 1) * P, cols], in_=res[:, b, cols])

@@ -30,7 +30,8 @@ FLOOR_AT = -28.0
 X_ROWS = 112
 E_ROWS = 48
 E_ROW = 4
-W_HEAD = 256
+E_COL = S - P
+W_HEAD = 384
 E_HEAD = 256
 
 KIB = 1024
@@ -76,9 +77,9 @@ def tile_picked_ysiglip_loss_p_kernel(
         xw_all = placed([P, T], I32, "xw_all", AT_XW_ALL)
 
         w_rows = w1.rearrange("(p j) c -> p (j c)", j=PACK)
+        nc.sync.dma_start(out=w_raw[:, 0:W_HEAD], in_=w_rows[:, 0:W_HEAD])
         nc.sync.dma_start(out=xs_all[X_ROWS : X_ROWS + SCALE_ROWS, :].bitcast(I32), in_=x_scales[0].bitcast(I32))
         nc.sync.dma_start(offs_sb[:], offs)
-        nc.sync.dma_start(out=w_raw[:, 0:W_HEAD], in_=w_rows[:, 0:W_HEAD])
         nc.sync.dma_start(out=es_all[E_ROWS : E_ROWS + SCALE_ROWS, :].bitcast(I32), in_=e_scales[0].bitcast(I32))
         nc.sync.dma_start(txt_sb[:], txt)
         nc.sync.dma_start(out=w_raw[:, W_HEAD:], in_=w_rows[:, W_HEAD:])
@@ -93,10 +94,9 @@ def tile_picked_ysiglip_loss_p_kernel(
         nc.vector.memset(xs_all[0:X_ROWS, :].bitcast(I32), 0)
         nc.vector.memset(es_all[0:E_ROWS, :].bitcast(I32), 0)
         nc.vector.memset(es_all[E_ROWS + SCALE_ROWS : P, :].bitcast(I32), 0)
-        xs = keep.tile([P, S], U8, name="xs", align_bytes=64)
-        nc.vector.memset(xs[:].bitcast(I32), 0)
-        es = keep.tile([P, V], U8, name="es", align_bytes=64)
-        nc.vector.memset(es[:].bitcast(I32), 0)
+        planes = keep.tile([P, E_COL + V], U8, name="planes", align_bytes=64)
+        nc.vector.memset(planes[:].bitcast(I32), 0)
+        xs, es = planes[:, 0:S], planes[:, E_COL : E_COL + V]
 
         xs_picked = keep.tile([P, S], U8, name="xs_picked", align_bytes=64)
         nc.vector.tensor_copy(xs_picked[:], xs_all[:].indirect(offs_sb[:]))
@@ -127,15 +127,15 @@ def tile_picked_ysiglip_loss_p_kernel(
             nc.tensor.matmul_mx(
                 out=warm[:],
                 lhsT=w_codes[:, 0:P].bitcast(FP8X4),
-                lhsT_scale=w_scales[:, 0:P],
+                lhsT_scale=moved_scales,
                 rhs=w_codes[:].bitcast(FP8X4),
-                rhs_scale=moved_scales,
+                rhs_scale=w_scales[:],
                 start=True,
                 stop=True,
             )
 
-        warm_up(w_scales[:])
-        warm_up(xs[:])
+        warm_up(w_scales[:, 0:P])
+        warm_up(xs[:, 0:P])
 
         lab_at = {0: AT_W_RAW, 1: AT_W_RAW + 2 * KIB, 3: AT_W_BF, 2: AT_XW_ALL}
         lab_sb = {b: placed([P, V], F32, "lab%d" % b, at) for b, at in lab_at.items()}
@@ -194,11 +194,12 @@ def tile_picked_ysiglip_loss_p_kernel(
                 stop=True,
             )
             y_ps[b, cols.start] = acc
-            y_ps.setdefault((b, HALF), acc)
+            if cols == whole:
+                y_ps[b, HALF] = acc
 
         quantise_h(0)
-        product(0, high, "h_ps0")
         product(0, low, "y_ps0")
+        product(0, high, "h_ps0")
         for b in range(1, BLOCKS):
             quantise_h(b)
             product(b, whole, "y_ps%d" % b)

@@ -20,7 +20,6 @@ PACK = 4
 BLOCKS = S // P
 HALF = V // 2
 SCALE_ROWS = 16
-LIST_HALF = HALF // 16
 
 SCALE = 1.5
 BIAS = -0.5
@@ -32,24 +31,24 @@ E_ROWS = 48
 E_ROW = 4
 E_COL = S - P
 W_HEAD = 384
-E_HEAD = 256
-
 KIB = 1024
+WARM1 = 256
+WARM2 = 128
+QUARTERED = (7,)
+QUARTER_STORES = ()
+
 AT_W_RAW = 0
 AT_ES_ALL = 8 * KIB
 AT_XW_ALL = 12 * KIB
 AT_EW_ALL = 20 * KIB
 AT_XS_ALL = 27 * KIB
-AT_H_BF = 32 * KIB
-AT_SIGNED = 36 * KIB
-AT_W_BF = 56 * KIB
-AT_W_CODES = 70 * KIB
 AT_ES_PICKED = 35 * KIB
+AT_W_BF = 56 * KIB
 
 
-def move_scale_rows(nc, operand, picked, first, row0):
+def move_scale_rows(queue, operand, picked, first, row0):
     for r in range(4):
-        nc.sync.dma_start(
+        queue.dma_start(
             out=operand[row0 + r : P : 32, :].bitcast(I32),
             in_=picked[first + r : first + SCALE_ROWS : 4, :].bitcast(I32),
         )
@@ -67,9 +66,11 @@ def tile_picked_ysiglip_loss_p_kernel(
         def placed(shape, dtype, name, offset):
             return reuse.tile(shape, dtype, name=name, align_bytes=64, offset=offset)
 
+        def own(shape, dtype, name):
+            return keep.tile(shape, dtype, name=name, align_bytes=64)
+
         offs_sb = keep.tile([P, S // 16], U16, name="offs_sb")
         txt_sb = keep.tile([P, V // 16], U16, name="txt_sb")
-        one_half = keep.tile([P, 1], F32, name="one_half")
 
         w_raw = placed([P, PACK * H], F32, "w_raw", AT_W_RAW)
         xs_all = placed([P, T], U8, "xs_all", AT_XS_ALL)
@@ -83,27 +84,33 @@ def tile_picked_ysiglip_loss_p_kernel(
         nc.sync.dma_start(out=es_all[E_ROWS : E_ROWS + SCALE_ROWS, :].bitcast(I32), in_=e_scales[0].bitcast(I32))
         nc.sync.dma_start(txt_sb[:], txt)
         nc.sync.dma_start(out=w_raw[:, W_HEAD:], in_=w_rows[:, W_HEAD:])
-        nc.sync.dma_start(out=xw_all[:], in_=x_words[0].rearrange("p c r -> p (c r)").bitcast(I32))
+        x_rows = x_words[0].rearrange("p c r -> p (c r)").bitcast(I32)
+        for cols in (slice(0, T // 2), slice(T // 2, T)):
+            nc.sync.dma_start(out=xw_all[:, cols], in_=x_rows[:, cols])
 
-        one_col = keep.tile([P, 1], F32, name="one_col")
-        nc.vector.memset(one_col[:], 0.0)
-        nc.scalar.activation(out=one_half[:], in_=one_col[:], func=ACT.Sigmoid)
-        last_signed = keep.tile([P, V + 1], F32, name="last_signed", align_bytes=64)
-        nc.vector.memset(last_signed[:, V : V + 1], FLOOR_AT)
+        zero_col = own([P, 1], F32, "zero_col")
+        half_scale = own([P, 1], F32, "half_scale")
+        nc.vector.memset(zero_col[:], 0.0)
+        nc.scalar.activation(out=half_scale[:], in_=zero_col[:], func=ACT.Sigmoid)
+        n_sign = 6
+        signed = own([P, n_sign * HALF + 2], F32, "signed")
+        nc.vector.memset(signed[:, n_sign * HALF : n_sign * HALF + 1], FLOOR_AT)
+        nc.vector.memset(signed[:, n_sign * HALF + 1 :], 0.0)
 
         nc.vector.memset(xs_all[0:X_ROWS, :].bitcast(I32), 0)
         nc.vector.memset(es_all[0:E_ROWS, :].bitcast(I32), 0)
         nc.vector.memset(es_all[E_ROWS + SCALE_ROWS : P, :].bitcast(I32), 0)
-        planes = keep.tile([P, E_COL + V], U8, name="planes", align_bytes=64)
+        planes = own([P, E_COL + V], U8, "planes")
         nc.vector.memset(planes[:].bitcast(I32), 0)
         xs, es = planes[:, 0:S], planes[:, E_COL : E_COL + V]
 
-        xs_picked = keep.tile([P, S], U8, name="xs_picked", align_bytes=64)
+        xs_picked = own([P, S], U8, "xs_picked")
         nc.vector.tensor_copy(xs_picked[:], xs_all[:].indirect(offs_sb[:]))
         ew_all = placed([P, W], I32, "ew_all", AT_EW_ALL)
+        move_scale_rows(nc.sync, xs, xs_picked, X_ROWS, 0)
         e_rows = e_words[0].rearrange("p c r -> p (c r)").bitcast(I32)
-        move_scale_rows(nc, xs, xs_picked, X_ROWS, 0)
-        nc.sync.dma_start(out=ew_all[:], in_=e_rows)
+        for cols in (slice(0, W // 2), slice(W // 2, W)):
+            nc.sync.dma_start(out=ew_all[:, cols], in_=e_rows[:, cols])
 
         w_src = w_raw[:].rearrange("p (j m t) -> p m j t", j=PACK, t=PACK)
         w_bf = [placed([P, 2 * P * PACK], BF16, "w_bf%d" % half, AT_W_BF + 2 * half * KIB) for half in range(2)]
@@ -113,162 +120,189 @@ def tile_picked_ysiglip_loss_p_kernel(
 
         es_picked = placed([P, V], U8, "es_picked", AT_ES_PICKED)
         nc.vector.tensor_copy(es_picked[:], es_all[:].indirect(txt_sb[:]))
-        move_scale_rows(nc, es, es_picked, E_ROWS, E_ROW)
+        move_scale_rows(nc.sync, es, es_picked, E_ROWS, E_ROW)
 
-        w_codes = placed([P, H], U32, "w_codes", AT_W_CODES)
-        w_scales = keep.tile([P, H], U8, name="w_scales", align_bytes=64)
+        w_codes = own([P, H], U32, "w_codes")
+        w_scales = own([P, H], U8, "w_scales")
         for half in range(2):
             cols = slice(half * 2 * P, (half + 1) * 2 * P)
             nc.vector.quantize_mx(out=w_codes[:, cols].bitcast(FP8X4), scales=w_scales[:, cols], in_=w_bf[half][:])
 
-        warm = psum.tile([P, H], F32, name="warm", tag="y_ps3")
+        warm = psum.tile([P, H], F32, name="warm", tag="bank7")
 
-        def warm_up(moved_scales):
+        def warm_up(moved_scales, n):
             nc.tensor.matmul_mx(
-                out=warm[:],
+                out=warm[:, 0:n],
                 lhsT=w_codes[:, 0:P].bitcast(FP8X4),
                 lhsT_scale=moved_scales,
-                rhs=w_codes[:].bitcast(FP8X4),
-                rhs_scale=w_scales[:],
+                rhs=w_codes[:, 0:n].bitcast(FP8X4),
+                rhs_scale=w_scales[:, 0:n],
                 start=True,
                 stop=True,
             )
 
-        warm_up(w_scales[:, 0:P])
-        warm_up(xs[:, 0:P])
+        warm_up(w_scales[:, 0:P], WARM1)
+        warm_up(xs[:, 0:P], WARM2)
 
-        lab_at = {0: AT_W_RAW, 1: AT_W_RAW + 2 * KIB, 3: AT_W_BF, 2: AT_XW_ALL}
-        lab_sb = {b: placed([P, V], F32, "lab%d" % b, at) for b, at in lab_at.items()}
+        lab01 = placed([P, 2, V], F32, "lab01", AT_W_RAW)
+        lab2 = placed([P, V], F32, "lab2", AT_W_RAW + 7 * KIB)
+        lab3 = placed([P, V], F32, "lab3", AT_W_RAW + 4 * KIB)
+        lab_rows = lab.rearrange("(b p) v -> p b v", p=P)
 
-        xw = [keep.tile([P, HALF], U32, name="xw%d" % half, align_bytes=64) for half in range(2)]
-        for half in range(2):
-            nc.vector.tensor_copy(
-                xw[half][:],
-                xw_all[:].bitcast(U32).indirect(offs_sb[:, half * LIST_HALF : (half + 1) * LIST_HALF]),
-            )
-        for b in lab_at:
-            nc.sync.dma_start(out=lab_sb[b][:], in_=lab[b * P : (b + 1) * P, :])
+        pieces = [(0, 1), (1, 2), (2, 4)]
+        xw = {}
+        for lo, hi in pieces:
+            piece = own([P, (hi - lo) * P], U32, "xw%d" % lo)
+            nc.vector.tensor_copy(piece[:], xw_all[:].bitcast(U32).indirect(offs_sb[:, lo * 8 : hi * 8]))
+            for b in range(lo, hi):
+                xw[b] = piece[:, (b - lo) * P : (b - lo + 1) * P]
+        nc.sync.dma_start(out=lab01[:, 0, 0:HALF], in_=lab_rows[:, 0, 0:HALF])
+        nc.sync.dma_start(out=lab01[:, 1, HALF:], in_=lab_rows[:, 1, HALF:])
+        nc.sync.dma_start(out=lab2[:], in_=lab_rows[:, 2, :])
+        nc.sync.dma_start(out=lab3[:], in_=lab_rows[:, 3, :])
+        nc.sync.dma_start(out=lab01[:, 1, 0:HALF], in_=lab_rows[:, 1, 0:HALF])
+        nc.sync.dma_start(out=lab01[:, 0, HALF:], in_=lab_rows[:, 0, HALF:])
 
-        h_late = keep.tile([P, 2, P, PACK], BF16, name="h_late", align_bytes=64)
-        h_bf = [placed([P, P, PACK], BF16, "h_bf%d" % b, AT_H_BF + b * KIB)[:] for b in range(2)]
-        h_bf += [h_late[:, 0], h_late[:, 1]]
+        h_bf = [own([P, P, PACK], BF16, "h_bf%d" % b) for b in range(BLOCKS)]
         for b in range(BLOCKS):
             images = slice(b * P, (b + 1) * P)
-            h_ps = psum.tile([P, PACK, P], F32, name="h_ps%d" % b, tag="h_ps%d" % b)
+            h_ps = psum.tile([P, PACK, P], F32, name="h_ps%d" % b, tag="bank%d" % b)
             for t in range(PACK):
                 cols = slice(t * P, (t + 1) * P)
                 nc.tensor.matmul_mx(
                     out=h_ps[:, t, :],
                     lhsT=w_codes[:, cols].bitcast(FP8X4),
                     lhsT_scale=w_scales[:, cols],
-                    rhs=xw[b // 2][:, (b % 2) * P : (b % 2 + 1) * P].bitcast(FP8X4),
+                    rhs=xw[b].bitcast(FP8X4),
                     rhs_scale=xs[:, images],
                     start=True,
                     stop=True,
                 )
-            nc.scalar.copy(out=h_bf[b], in_=h_ps[:].rearrange("p t n -> p n t"))
-        h_codes = keep.tile([P, S], U32, name="h_codes", align_bytes=64)
-        h_scales = [placed([P, P], U8, "h_scales%d" % b, AT_ES_PICKED + b * P) for b in range(BLOCKS)]
+            nc.scalar.copy(out=h_bf[b][:], in_=h_ps[:].rearrange("p t n -> p n t"))
 
-        def quantise_h(b):
+        h_codes = [own([P, P], U32, "h_codes%d" % b) for b in range(BLOCKS)]
+        h_scales = {}
+
+        def quantise_h(b, held):
+            if held:
+                h_scales[b] = placed([P, P], U8, "h_scales%d" % b, AT_ES_PICKED + b * P)
+            else:
+                h_scales[b] = own([P, P], U8, "h_scales%d" % b)
             nc.vector.quantize_mx(
-                out=h_codes[:, b * P : (b + 1) * P].bitcast(FP8X4),
+                out=h_codes[b][:].bitcast(FP8X4),
                 scales=h_scales[b][:],
-                in_=h_bf[b].rearrange("p n t -> p (n t)"),
+                in_=h_bf[b][:].rearrange("p n t -> p (n t)"),
             )
 
-        ew = keep.tile([P, V], U32, name="ew", align_bytes=64)
-        nc.vector.tensor_copy(ew[:], ew_all[:].bitcast(U32).indirect(txt_sb[:]))
-        whole, low, high = slice(0, V), slice(0, HALF), slice(HALF, V)
-        y_ps = {}
+        ew = [own([P, HALF], U32, "ew0"), placed([P, HALF], U32, "ew1", AT_ES_PICKED + P - KIB)]
 
-        def product(b, cols, bank):
-            acc = psum.tile([P, V], F32, name="y_ps%d_%d" % (b, cols.start), tag=bank)
+        def gather_e(half):
+            nc.vector.tensor_copy(ew[half][:], ew_all[:].bitcast(U32).indirect(txt_sb[:, half * 16 : (half + 1) * 16]))
+
+        def product(acc, b, half):
             nc.tensor.matmul_mx(
-                out=acc[:, cols],
-                lhsT=h_codes[:, b * P : (b + 1) * P].bitcast(FP8X4),
+                out=acc,
+                lhsT=h_codes[b][:].bitcast(FP8X4),
                 lhsT_scale=h_scales[b][:],
-                rhs=ew[:, cols].bitcast(FP8X4),
-                rhs_scale=es[E_ROW:P, cols],
+                rhs=ew[half][:].bitcast(FP8X4),
+                rhs_scale=es[E_ROW:P, half * HALF : (half + 1) * HALF],
                 start=True,
                 stop=True,
             )
-            y_ps[b, cols.start] = acc
-            if cols == whole:
-                y_ps[b, HALF] = acc
 
-        quantise_h(0)
-        product(0, low, "y_ps0")
-        product(0, high, "h_ps0")
-        for b in range(1, BLOCKS):
-            quantise_h(b)
-            product(b, whole, "y_ps%d" % b)
+        def bank(name, tag):
+            return psum.tile([P, 2, HALF], F32, name=name, tag=tag)
 
-        def signed_logits(dst, b, cols):
-            nc.vector.scalar_tensor_tensor(
-                out=dst, in0=y_ps[b, cols.start][:, cols], scalar=SHIFT, in1=lab_sb[b][:, cols], op0=ALU.subtract, op1=ALU.mult
-            )
+        def logits(dst, acc, labels):
+            nc.vector.scalar_tensor_tensor(out=dst, in0=acc, scalar=SHIFT, in1=labels, op0=ALU.subtract, op1=ALU.mult)
 
-        tanh = keep.tile([P, HALF + V], F32, name="tanh", align_bytes=64)
-        prob_1 = keep.tile([P, V], F32, name="prob_1", align_bytes=64)
-        prob_3 = keep.tile([P, V + 1], F32, name="prob_3", align_bytes=64)
-        floor = prob_3[:, V : V + 1]
-        signed_1 = placed([P, V], F32, "signed_1", AT_SIGNED)
-        signed_early = keep.tile([P, HALF], F32, name="signed_early", align_bytes=64)
-        nc.scalar.activation(out=tanh[:, 0:HALF], in_=y_ps[0, HALF][:, high], func=ACT.Tanh, scale=SCALE / 2, bias=BIAS / 2)
-        signed_logits(signed_early[:], 0, low)
-        prob_0 = keep.tile([P, HALF], F32, name="prob_0", align_bytes=64)
-        nc.scalar.activation(out=prob_0[:], in_=signed_early[:], func=ACT.Sigmoid, scale=SCALE)
-        signed_logits(signed_1[:], 1, whole)
-        nc.scalar.activation(out=tanh[:, HALF:], in_=y_ps[2, 0][:], func=ACT.Tanh, scale=SCALE / 2, bias=BIAS / 2)
-        nc.scalar.activation(out=prob_1[:], in_=signed_1[:], func=ACT.Sigmoid, scale=SCALE)
-        signed_logits(last_signed[:, low], 3, low)
-        nc.scalar.activation(out=prob_3[:, low], in_=last_signed[:, low], func=ACT.Sigmoid, scale=SCALE)
-        signed_logits(last_signed[:, high], 3, high)
-        nc.scalar.activation(out=prob_3[:, HALF:], in_=last_signed[:, HALF:], func=ACT.Sigmoid, scale=SCALE)
-        linear = placed([P, BLOCKS, V], F32, "linear", AT_W_BF + 3 * KIB // 2)
-        signed_even = placed([P, 2, V], F32, "signed_even", AT_W_BF - 7 * KIB // 2)
-        magnitude = placed([P, HALF + V], F32, "magnitude", AT_SIGNED)
+        tanh = own([P, 2 * HALF], F32, "tanh")
+        prob = own([P, n_sign * HALF + 2], F32, "prob")
+        floor = prob[:, n_sign * HALF : n_sign * HALF + 1]
+        one_half = prob[:, n_sign * HALF + 1 :]
+
+        def span(lo, hi):
+            return slice(lo * HALF, hi * HALF)
+
+        def half_tanh(n, acc):
+            nc.scalar.activation(out=tanh[:, span(n, n + 1)], in_=acc, func=ACT.Tanh, scale=SCALE / 2, bias=BIAS / 2)
+
+        def sig(lo, hi, extra=0):
+            cols = slice(lo * HALF, hi * HALF + extra)
+            nc.scalar.activation(out=prob[:, cols], in_=signed[:, cols], func=ACT.Sigmoid, scale=SCALE)
+
+        quantise_h(0, False)
+        gather_e(0)
+        y0a, y1a, y0b, y1b = bank("y0a", "bank4"), bank("y1a", "bank5"), bank("y0b", "bank6"), bank("y1b", "bank7")
+        product(y0a[:, 0, :], 0, 0)
+        quantise_h(1, True)
+        product(y1a[:, 0, :], 1, 0)
+        gather_e(1)
+        product(y0b[:, 0, :], 0, 1)
+        product(y1b[:, 0, :], 1, 1)
+        quantise_h(2, True)
+        y2 = bank("y2", "bank0")
+        product(y2[:, 0, :], 2, 0)
+        product(y2[:, 1, :], 2, 1)
+        logits(signed[:, span(0, 1)], y0a[:, 0, :], lab01[:, 0, 0:HALF])
+        quantise_h(3, True)
+        y3 = bank("y3", "bank1")
+        product(y3[:, 0, :], 3, 0)
+        product(y3[:, 1, :], 3, 1)
+
+        half_tanh(0, y1a[:, 0, :])
+        sig(0, 1)
+        half_tanh(1, y0b[:, 0, :])
+        logits(signed[:, span(1, 2)], y1b[:, 0, :], lab01[:, 1, HALF:])
+        sig(1, 2)
+        logits(signed[:, span(2, 3)], y2[:, 0, :], lab2[:, 0:HALF])
+        sig(2, 3)
+        logits(signed[:, span(3, 4)], y2[:, 1, :], lab2[:, HALF:])
+        sig(3, 4)
+        logits(signed[:, span(4, 5)], y3[:, 0, :], lab3[:, 0:HALF])
+        sig(4, 5)
+        logits(signed[:, span(5, 6)], y3[:, 1, :], lab3[:, HALF:])
+        sig(5, 6, 2)
+        linear = own([P, 8 * HALF], F32, "linear")
+        late = placed([P, 2 * HALF], F32, "late", AT_W_RAW + 8 * KIB)
+        magnitude = placed([P, 2 * HALF], F32, "magnitude", AT_W_RAW + 6 * KIB)
 
         def linear_part(dst, src):
             nc.vector.tensor_scalar(out=dst, in0=src, scalar1=-SCALE, scalar2=0.0, op0=ALU.mult, op1=ALU.max)
 
-        linear_part(linear[:, 1, :], signed_1[:])
-        linear_part(linear[:, 3, :], last_signed[:, whole])
-        linear_part(linear[:, 0, low], signed_early[:])
-        signed_logits(signed_even[:, 0, high], 0, high)
-        signed_logits(signed_even[:, 1, :], 2, whole)
+        linear_part(linear[:, span(0, 6)], signed[:, span(0, 6)])
+        logits(late[:, span(0, 1)], y1a[:, 0, :], lab01[:, 1, 0:HALF])
+        logits(late[:, span(1, 2)], y0b[:, 0, :], lab01[:, 0, HALF:])
         nc.vector.scalar_tensor_tensor(
             out=magnitude[:], in0=tanh[:], scalar=-1.0, in1=tanh[:], op0=ALU.mult, op1=ALU.max
         )
-        linear_part(linear[:, 0, high], signed_even[:, 0, high])
-        linear_part(linear[:, 2, :], signed_even[:, 1, :])
+        linear_part(linear[:, span(6, 8)], late[:])
 
-        log_prob = keep.tile([P, BLOCKS, V], F32, name="log_prob", align_bytes=64)
-        res = keep.tile([P, BLOCKS, V], F32, name="res", align_bytes=64)
-        by_sign = [(0, low, prob_0[:]), (1, low, prob_1[:, low]), (1, high, prob_1[:, high])]
-        by_sign += [(3, low, prob_3[:, low]), (3, high, prob_3[:, high])]
-        by_magnitude = [(0, high), (2, low), (2, high)]
-        for b, cols, prob in by_sign:
-            nc.scalar.activation(out=log_prob[:, b, cols], in_=prob, func=ACT.Ln, bias=floor)
-            nc.vector.scalar_tensor_tensor(
-                out=res[:, b, cols],
-                in0=log_prob[:, b, cols],
-                scalar=-1.0,
-                in1=linear[:, b, cols],
-                op0=ALU.mult,
-                op1=ALU.max,
-            )
-            nc.sync.dma_start(out=out[b * P : (b + 1) * P, cols], in_=res[:, b, cols])
-        for n, (b, cols) in enumerate(by_magnitude):
-            nc.scalar.activation(
-                out=log_prob[:, b, cols],
-                in_=magnitude[:, n * HALF : (n + 1) * HALF],
-                func=ACT.Ln,
-                scale=0.5,
-                bias=one_half[:],
-            )
-            nc.vector.tensor_tensor(
-                out=res[:, b, cols], in0=linear[:, b, cols], in1=log_prob[:, b, cols], op=ALU.subtract
-            )
-            nc.sync.dma_start(out=out[b * P : (b + 1) * P, cols], in_=res[:, b, cols])
+        log_prob = own([P, 8 * HALF], F32, "log_prob")
+        res = own([P, 8 * HALF], F32, "res")
+        where = [(0, 0), (1, 1), (2, 0), (2, 1), (3, 0), (3, 1), (1, 0), (0, 1)]
+        quarter = HALF // 2
+        for n, (b, half) in enumerate(where):
+            cuts = [(0, quarter), (quarter, HALF)] if n in QUARTERED else [(0, HALF)]
+            for lo, hi in cuts:
+                cols = slice(n * HALF + lo, n * HALF + hi)
+                if n < n_sign:
+                    nc.scalar.activation(out=log_prob[:, cols], in_=prob[:, cols], func=ACT.Ln, bias=floor)
+                    nc.vector.scalar_tensor_tensor(
+                        out=res[:, cols], in0=log_prob[:, cols], scalar=-1.0, in1=linear[:, cols], op0=ALU.mult, op1=ALU.max
+                    )
+                else:
+                    nc.scalar.activation(
+                        out=log_prob[:, cols],
+                        in_=magnitude[:, (n - n_sign) * HALF + lo : (n - n_sign) * HALF + hi],
+                        func=ACT.Ln,
+                        scale=half_scale[:],
+                        bias=one_half,
+                    )
+                    nc.vector.tensor_tensor(out=res[:, cols], in0=linear[:, cols], in1=log_prob[:, cols], op=ALU.subtract)
+                if n in QUARTER_STORES or hi == HALF:
+                    first = lo if n in QUARTER_STORES else 0
+                    nc.sync.dma_start(
+                        out=out[b * P : (b + 1) * P, half * HALF + first : half * HALF + hi],
+                        in_=res[:, n * HALF + first : n * HALF + hi],
+                    )

@@ -80,8 +80,8 @@ def tile_picked_ysiglip_loss_p_kernel(
         w_rows = w1.rearrange("(p j) c -> p (j c)", j=PACK)
         nc.sync.dma_start(out=w_raw[:, 0:W_HEAD], in_=w_rows[:, 0:W_HEAD])
         nc.sync.dma_start(out=xs_all[X_ROWS : X_ROWS + SCALE_ROWS, :].bitcast(I32), in_=x_scales[0].bitcast(I32))
-        nc.sync.dma_start(offs_sb[:], offs)
         nc.sync.dma_start(out=es_all[E_ROWS : E_ROWS + SCALE_ROWS, :].bitcast(I32), in_=e_scales[0].bitcast(I32))
+        nc.sync.dma_start(offs_sb[:], offs)
         nc.sync.dma_start(txt_sb[:], txt)
         nc.sync.dma_start(out=w_raw[:, W_HEAD:], in_=w_rows[:, W_HEAD:])
         x_rows = x_words[0].rearrange("p c r -> p (c r)").bitcast(I32)
@@ -251,8 +251,8 @@ def tile_picked_ysiglip_loss_p_kernel(
         product(y3[:, 1, :], 3, 1)
 
         half_tanh(0, y1a[:, 0, :])
-        sig(0, 1)
         half_tanh(1, y0b[:, 0, :])
+        sig(0, 1)
         logits(signed[:, span(1, 2)], y1b[:, 0, :], lab01[:, 1, HALF:])
         sig(1, 2)
         logits(signed[:, span(2, 3)], y2[:, 0, :], lab2[:, 0:HALF])

@@ -32,8 +32,6 @@ E_ROW = 4
 E_COL = S - P
 W_HEAD = 384
 KIB = 1024
-WARM1 = 256
-WARM2 = 128
 QUARTERED = (7,)
 QUARTER_STORES = ()
 
@@ -127,22 +125,6 @@ def tile_picked_ysiglip_loss_p_kernel(
         for half in range(2):
             cols = slice(half * 2 * P, (half + 1) * 2 * P)
             nc.vector.quantize_mx(out=w_codes[:, cols].bitcast(FP8X4), scales=w_scales[:, cols], in_=w_bf[half][:])
-
-        warm = psum.tile([P, H], F32, name="warm", tag="bank7")
-
-        def warm_up(moved_scales, n):
-            nc.tensor.matmul_mx(
-                out=warm[:, 0:n],
-                lhsT=w_codes[:, 0:P].bitcast(FP8X4),
-                lhsT_scale=moved_scales,
-                rhs=w_codes[:, 0:n].bitcast(FP8X4),
-                rhs_scale=w_scales[:, 0:n],
-                start=True,
-                stop=True,
-            )
-
-        warm_up(w_scales[:, 0:P], WARM1)
-        warm_up(xs[:, 0:P], WARM2)
 
         lab01 = placed([P, 2, V], F32, "lab01", AT_W_RAW)
         lab2 = placed([P, V], F32, "lab2", AT_W_RAW + 7 * KIB)

@@ -90,7 +90,7 @@ def tile_picked_ysiglip_loss_p_kernel(
         half_scale = own([P, 1], F32, "half_scale")
         nc.vector.memset(zero_col[:], 0.0)
         nc.scalar.activation(out=half_scale[:], in_=zero_col[:], func=ACT.Sigmoid)
-        n_sign = 6
+        n_sign = 5
         signed = own([P, n_sign * HALF + 2], F32, "signed")
         nc.vector.memset(signed[:, n_sign * HALF : n_sign * HALF + 1], FLOOR_AT)
         nc.vector.memset(signed[:, n_sign * HALF + 1 :], 0.0)
@@ -127,7 +127,8 @@ def tile_picked_ysiglip_loss_p_kernel(
             nc.vector.quantize_mx(out=w_codes[:, cols].bitcast(FP8X4), scales=w_scales[:, cols], in_=w_bf[half][:])
 
         lab01 = placed([P, 2, V], F32, "lab01", AT_W_RAW)
-        lab2 = placed([P, V], F32, "lab2", AT_W_RAW + 7 * KIB)
+        lab2b = placed([P, HALF], F32, "lab2b", AT_W_RAW + 7 * KIB + 512)
+        lab12a = placed([P, 2, HALF], F32, "lab12a", AT_W_BF)
         lab3 = placed([P, V], F32, "lab3", AT_W_RAW + 4 * KIB)
         lab_rows = lab.rearrange("(b p) v -> p b v", p=P)
 
@@ -140,9 +141,9 @@ def tile_picked_ysiglip_loss_p_kernel(
                 xw[b] = piece[:, (b - lo) * P : (b - lo + 1) * P]
         nc.sync.dma_start(out=lab01[:, 0, 0:HALF], in_=lab_rows[:, 0, 0:HALF])
         nc.sync.dma_start(out=lab01[:, 1, HALF:], in_=lab_rows[:, 1, HALF:])
-        nc.sync.dma_start(out=lab2[:], in_=lab_rows[:, 2, :])
+        nc.sync.dma_start(out=lab2b[:], in_=lab_rows[:, 2, HALF:])
         nc.sync.dma_start(out=lab3[:], in_=lab_rows[:, 3, :])
-        nc.sync.dma_start(out=lab01[:, 1, 0:HALF], in_=lab_rows[:, 1, 0:HALF])
+        nc.sync.dma_start(out=lab12a[:], in_=lab_rows[:, 1:3, 0:HALF])
         nc.sync.dma_start(out=lab01[:, 0, HALF:], in_=lab_rows[:, 0, HALF:])
 
         h_bf = [own([P, P, PACK], BF16, "h_bf%d" % b) for b in range(BLOCKS)]
@@ -198,7 +199,7 @@ def tile_picked_ysiglip_loss_p_kernel(
         def logits(dst, acc, labels):
             nc.vector.scalar_tensor_tensor(out=dst, in0=acc, scalar=SHIFT, in1=labels, op0=ALU.subtract, op1=ALU.mult)
 
-        tanh = own([P, 2 * HALF], F32, "tanh")
+        tanh = own([P, 3 * HALF], F32, "tanh")
         prob = own([P, n_sign * HALF + 2], F32, "prob")
         floor = prob[:, n_sign * HALF : n_sign * HALF + 1]
         one_half = prob[:, n_sign * HALF + 1 :]
@@ -208,6 +209,8 @@ def tile_picked_ysiglip_loss_p_kernel(
 
         def half_tanh(n, acc):
             nc.scalar.activation(out=tanh[:, span(n, n + 1)], in_=acc, func=ACT.Tanh, scale=SCALE / 2, bias=BIAS / 2)
+
+        linear = own([P, 8 * HALF], F32, "linear")
 
         def sig(lo, hi, extra=0):
             cols = slice(lo * HALF, hi * HALF + extra)
@@ -220,12 +223,12 @@ def tile_picked_ysiglip_loss_p_kernel(
         quantise_h(1, True)
         product(y1a[:, 0, :], 1, 0)
         gather_e(1)
-        product(y0b[:, 0, :], 0, 1)
         product(y1b[:, 0, :], 1, 1)
+        product(y0b[:, 0, :], 0, 1)
         quantise_h(2, True)
-        y2 = bank("y2", "bank0")
-        product(y2[:, 0, :], 2, 0)
-        product(y2[:, 1, :], 2, 1)
+        y2a, y2b = bank("y2a", "bank2"), bank("y2b", "bank0")
+        product(y2a[:, 0, :], 2, 0)
+        product(y2b[:, 0, :], 2, 1)
         logits(signed[:, span(0, 1)], y0a[:, 0, :], lab01[:, 0, 0:HALF])
         quantise_h(3, True)
         y3 = bank("y3", "bank1")
@@ -233,36 +236,35 @@ def tile_picked_ysiglip_loss_p_kernel(
         product(y3[:, 1, :], 3, 1)
 
         half_tanh(0, y1a[:, 0, :])
-        half_tanh(1, y0b[:, 0, :])
         sig(0, 1)
+        half_tanh(1, y0b[:, 0, :])
+        half_tanh(2, y2a[:, 0, :])
         logits(signed[:, span(1, 2)], y1b[:, 0, :], lab01[:, 1, HALF:])
         sig(1, 2)
-        logits(signed[:, span(2, 3)], y2[:, 0, :], lab2[:, 0:HALF])
+        logits(signed[:, span(2, 3)], y2b[:, 0, :], lab2b[:])
         sig(2, 3)
-        logits(signed[:, span(3, 4)], y2[:, 1, :], lab2[:, HALF:])
+        logits(signed[:, span(3, 4)], y3[:, 0, :], lab3[:, 0:HALF])
         sig(3, 4)
-        logits(signed[:, span(4, 5)], y3[:, 0, :], lab3[:, 0:HALF])
-        sig(4, 5)
-        logits(signed[:, span(5, 6)], y3[:, 1, :], lab3[:, HALF:])
-        sig(5, 6, 2)
-        linear = own([P, 8 * HALF], F32, "linear")
-        late = placed([P, 2 * HALF], F32, "late", AT_W_RAW + 8 * KIB)
-        magnitude = placed([P, 2 * HALF], F32, "magnitude", AT_W_RAW + 6 * KIB)
+        logits(signed[:, span(4, 5)], y3[:, 1, :], lab3[:, HALF:])
+        sig(4, 5, 2)
+        late = placed([P, 3 * HALF], F32, "late", AT_W_RAW + 7 * KIB + 512)
+        magnitude = placed([P, 3 * HALF], F32, "magnitude", AT_W_RAW + 4 * KIB + 512)
 
         def linear_part(dst, src):
             nc.vector.tensor_scalar(out=dst, in0=src, scalar1=-SCALE, scalar2=0.0, op0=ALU.mult, op1=ALU.max)
 
-        linear_part(linear[:, span(0, 6)], signed[:, span(0, 6)])
-        logits(late[:, span(0, 1)], y1a[:, 0, :], lab01[:, 1, 0:HALF])
+        logits(late[:, span(0, 1)], y1a[:, 0, :], lab12a[:, 0, :])
         logits(late[:, span(1, 2)], y0b[:, 0, :], lab01[:, 0, HALF:])
+        logits(late[:, span(2, 3)], y2a[:, 0, :], lab12a[:, 1, :])
+        linear_part(linear[:, span(0, 5)], signed[:, span(0, 5)])
         nc.vector.scalar_tensor_tensor(
             out=magnitude[:], in0=tanh[:], scalar=-1.0, in1=tanh[:], op0=ALU.mult, op1=ALU.max
         )
-        linear_part(linear[:, span(6, 8)], late[:])
+        linear_part(linear[:, span(5, 8)], late[:])
 
         log_prob = own([P, 8 * HALF], F32, "log_prob")
         res = own([P, 8 * HALF], F32, "res")
-        where = [(0, 0), (1, 1), (2, 0), (2, 1), (3, 0), (3, 1), (1, 0), (0, 1)]
+        where = [(0, 0), (1, 1), (2, 1), (3, 0), (3, 1), (1, 0), (0, 1), (2, 0)]
         quarter = HALF // 2
         for n, (b, half) in enumerate(where):
             cuts = [(0, quarter), (quarter, HALF)] if n in QUARTERED else [(0, HALF)]

@@ -19,6 +19,8 @@ P = 128
 PACK = 4
 BLOCKS = S // P
 HALF = V // 2
+QUARTER = HALF // 2
+GROUP = 16
 SCALE_ROWS = 16
 
 SCALE = 1.5
@@ -26,30 +28,53 @@ BIAS = -0.5
 SHIFT = 0.5 / 1.5
 FLOOR_AT = -28.0
 
+BY_SIGN = [(0, 0), (1, 1), (2, 1), (3, 0), (3, 1)]
+BY_MAGNITUDE = [(1, 0), (0, 1), (2, 0)]
+PIECES = BY_SIGN + BY_MAGNITUDE
+SIGNED = len(BY_SIGN) * HALF
+
 X_ROWS = 112
 E_ROWS = 48
 E_ROW = 4
 E_COL = S - P
 W_HEAD = 384
-KIB = 1024
-QUARTERED = (7,)
-QUARTER_STORES = ()
+X_GATHERS = [(0, 1), (1, 2), (2, 4)]
 
+KIB = 1024
+DMA_ALIGN = 512
 AT_W_RAW = 0
 AT_ES_ALL = 8 * KIB
 AT_XW_ALL = 12 * KIB
 AT_EW_ALL = 20 * KIB
 AT_XS_ALL = 27 * KIB
 AT_ES_PICKED = 35 * KIB
+AT_EW_SECOND = AT_ES_PICKED + V
 AT_W_BF = 56 * KIB
+AT_LAB_0 = AT_W_RAW
+AT_LAB_3 = AT_W_RAW + 4 * KIB
+AT_LAB_12_SECOND = AT_W_RAW + 13 * KIB // 2
+AT_LAB_12_FIRST = AT_W_BF
+AT_MAGNITUDE = AT_W_RAW + 3 * KIB
+AT_LATE = AT_W_RAW + 15 * KIB // 2
 
 
-def move_scale_rows(queue, operand, picked, first, row0):
+def move_scale_rows(nc, operand, picked, first, row0):
     for r in range(4):
-        queue.dma_start(
+        nc.sync.dma_start(
             out=operand[row0 + r : P : 32, :].bitcast(I32),
             in_=picked[first + r : first + SCALE_ROWS : 4, :].bitcast(I32),
         )
+
+
+def load_words(nc, window, words):
+    rows = words[0].rearrange("p c r -> p (c r)").bitcast(I32)
+    columns = rows.shape[1]
+    for cols in (slice(0, columns // 2), slice(columns // 2, columns)):
+        nc.sync.dma_start(out=window[:, cols], in_=rows[:, cols])
+
+
+def span(lo, hi):
+    return slice(lo * HALF, hi * HALF)
 
 
 def tile_picked_ysiglip_loss_p_kernel(
@@ -61,16 +86,16 @@ def tile_picked_ysiglip_loss_p_kernel(
         reuse = ctx.enter_context(tc.tile_pool(name="reuse", bufs=1))
         psum = ctx.enter_context(tc.psum_pool(name="psum", bufs=1))
 
-        def placed(shape, dtype, name, offset):
-            return reuse.tile(shape, dtype, name=name, align_bytes=64, offset=offset)
+        def placed(shape, dtype, name, offset, align=64):
+            return reuse.tile(shape, dtype, name=name, align_bytes=align, offset=offset)
 
-        def own(shape, dtype, name):
-            return keep.tile(shape, dtype, name=name, align_bytes=64)
+        def own(shape, dtype, name, align=64):
+            return keep.tile(shape, dtype, name=name, align_bytes=align)
 
-        offs_sb = keep.tile([P, S // 16], U16, name="offs_sb")
-        txt_sb = keep.tile([P, V // 16], U16, name="txt_sb")
+        offs_sb = keep.tile([P, S // GROUP], U16, name="offs_sb")
+        txt_sb = keep.tile([P, V // GROUP], U16, name="txt_sb")
 
-        w_raw = placed([P, PACK * H], F32, "w_raw", AT_W_RAW)
+        w_raw = placed([P, PACK * H], F32, "w_raw", AT_W_RAW, DMA_ALIGN)
         xs_all = placed([P, T], U8, "xs_all", AT_XS_ALL)
         es_all = placed([P, W], U8, "es_all", AT_ES_ALL)
         xw_all = placed([P, T], I32, "xw_all", AT_XW_ALL)
@@ -82,73 +107,78 @@ def tile_picked_ysiglip_loss_p_kernel(
         nc.sync.dma_start(offs_sb[:], offs)
         nc.sync.dma_start(txt_sb[:], txt)
         nc.sync.dma_start(out=w_raw[:, W_HEAD:], in_=w_rows[:, W_HEAD:])
-        x_rows = x_words[0].rearrange("p c r -> p (c r)").bitcast(I32)
-        for cols in (slice(0, T // 2), slice(T // 2, T)):
-            nc.sync.dma_start(out=xw_all[:, cols], in_=x_rows[:, cols])
+        load_words(nc, xw_all, x_words)
 
         zero_col = own([P, 1], F32, "zero_col")
         half_scale = own([P, 1], F32, "half_scale")
         nc.vector.memset(zero_col[:], 0.0)
         nc.scalar.activation(out=half_scale[:], in_=zero_col[:], func=ACT.Sigmoid)
-        n_sign = 5
-        signed = own([P, n_sign * HALF + 2], F32, "signed")
-        nc.vector.memset(signed[:, n_sign * HALF : n_sign * HALF + 1], FLOOR_AT)
-        nc.vector.memset(signed[:, n_sign * HALF + 1 :], 0.0)
+        signed = own([P, SIGNED + 2], F32, "signed")
+        nc.vector.memset(signed[:, SIGNED : SIGNED + 1], FLOOR_AT)
+        nc.vector.memset(signed[:, SIGNED + 1 :], 0.0)
 
         nc.vector.memset(xs_all[0:X_ROWS, :].bitcast(I32), 0)
         nc.vector.memset(es_all[0:E_ROWS, :].bitcast(I32), 0)
         nc.vector.memset(es_all[E_ROWS + SCALE_ROWS : P, :].bitcast(I32), 0)
-        planes = own([P, E_COL + V], U8, "planes")
-        nc.vector.memset(planes[:].bitcast(I32), 0)
-        xs, es = planes[:, 0:S], planes[:, E_COL : E_COL + V]
+        moved_scales = own([P, E_COL + V], U8, "moved_scales")
+        nc.vector.memset(moved_scales[:].bitcast(I32), 0)
+        xs, es = moved_scales[:, 0:S], moved_scales[:, E_COL : E_COL + V]
 
         xs_picked = own([P, S], U8, "xs_picked")
         nc.vector.tensor_copy(xs_picked[:], xs_all[:].indirect(offs_sb[:]))
         ew_all = placed([P, W], I32, "ew_all", AT_EW_ALL)
-        move_scale_rows(nc.sync, xs, xs_picked, X_ROWS, 0)
-        e_rows = e_words[0].rearrange("p c r -> p (c r)").bitcast(I32)
-        for cols in (slice(0, W // 2), slice(W // 2, W)):
-            nc.sync.dma_start(out=ew_all[:, cols], in_=e_rows[:, cols])
+        move_scale_rows(nc, xs, xs_picked, X_ROWS, 0)
+        load_words(nc, ew_all, e_words)
 
         w_src = w_raw[:].rearrange("p (j m t) -> p m j t", j=PACK, t=PACK)
-        w_bf = [placed([P, 2 * P * PACK], BF16, "w_bf%d" % half, AT_W_BF + 2 * half * KIB) for half in range(2)]
-        w_dst = [w_bf[half][:].rearrange("p (t m j) -> p m j t", t=2, j=PACK) for half in range(2)]
+        w_bf = [placed([P, 2 * P * PACK], BF16, "w_bf%d" % pair, AT_W_BF + 2 * pair * KIB) for pair in range(2)]
+        w_dst = [w_bf[pair][:].rearrange("p (t m j) -> p m j t", t=2, j=PACK) for pair in range(2)]
         nc.vector.tensor_copy(out=w_dst[0], in_=w_src[:, :, :, 0:2])
         nc.scalar.copy(out=w_dst[1], in_=w_src[:, :, :, 2:4])
 
-        es_picked = placed([P, V], U8, "es_picked", AT_ES_PICKED)
-        nc.vector.tensor_copy(es_picked[:], es_all[:].indirect(txt_sb[:]))
-        move_scale_rows(nc.sync, es, es_picked, E_ROWS, E_ROW)
+        es_picked = placed([P, V + P], U8, "es_picked", AT_ES_PICKED)
+        nc.vector.tensor_copy(es_picked[:, 0:V], es_all[:].indirect(txt_sb[:]))
+        move_scale_rows(nc, es, es_picked[:, 0:V], E_ROWS, E_ROW)
 
         w_codes = own([P, H], U32, "w_codes")
         w_scales = own([P, H], U8, "w_scales")
-        for half in range(2):
-            cols = slice(half * 2 * P, (half + 1) * 2 * P)
-            nc.vector.quantize_mx(out=w_codes[:, cols].bitcast(FP8X4), scales=w_scales[:, cols], in_=w_bf[half][:])
+        for pair in range(2):
+            cols = slice(pair * 2 * P, (pair + 1) * 2 * P)
+            nc.vector.quantize_mx(out=w_codes[:, cols].bitcast(FP8X4), scales=w_scales[:, cols], in_=w_bf[pair][:])
 
-        lab01 = placed([P, 2, V], F32, "lab01", AT_W_RAW)
-        lab2b = placed([P, HALF], F32, "lab2b", AT_W_RAW + 7 * KIB + 512)
-        lab12a = placed([P, 2, HALF], F32, "lab12a", AT_W_BF)
-        lab3 = placed([P, V], F32, "lab3", AT_W_RAW + 4 * KIB)
+        lab_0 = placed([P, 1, V], F32, "lab_0", AT_LAB_0)
+        lab_12_second = placed([P, 2, HALF], F32, "lab_12_second", AT_LAB_12_SECOND)
+        lab_12_first = placed([P, 2, HALF], F32, "lab_12_first", AT_LAB_12_FIRST)
+        lab_3 = placed([P, V], F32, "lab_3", AT_LAB_3)
         lab_rows = lab.rearrange("(b p) v -> p b v", p=P)
+        first, second = slice(0, HALF), slice(HALF, V)
+        labels = {
+            (0, 0): lab_0[:, 0, first],
+            (0, 1): lab_0[:, 0, second],
+            (1, 0): lab_12_first[:, 0, :],
+            (1, 1): lab_12_second[:, 0, :],
+            (2, 0): lab_12_first[:, 1, :],
+            (2, 1): lab_12_second[:, 1, :],
+            (3, 0): lab_3[:, first],
+            (3, 1): lab_3[:, second],
+        }
 
-        pieces = [(0, 1), (1, 2), (2, 4)]
         xw = {}
-        for lo, hi in pieces:
-            piece = own([P, (hi - lo) * P], U32, "xw%d" % lo)
-            nc.vector.tensor_copy(piece[:], xw_all[:].bitcast(U32).indirect(offs_sb[:, lo * 8 : hi * 8]))
+        for lo, hi in X_GATHERS:
+            picked = own([P, (hi - lo) * P], U32, "xw%d" % lo)
+            entries = offs_sb[:, lo * P // GROUP : hi * P // GROUP]
+            nc.vector.tensor_copy(picked[:], xw_all[:].bitcast(U32).indirect(entries))
             for b in range(lo, hi):
-                xw[b] = piece[:, (b - lo) * P : (b - lo + 1) * P]
-        nc.sync.dma_start(out=lab01[:, 0, 0:HALF], in_=lab_rows[:, 0, 0:HALF])
-        nc.sync.dma_start(out=lab01[:, 1, HALF:], in_=lab_rows[:, 1, HALF:])
-        nc.sync.dma_start(out=lab2b[:], in_=lab_rows[:, 2, HALF:])
-        nc.sync.dma_start(out=lab3[:], in_=lab_rows[:, 3, :])
-        nc.sync.dma_start(out=lab12a[:], in_=lab_rows[:, 1:3, 0:HALF])
-        nc.sync.dma_start(out=lab01[:, 0, HALF:], in_=lab_rows[:, 0, HALF:])
+                xw[b] = picked[:, (b - lo) * P : (b - lo + 1) * P]
+
+        nc.sync.dma_start(out=labels[0, 0], in_=lab_rows[:, 0, first])
+        nc.sync.dma_start(out=lab_12_second[:], in_=lab_rows[:, 1:3, second])
+        nc.sync.dma_start(out=lab_3[:], in_=lab_rows[:, 3, :])
+        nc.sync.dma_start(out=lab_12_first[:], in_=lab_rows[:, 1:3, first])
+        nc.sync.dma_start(out=labels[0, 1], in_=lab_rows[:, 0, second])
 
         h_bf = [own([P, P, PACK], BF16, "h_bf%d" % b) for b in range(BLOCKS)]
         for b in range(BLOCKS):
-            images = slice(b * P, (b + 1) * P)
             h_ps = psum.tile([P, PACK, P], F32, name="h_ps%d" % b, tag="bank%d" % b)
             for t in range(PACK):
                 cols = slice(t * P, (t + 1) * P)
@@ -157,7 +187,7 @@ def tile_picked_ysiglip_loss_p_kernel(
                     lhsT=w_codes[:, cols].bitcast(FP8X4),
                     lhsT_scale=w_scales[:, cols],
                     rhs=xw[b].bitcast(FP8X4),
-                    rhs_scale=xs[:, images],
+                    rhs_scale=xs[:, b * P : (b + 1) * P],
                     start=True,
                     stop=True,
                 )
@@ -166,127 +196,132 @@ def tile_picked_ysiglip_loss_p_kernel(
         h_codes = [own([P, P], U32, "h_codes%d" % b) for b in range(BLOCKS)]
         h_scales = {}
 
-        def quantise_h(b, held):
-            if held:
-                h_scales[b] = placed([P, P], U8, "h_scales%d" % b, AT_ES_PICKED + b * P)
-            else:
-                h_scales[b] = own([P, P], U8, "h_scales%d" % b)
+        def quantise_h(b):
+            h_scales[b] = placed([P, P], U8, "h_scales%d" % b, AT_ES_PICKED + b * P)
             nc.vector.quantize_mx(
-                out=h_codes[b][:].bitcast(FP8X4),
-                scales=h_scales[b][:],
-                in_=h_bf[b][:].rearrange("p n t -> p (n t)"),
+                out=h_codes[b][:].bitcast(FP8X4), scales=h_scales[b][:], in_=h_bf[b][:].rearrange("p n t -> p (n t)")
             )
 
-        ew = [own([P, HALF], U32, "ew0"), placed([P, HALF], U32, "ew1", AT_ES_PICKED + P - KIB)]
+        ew = [own([P, HALF], U32, "ew0"), placed([P, HALF], U32, "ew1", AT_EW_SECOND)]
 
         def gather_e(half):
-            nc.vector.tensor_copy(ew[half][:], ew_all[:].bitcast(U32).indirect(txt_sb[:, half * 16 : (half + 1) * 16]))
+            entries = txt_sb[:, half * HALF // GROUP : (half + 1) * HALF // GROUP]
+            nc.vector.tensor_copy(ew[half][:], ew_all[:].bitcast(U32).indirect(entries))
 
-        def product(acc, b, half):
+        y_bank = {(0, 0): 4, (1, 0): 5, (0, 1): 6, (1, 1): 7, (2, 0): 2, (2, 1): 0, (3, 0): 1, (3, 1): 3}
+        y_ps = {}
+
+        def product(b, half):
+            acc = psum.tile([P, V], F32, name="y_ps%d_%d" % (b, half), tag="bank%d" % y_bank[b, half])
+            y_ps[b, half] = acc[:, first]
             nc.tensor.matmul_mx(
-                out=acc,
+                out=y_ps[b, half],
                 lhsT=h_codes[b][:].bitcast(FP8X4),
                 lhsT_scale=h_scales[b][:],
                 rhs=ew[half][:].bitcast(FP8X4),
-                rhs_scale=es[E_ROW:P, half * HALF : (half + 1) * HALF],
+                rhs_scale=es[E_ROW:P, span(half, half + 1)],
                 start=True,
                 stop=True,
             )
 
-        def bank(name, tag):
-            return psum.tile([P, 2, HALF], F32, name=name, tag=tag)
+        def logits(rows, n, piece):
+            nc.vector.scalar_tensor_tensor(
+                out=rows[:, span(n, n + 1)],
+                in0=y_ps[piece],
+                scalar=SHIFT,
+                in1=labels[piece],
+                op0=ALU.subtract,
+                op1=ALU.mult,
+            )
 
-        def logits(dst, acc, labels):
-            nc.vector.scalar_tensor_tensor(out=dst, in0=acc, scalar=SHIFT, in1=labels, op0=ALU.subtract, op1=ALU.mult)
+        tanh = own([P, len(BY_MAGNITUDE) * HALF], F32, "tanh")
+        prob = own([P, SIGNED + 2], F32, "prob")
+        floor = prob[:, SIGNED : SIGNED + 1]
+        half_bias = prob[:, SIGNED + 1 :]
+        linear = own([P, len(PIECES) * HALF], F32, "linear")
 
-        tanh = own([P, 3 * HALF], F32, "tanh")
-        prob = own([P, n_sign * HALF + 2], F32, "prob")
-        floor = prob[:, n_sign * HALF : n_sign * HALF + 1]
-        one_half = prob[:, n_sign * HALF + 1 :]
+        def tanh_of(n):
+            nc.scalar.activation(
+                out=tanh[:, span(n, n + 1)], in_=y_ps[BY_MAGNITUDE[n]], func=ACT.Tanh, scale=SCALE / 2, bias=BIAS / 2
+            )
 
-        def span(lo, hi):
-            return slice(lo * HALF, hi * HALF)
-
-        def half_tanh(n, acc):
-            nc.scalar.activation(out=tanh[:, span(n, n + 1)], in_=acc, func=ACT.Tanh, scale=SCALE / 2, bias=BIAS / 2)
-
-        linear = own([P, 8 * HALF], F32, "linear")
-
-        def sig(lo, hi, extra=0):
-            cols = slice(lo * HALF, hi * HALF + extra)
+        def sigmoid_of(cols):
             nc.scalar.activation(out=prob[:, cols], in_=signed[:, cols], func=ACT.Sigmoid, scale=SCALE)
 
-        quantise_h(0, False)
         gather_e(0)
-        y0a, y1a, y0b, y1b = bank("y0a", "bank4"), bank("y1a", "bank5"), bank("y0b", "bank6"), bank("y1b", "bank7")
-        product(y0a[:, 0, :], 0, 0)
-        quantise_h(1, True)
-        product(y1a[:, 0, :], 1, 0)
+        quantise_h(0)
+        product(0, 0)
+        quantise_h(1)
+        product(1, 0)
         gather_e(1)
-        product(y1b[:, 0, :], 1, 1)
-        product(y0b[:, 0, :], 0, 1)
-        quantise_h(2, True)
-        y2a, y2b = bank("y2a", "bank2"), bank("y2b", "bank0")
-        product(y2a[:, 0, :], 2, 0)
-        product(y2b[:, 0, :], 2, 1)
-        logits(signed[:, span(0, 1)], y0a[:, 0, :], lab01[:, 0, 0:HALF])
-        quantise_h(3, True)
-        y3 = bank("y3", "bank1")
-        product(y3[:, 0, :], 3, 0)
-        product(y3[:, 1, :], 3, 1)
+        product(1, 1)
+        product(0, 1)
+        quantise_h(2)
+        product(2, 1)
+        product(2, 0)
+        logits(signed, 0, BY_SIGN[0])
+        quantise_h(3)
+        product(3, 0)
+        product(3, 1)
 
-        half_tanh(0, y1a[:, 0, :])
-        sig(0, 1)
-        half_tanh(1, y0b[:, 0, :])
-        half_tanh(2, y2a[:, 0, :])
-        logits(signed[:, span(1, 2)], y1b[:, 0, :], lab01[:, 1, HALF:])
-        sig(1, 2)
-        logits(signed[:, span(2, 3)], y2b[:, 0, :], lab2b[:])
-        sig(2, 3)
-        logits(signed[:, span(3, 4)], y3[:, 0, :], lab3[:, 0:HALF])
-        sig(3, 4)
-        logits(signed[:, span(4, 5)], y3[:, 1, :], lab3[:, HALF:])
-        sig(4, 5, 2)
-        late = placed([P, 3 * HALF], F32, "late", AT_W_RAW + 7 * KIB + 512)
-        magnitude = placed([P, 3 * HALF], F32, "magnitude", AT_W_RAW + 4 * KIB + 512)
+        last = len(BY_SIGN) - 1
+        tanh_of(0)
+        sigmoid_of(span(0, 1))
+        for n in range(1, len(BY_SIGN)):
+            if n == 1:
+                tanh_of(1)
+            logits(signed, n, BY_SIGN[n])
+            sigmoid_of(span(n, n + 1) if n < last else slice(n * HALF, SIGNED + 2))
+            if n == 1:
+                tanh_of(2)
+
+        late = placed([P, len(BY_MAGNITUDE) * HALF], F32, "late", AT_LATE)
+        magnitude = placed([P, len(BY_MAGNITUDE) * HALF], F32, "magnitude", AT_MAGNITUDE)
 
         def linear_part(dst, src):
             nc.vector.tensor_scalar(out=dst, in0=src, scalar1=-SCALE, scalar2=0.0, op0=ALU.mult, op1=ALU.max)
 
-        logits(late[:, span(0, 1)], y1a[:, 0, :], lab12a[:, 0, :])
-        logits(late[:, span(1, 2)], y0b[:, 0, :], lab01[:, 0, HALF:])
-        logits(late[:, span(2, 3)], y2a[:, 0, :], lab12a[:, 1, :])
-        linear_part(linear[:, span(0, 5)], signed[:, span(0, 5)])
+        for n, piece in enumerate(BY_MAGNITUDE):
+            logits(late, n, piece)
+        linear_part(linear[:, 0:SIGNED], signed[:, 0:SIGNED])
         nc.vector.scalar_tensor_tensor(
             out=magnitude[:], in0=tanh[:], scalar=-1.0, in1=tanh[:], op0=ALU.mult, op1=ALU.max
         )
-        linear_part(linear[:, span(5, 8)], late[:])
+        linear_part(linear[:, SIGNED:], late[:])
 
-        log_prob = own([P, 8 * HALF], F32, "log_prob")
-        res = own([P, 8 * HALF], F32, "res")
-        where = [(0, 0), (1, 1), (2, 1), (3, 0), (3, 1), (1, 0), (0, 1), (2, 0)]
-        quarter = HALF // 2
-        for n, (b, half) in enumerate(where):
-            cuts = [(0, quarter), (quarter, HALF)] if n in QUARTERED else [(0, HALF)]
-            for lo, hi in cuts:
-                cols = slice(n * HALF + lo, n * HALF + hi)
-                if n < n_sign:
-                    nc.scalar.activation(out=log_prob[:, cols], in_=prob[:, cols], func=ACT.Ln, bias=floor)
-                    nc.vector.scalar_tensor_tensor(
-                        out=res[:, cols], in0=log_prob[:, cols], scalar=-1.0, in1=linear[:, cols], op0=ALU.mult, op1=ALU.max
-                    )
-                else:
-                    nc.scalar.activation(
-                        out=log_prob[:, cols],
-                        in_=magnitude[:, (n - n_sign) * HALF + lo : (n - n_sign) * HALF + hi],
-                        func=ACT.Ln,
-                        scale=half_scale[:],
-                        bias=one_half,
-                    )
-                    nc.vector.tensor_tensor(out=res[:, cols], in0=linear[:, cols], in1=log_prob[:, cols], op=ALU.subtract)
-                if n in QUARTER_STORES or hi == HALF:
-                    first = lo if n in QUARTER_STORES else 0
-                    nc.sync.dma_start(
-                        out=out[b * P : (b + 1) * P, half * HALF + first : half * HALF + hi],
-                        in_=res[:, n * HALF + first : n * HALF + hi],
-                    )
+        log_prob = own([P, len(PIECES) * HALF], F32, "log_prob")
+        res = own([P, len(PIECES) * HALF], F32, "res", DMA_ALIGN)
+
+        def finish(at, width):
+            cols = slice(at, at + width)
+            if at < SIGNED:
+                nc.scalar.activation(out=log_prob[:, cols], in_=prob[:, cols], func=ACT.Ln, bias=floor)
+                nc.vector.scalar_tensor_tensor(
+                    out=res[:, cols], in0=log_prob[:, cols], scalar=-1.0, in1=linear[:, cols], op0=ALU.mult, op1=ALU.max
+                )
+            else:
+                nc.scalar.activation(
+                    out=log_prob[:, cols],
+                    in_=magnitude[:, at - SIGNED : at - SIGNED + width],
+                    func=ACT.Ln,
+                    scale=half_scale[:],
+                    bias=half_bias,
+                )
+                nc.vector.tensor_tensor(out=res[:, cols], in0=linear[:, cols], in1=log_prob[:, cols], op=ALU.subtract)
+
+        def store(n, lo, width):
+            b, half = PIECES[n]
+            nc.sync.dma_start(
+                out=out[b * P : (b + 1) * P, half * HALF + lo : half * HALF + lo + width],
+                in_=res[:, n * HALF + lo : n * HALF + lo + width],
+            )
+
+        for lo in (0, QUARTER):
+            finish(lo, QUARTER)
+            store(0, lo, QUARTER)
+        for n in range(1, len(PIECES) - 1):
+            finish(n * HALF, HALF)
+            store(n, 0, HALF)
+        for lo in (0, QUARTER):
+            finish((len(PIECES) - 1) * HALF + lo, QUARTER)
+        store(len(PIECES) - 1, 0, HALF)

from contextlib import ExitStack

import concourse.mybir as mybir

K, T, S, H, V, W = 512, 2048, 512, 512, 512, 2048
FLOPS = 2 * K * H * S + 2 * H * S * V

F32 = mybir.dt.float32
BF16 = mybir.dt.bfloat16
I32 = mybir.dt.int32
U32 = mybir.dt.uint32
U16 = mybir.dt.uint16
U8 = mybir.dt.uint8
FP8X4 = mybir.dt.float8_e4m3fn_x4
ALU = mybir.AluOpType
ACT = mybir.ActivationFunctionType

P = 128
PACK = 4
BLOCKS = S // P
HALF = V // 2
QUARTER = HALF // 2
GROUP = 16
SCALE_ROWS = 16

SCALE = 1.5
BIAS = -0.5
SHIFT = 0.5 / 1.5
FLOOR_AT = -28.0

BY_SIGN = [(0, 0), (1, 1), (2, 1), (3, 0), (3, 1)]
BY_MAGNITUDE = [(1, 0), (0, 1), (2, 0)]
PIECES = BY_SIGN + BY_MAGNITUDE
SIGNED = len(BY_SIGN) * HALF

X_ROWS = 112
E_ROWS = 48
E_ROW = 4
E_COL = S - P
W_HEAD = 384
X_GATHERS = [(0, 1), (1, 2), (2, 4)]

KIB = 1024
DMA_ALIGN = 512
AT_W_RAW = 0
AT_ES_ALL = 8 * KIB
AT_XW_ALL = 12 * KIB
AT_EW_ALL = 20 * KIB
AT_XS_ALL = 27 * KIB
AT_ES_PICKED = 35 * KIB
AT_EW_SECOND = AT_ES_PICKED + V
AT_W_BF = 56 * KIB
AT_LAB_0 = AT_W_RAW
AT_LAB_3 = AT_W_RAW + 4 * KIB
AT_LAB_12_SECOND = AT_W_RAW + 13 * KIB // 2
AT_LAB_12_FIRST = AT_W_BF
AT_MAGNITUDE = AT_W_RAW + 3 * KIB
AT_LATE = AT_W_RAW + 15 * KIB // 2


def move_scale_rows(nc, operand, picked, first, row0):
    for r in range(4):
        nc.sync.dma_start(
            out=operand[row0 + r : P : 32, :].bitcast(I32),
            in_=picked[first + r : first + SCALE_ROWS : 4, :].bitcast(I32),
        )


def load_words(nc, window, words):
    rows = words[0].rearrange("p c r -> p (c r)").bitcast(I32)
    columns = rows.shape[1]
    for cols in (slice(0, columns // 2), slice(columns // 2, columns)):
        nc.sync.dma_start(out=window[:, cols], in_=rows[:, cols])


def span(lo, hi):
    return slice(lo * HALF, hi * HALF)


def tile_picked_ysiglip_loss_p_kernel(
    tc, x_words, x_scales, w1, e_words, e_scales, lab, offs, txt, out
):
    nc = tc.nc
    with ExitStack() as ctx:
        keep = ctx.enter_context(tc.tile_pool(name="keep", bufs=1))
        reuse = ctx.enter_context(tc.tile_pool(name="reuse", bufs=1))
        psum = ctx.enter_context(tc.psum_pool(name="psum", bufs=1))

        def placed(shape, dtype, name, offset, align=64):
            return reuse.tile(shape, dtype, name=name, align_bytes=align, offset=offset)

        def own(shape, dtype, name, align=64):
            return keep.tile(shape, dtype, name=name, align_bytes=align)

        offs_sb = keep.tile([P, S // GROUP], U16, name="offs_sb")
        txt_sb = keep.tile([P, V // GROUP], U16, name="txt_sb")

        w_raw = placed([P, PACK * H], F32, "w_raw", AT_W_RAW, DMA_ALIGN)
        xs_all = placed([P, T], U8, "xs_all", AT_XS_ALL)
        es_all = placed([P, W], U8, "es_all", AT_ES_ALL)
        xw_all = placed([P, T], I32, "xw_all", AT_XW_ALL)

        w_rows = w1.rearrange("(p j) c -> p (j c)", j=PACK)
        nc.sync.dma_start(out=w_raw[:, 0:W_HEAD], in_=w_rows[:, 0:W_HEAD])
        nc.sync.dma_start(out=xs_all[X_ROWS : X_ROWS + SCALE_ROWS, :].bitcast(I32), in_=x_scales[0].bitcast(I32))
        nc.sync.dma_start(out=es_all[E_ROWS : E_ROWS + SCALE_ROWS, :].bitcast(I32), in_=e_scales[0].bitcast(I32))
        nc.sync.dma_start(offs_sb[:], offs)
        nc.sync.dma_start(txt_sb[:], txt)
        nc.sync.dma_start(out=w_raw[:, W_HEAD:], in_=w_rows[:, W_HEAD:])
        load_words(nc, xw_all, x_words)

        zero_col = own([P, 1], F32, "zero_col")
        half_scale = own([P, 1], F32, "half_scale")
        nc.vector.memset(zero_col[:], 0.0)
        nc.scalar.activation(out=half_scale[:], in_=zero_col[:], func=ACT.Sigmoid)
        signed = own([P, SIGNED + 2], F32, "signed")
        nc.vector.memset(signed[:, SIGNED : SIGNED + 1], FLOOR_AT)
        nc.vector.memset(signed[:, SIGNED + 1 :], 0.0)

        nc.vector.memset(xs_all[0:X_ROWS, :].bitcast(I32), 0)
        nc.vector.memset(es_all[0:E_ROWS, :].bitcast(I32), 0)
        nc.vector.memset(es_all[E_ROWS + SCALE_ROWS : P, :].bitcast(I32), 0)
        moved_scales = own([P, E_COL + V], U8, "moved_scales")
        nc.vector.memset(moved_scales[:].bitcast(I32), 0)
        xs, es = moved_scales[:, 0:S], moved_scales[:, E_COL : E_COL + V]

        xs_picked = own([P, S], U8, "xs_picked")
        nc.vector.tensor_copy(xs_picked[:], xs_all[:].indirect(offs_sb[:]))
        ew_all = placed([P, W], I32, "ew_all", AT_EW_ALL)
        move_scale_rows(nc, xs, xs_picked, X_ROWS, 0)
        load_words(nc, ew_all, e_words)

        w_src = w_raw[:].rearrange("p (j m t) -> p m j t", j=PACK, t=PACK)
        w_bf = [placed([P, 2 * P * PACK], BF16, "w_bf%d" % pair, AT_W_BF + 2 * pair * KIB) for pair in range(2)]
        w_dst = [w_bf[pair][:].rearrange("p (t m j) -> p m j t", t=2, j=PACK) for pair in range(2)]
        nc.vector.tensor_copy(out=w_dst[0], in_=w_src[:, :, :, 0:2])
        nc.scalar.copy(out=w_dst[1], in_=w_src[:, :, :, 2:4])

        es_picked = placed([P, V + P], U8, "es_picked", AT_ES_PICKED)
        nc.vector.tensor_copy(es_picked[:, 0:V], es_all[:].indirect(txt_sb[:]))
        move_scale_rows(nc, es, es_picked[:, 0:V], E_ROWS, E_ROW)

        w_codes = own([P, H], U32, "w_codes")
        w_scales = own([P, H], U8, "w_scales")
        for pair in range(2):
            cols = slice(pair * 2 * P, (pair + 1) * 2 * P)
            nc.vector.quantize_mx(out=w_codes[:, cols].bitcast(FP8X4), scales=w_scales[:, cols], in_=w_bf[pair][:])

        lab_0 = placed([P, 1, V], F32, "lab_0", AT_LAB_0)
        lab_12_second = placed([P, 2, HALF], F32, "lab_12_second", AT_LAB_12_SECOND)
        lab_12_first = placed([P, 2, HALF], F32, "lab_12_first", AT_LAB_12_FIRST)
        lab_3 = placed([P, V], F32, "lab_3", AT_LAB_3)
        lab_rows = lab.rearrange("(b p) v -> p b v", p=P)
        first, second = slice(0, HALF), slice(HALF, V)
        labels = {
            (0, 0): lab_0[:, 0, first],
            (0, 1): lab_0[:, 0, second],
            (1, 0): lab_12_first[:, 0, :],
            (1, 1): lab_12_second[:, 0, :],
            (2, 0): lab_12_first[:, 1, :],
            (2, 1): lab_12_second[:, 1, :],
            (3, 0): lab_3[:, first],
            (3, 1): lab_3[:, second],
        }

        xw = {}
        for lo, hi in X_GATHERS:
            picked = own([P, (hi - lo) * P], U32, "xw%d" % lo)
            entries = offs_sb[:, lo * P // GROUP : hi * P // GROUP]
            nc.vector.tensor_copy(picked[:], xw_all[:].bitcast(U32).indirect(entries))
            for b in range(lo, hi):
                xw[b] = picked[:, (b - lo) * P : (b - lo + 1) * P]

        nc.sync.dma_start(out=labels[0, 0], in_=lab_rows[:, 0, first])
        nc.sync.dma_start(out=lab_12_second[:], in_=lab_rows[:, 1:3, second])
        nc.sync.dma_start(out=lab_3[:], in_=lab_rows[:, 3, :])
        nc.sync.dma_start(out=lab_12_first[:], in_=lab_rows[:, 1:3, first])
        nc.sync.dma_start(out=labels[0, 1], in_=lab_rows[:, 0, second])

        h_bf = [own([P, P, PACK], BF16, "h_bf%d" % b) for b in range(BLOCKS)]
        for b in range(BLOCKS):
            h_ps = psum.tile([P, PACK, P], F32, name="h_ps%d" % b, tag="bank%d" % b)
            for t in range(PACK):
                cols = slice(t * P, (t + 1) * P)
                nc.tensor.matmul_mx(
                    out=h_ps[:, t, :],
                    lhsT=w_codes[:, cols].bitcast(FP8X4),
                    lhsT_scale=w_scales[:, cols],
                    rhs=xw[b].bitcast(FP8X4),
                    rhs_scale=xs[:, b * P : (b + 1) * P],
                    start=True,
                    stop=True,
                )
            nc.scalar.copy(out=h_bf[b][:], in_=h_ps[:].rearrange("p t n -> p n t"))

        h_codes = [own([P, P], U32, "h_codes%d" % b) for b in range(BLOCKS)]
        h_scales = {}

        def quantise_h(b):
            h_scales[b] = placed([P, P], U8, "h_scales%d" % b, AT_ES_PICKED + b * P)
            nc.vector.quantize_mx(
                out=h_codes[b][:].bitcast(FP8X4), scales=h_scales[b][:], in_=h_bf[b][:].rearrange("p n t -> p (n t)")
            )

        ew = [own([P, HALF], U32, "ew0"), placed([P, HALF], U32, "ew1", AT_EW_SECOND)]

        def gather_e(half):
            entries = txt_sb[:, half * HALF // GROUP : (half + 1) * HALF // GROUP]
            nc.vector.tensor_copy(ew[half][:], ew_all[:].bitcast(U32).indirect(entries))

        y_bank = {(0, 0): 4, (1, 0): 5, (0, 1): 6, (1, 1): 7, (2, 0): 2, (2, 1): 0, (3, 0): 1, (3, 1): 3}
        y_ps = {}

        def product(b, half):
            acc = psum.tile([P, V], F32, name="y_ps%d_%d" % (b, half), tag="bank%d" % y_bank[b, half])
            y_ps[b, half] = acc[:, first]
            nc.tensor.matmul_mx(
                out=y_ps[b, half],
                lhsT=h_codes[b][:].bitcast(FP8X4),
                lhsT_scale=h_scales[b][:],
                rhs=ew[half][:].bitcast(FP8X4),
                rhs_scale=es[E_ROW:P, span(half, half + 1)],
                start=True,
                stop=True,
            )

        def logits(rows, n, piece):
            nc.vector.scalar_tensor_tensor(
                out=rows[:, span(n, n + 1)],
                in0=y_ps[piece],
                scalar=SHIFT,
                in1=labels[piece],
                op0=ALU.subtract,
                op1=ALU.mult,
            )

        tanh = own([P, len(BY_MAGNITUDE) * HALF], F32, "tanh")
        prob = own([P, SIGNED + 2], F32, "prob")
        floor = prob[:, SIGNED : SIGNED + 1]
        half_bias = prob[:, SIGNED + 1 :]
        linear = own([P, len(PIECES) * HALF], F32, "linear")

        def tanh_of(n):
            nc.scalar.activation(
                out=tanh[:, span(n, n + 1)], in_=y_ps[BY_MAGNITUDE[n]], func=ACT.Tanh, scale=SCALE / 2, bias=BIAS / 2
            )

        def sigmoid_of(cols):
            nc.scalar.activation(out=prob[:, cols], in_=signed[:, cols], func=ACT.Sigmoid, scale=SCALE)

        gather_e(0)
        quantise_h(0)
        product(0, 0)
        quantise_h(1)
        product(1, 0)
        gather_e(1)
        product(1, 1)
        product(0, 1)
        quantise_h(2)
        product(2, 1)
        product(2, 0)
        logits(signed, 0, BY_SIGN[0])
        quantise_h(3)
        product(3, 0)
        product(3, 1)

        last = len(BY_SIGN) - 1
        tanh_of(0)
        sigmoid_of(span(0, 1))
        for n in range(1, len(BY_SIGN)):
            if n == 1:
                tanh_of(1)
            logits(signed, n, BY_SIGN[n])
            sigmoid_of(span(n, n + 1) if n < last else slice(n * HALF, SIGNED + 2))
            if n == 1:
                tanh_of(2)

        late = placed([P, len(BY_MAGNITUDE) * HALF], F32, "late", AT_LATE)
        magnitude = placed([P, len(BY_MAGNITUDE) * HALF], F32, "magnitude", AT_MAGNITUDE)

        def linear_part(dst, src):
            nc.vector.tensor_scalar(out=dst, in0=src, scalar1=-SCALE, scalar2=0.0, op0=ALU.mult, op1=ALU.max)

        for n, piece in enumerate(BY_MAGNITUDE):
            logits(late, n, piece)
        linear_part(linear[:, 0:SIGNED], signed[:, 0:SIGNED])
        nc.vector.scalar_tensor_tensor(
            out=magnitude[:], in0=tanh[:], scalar=-1.0, in1=tanh[:], op0=ALU.mult, op1=ALU.max
        )
        linear_part(linear[:, SIGNED:], late[:])

        log_prob = own([P, len(PIECES) * HALF], F32, "log_prob")
        res = own([P, len(PIECES) * HALF], F32, "res", DMA_ALIGN)

        def finish(at, width):
            cols = slice(at, at + width)
            if at < SIGNED:
                nc.scalar.activation(out=log_prob[:, cols], in_=prob[:, cols], func=ACT.Ln, bias=floor)
                nc.vector.scalar_tensor_tensor(
                    out=res[:, cols], in0=log_prob[:, cols], scalar=-1.0, in1=linear[:, cols], op0=ALU.mult, op1=ALU.max
                )
            else:
                nc.scalar.activation(
                    out=log_prob[:, cols],
                    in_=magnitude[:, at - SIGNED : at - SIGNED + width],
                    func=ACT.Ln,
                    scale=half_scale[:],
                    bias=half_bias,
                )
                nc.vector.tensor_tensor(out=res[:, cols], in0=linear[:, cols], in1=log_prob[:, cols], op=ALU.subtract)

        def store(n, lo, width):
            b, half = PIECES[n]
            nc.sync.dma_start(
                out=out[b * P : (b + 1) * P, half * HALF + lo : half * HALF + lo + width],
                in_=res[:, n * HALF + lo : n * HALF + lo + width],
            )

        for lo in (0, QUARTER):
            finish(lo, QUARTER)
            store(0, lo, QUARTER)
        for n in range(1, len(PIECES) - 1):
            finish(n * HALF, HALF)
            store(n, 0, HALF)
        for lo in (0, QUARTER):
            finish((len(PIECES) - 1) * HALF + lo, QUARTER)
        store(len(PIECES) - 1, 0, HALF)
